import numpy as np
import ml_dtypes


def mxq(x, axis, fmt="e4m3"):
    dtype, down = {"e4m3": (ml_dtypes.float8_e4m3fn, 7), "e5m2": (ml_dtypes.float8_e5m2, 14)}[fmt]
    v = np.moveaxis(np.asarray(x, np.float32).astype(ml_dtypes.bfloat16).astype(np.float64), axis, -1)
    blocks = v.reshape(v.shape[:-1] + (-1, 32))
    amax = np.abs(blocks).max(-1, keepdims=True)
    byte = np.maximum(np.where(amax > 0, np.frexp(amax)[1] - 1 + 127, 0) - down, 1)
    scale = np.exp2(byte - 127.0)
    codes = (blocks / scale).astype(np.float32).astype(dtype).astype(np.float64)
    return np.moveaxis((codes * scale).reshape(v.shape), -1, axis)


WIDE = False


def mx_kscale(k):
    if not WIDE:
        return np.ones(k)
    levels = np.array([18, -18])
    if k % 512:
        return np.exp2(np.random.permutation(np.resize(levels, k // 32))).repeat(32)
    a = np.empty((k // 512, 16))
    for p in range(k // 512):
        a[p, :8] = np.random.permutation(np.resize(levels, 8))
        for g in range(8):
            far = levels[np.abs(levels - a[p, g]) >= 10]
            a[p, g + 8] = far[np.random.randint(len(far))]
    return np.exp2(a.ravel()).repeat(32)


def f64(x):
    return np.asarray(x).astype(np.float64)


def striped(idx):
    return np.tile(np.asarray(idx).reshape(-1, 16).T, (8, 1)).astype(np.uint16)


def unstriped(offs):
    return offs[:16].T.reshape(-1).astype(np.int64)


B, N, T, D, R = 1, 512, 2048, 512, 512


def setup_inputs():
    n = np.random.standard_normal
    idx = np.random.permutation(T)[:B * N]
    s = mx_kscale(D)[:, None]
    z = mx_kscale(R)[:, None]
    u = np.ones(T)
    u[idx] = mx_kscale(B * N)
    r = np.random.uniform(0.5, 2.0, T) * u
    x = n((B, D, R))
    teach = np.exp(n((B, R, N)))
    teach = teach / teach.sum(-1, keepdims=True)
    return {
        "xT": (x * s).astype(np.float32),
        "wT": (n((D, T)) * (0.50 / np.sqrt(D)) / s / r).astype(np.float32),
        "y": teach.astype(np.float32),
        "lse": (np.log(N) + 0.12 + 0.1 * n((B, R, 1))).astype(np.float32),
        "wt": (np.random.uniform(0.5, 1.5, (B, R, 1)) * N / np.sqrt(R) * z).astype(np.float32),
        "ts": np.tile(r, (128, 1)).astype(np.float32),
        "xm": (x.transpose(0, 2, 1) / z).astype(np.float32),
        "offs": striped(idx),
    }


def reference(xT, wT, y, lse, wt, ts, xm, offs):
    idx = unstriped(offs)
    pick = lambda x: x[:, idx].reshape(x.shape[0], B, N).transpose(1, 0, 2)
    w = pick(f64(wT))
    a = mxq(f64(xT), 1, "e4m3").transpose(0, 2, 1) @ mxq(w, 1, "e4m3")
    ts_ = pick(f64(ts))[:, :1, :]
    a = a * ts_
    g = f64(wt) * (np.exp(a - f64(lse)) - f64(y))
    g = g * ts_
    dw = mxq(f64(xm), 1, "e4m3").transpose(0, 2, 1) @ mxq(g, 1, "e5m2")
    gw = np.zeros((D, T))
    gw[:, idx] = dw.transpose(1, 0, 2).reshape(D, B * N)
    gx = mxq(g, 2, "e5m2") @ mxq(w, 2, "e4m3").transpose(0, 2, 1)
    return gw, gx

@@ -1,0 +1,186 @@
+from contextlib import ExitStack
+
+import concourse.mybir as mybir
+from concourse.masks import make_identity
+
+N, T, D, R = 512, 2048, 512, 512
+FLOPS = 3 * 2 * N * D * R
+
+F32 = mybir.dt.float32
+BF16 = mybir.dt.bfloat16
+U32 = mybir.dt.uint32
+U16 = mybir.dt.uint16
+U8 = mybir.dt.uint8
+E4 = mybir.dt.float8_e4m3fn_x4
+E5 = mybir.dt.float8_e5m2_x4
+ALU = mybir.AluOpType
+ACT = mybir.ActivationFunctionType
+
+P = 128
+PACK = 4
+WINDOWS = 3
+
+
+def tile_attend_glse_wx_ts_kernel(tc, xT, wT, y, lse, wt, ts, xm, offs, out_0, out_1):
+    nc = tc.nc
+    with ExitStack() as ctx:
+        sb = ctx.enter_context(tc.tile_pool(name="sb", bufs=1))
+        ps = ctx.enter_context(tc.psum_pool(name="ps", bufs=1))
+
+        def bank(tag):
+            return ps.tile([P, 512], F32, name=tag, tag=tag)
+
+        def mx_operand(name):
+            codes = sb.tile([P, 512], U32, name=name + "_codes", align_bytes=64)
+            scales = sb.tile([P, 512], U8, name=name + "_scales", align_bytes=64)
+            return codes, scales
+
+        def quantize(operand, fmt, src, c0, c1):
+            codes, scales = operand
+            nc.vector.quantize_mx(out=codes[:, c0:c1].bitcast(fmt), scales=scales[:, c0:c1],
+                                  in_=src[:, PACK * c0:PACK * c1])
+
+        def product(out, lhs, lhs_fmt, j, rhs, rhs_fmt):
+            cols = slice(j * P, (j + 1) * P)
+            nc.tensor.matmul_mx(out=out[:], lhsT=lhs[0][:, cols].bitcast(lhs_fmt), lhsT_scale=lhs[1][:, cols],
+                                rhs=rhs[0][:].bitcast(rhs_fmt), rhs_scale=rhs[1][:], start=True, stop=True)
+
+        def turn_pairs(src, u, out_bank):
+            words = src[:].bitcast(F32)
+            for s in range(PACK):
+                nc.tensor.transpose(out_bank[:, s * P:(s + 1) * P], words[:, 2 * s + u:2 * 512:2 * PACK], ident[:])
+
+        offsets = sb.tile([P, N // 16], U16, name="offsets")
+        nc.sync.dma_start(offsets[:], offs)
+        w_planes = [sb.tile([P, T], F32, name="w_plane%d" % t) for t in range(PACK)]
+        wT_planes = wT.rearrange("(p t) c -> t p c", t=PACK)
+        ts_table = sb.tile([P, T], F32, name="ts_table")
+        nc.gpsimd.memset(ts_table[0:P - 1, :], 0.0)
+        nc.sync.dma_start(ts_table[P - 1:P, :], ts[0:1, :])
+        nc.sync.dma_start(w_planes[0][:], wT_planes[0])
+        wt_sb = sb.tile([P, PACK], F32, name="wt_sb")
+        nc.sync.dma_start(wt_sb[:], wt[0].rearrange("(p t) o -> p (t o)", t=PACK))
+        lse_sb = sb.tile([P, PACK], F32, name="lse_sb")
+        nc.sync.dma_start(lse_sb[:], lse[0].rearrange("(p t) o -> p (t o)", t=PACK))
+        for t in range(1, PACK):
+            nc.sync.dma_start(w_planes[t][:], wT_planes[t])
+        x_raw = sb.tile([P, PACK, R], F32, name="x_raw")
+        nc.sync.dma_start(x_raw[:], xT[0].rearrange("(p t) r -> p t r", t=PACK))
+        y_sb = sb.tile([P, PACK, N], F32, name="y_sb")
+        nc.sync.dma_start(y_sb[:], y[0].rearrange("(p t) i -> p t i", t=PACK))
+        xm_raw = sb.tile([P, PACK, D], F32, name="xm_raw")
+        nc.sync.dma_start(xm_raw[:], xm[0].rearrange("(p t) d -> p t d", t=PACK))
+        ident = sb.tile([P, P], F32, name="ident")
+        make_identity(nc, ident[:])
+        neg_lse = sb.tile([P, PACK], F32, name="neg_lse")
+        nc.gpsimd.tensor_scalar(neg_lse[:], lse_sb[:], -1.0, 0.0, ALU.mult, ALU.add)
+        windows = [sb.tile([P, T], F32, name="window%d" % k) for k in range(WINDOWS)]
+        for k in range(WINDOWS):
+            nc.gpsimd.memset(windows[k][:], 0.0)
+
+        ts_row = sb.tile([P, N], F32, name="ts_row")
+        nc.vector.tensor_copy(ts_row[:], ts_table[:].indirect(offsets[:]))
+        ts_cols = bank("b0")
+        for k in range(4):
+            nc.tensor.transpose(ts_cols[:, k * P:(k + 1) * P], ts_row[:, k * P:(k + 1) * P], ident[:])
+        ts_rep = sb.tile([P, 4, P], F32, name="ts_rep")
+        nc.scalar.copy(ts_rep[:], ts_cols[:].rearrange("q (k m) -> q k m", k=4)[:, :, P - 1:P].to_broadcast([P, 4, P]))
+        ts_all_ps = bank("b1")
+        for k in range(4):
+            nc.tensor.transpose(ts_all_ps[:, k * P:(k + 1) * P], ts_rep[:, k, :], ident[:])
+        ts_all = sb.tile([P, N], F32, name="ts_all")
+        nc.scalar.copy(ts_all[:], ts_all_ps[:])
+        wt_ts = sb.tile([P, PACK, N], F32, name="wt_ts")
+        for t in range(PACK):
+            nc.scalar.activation(wt_ts[:, t, :], ts_all_ps[:], ACT.Copy, scale=wt_sb[:, t:t + 1])
+
+        w_bf = sb.tile([P, N * PACK], BF16, name="w_bf", align_bytes=64)
+        w_bf3 = w_bf[:].rearrange("p (i t) -> p i t", t=PACK)
+        for t in range(PACK):
+            nc.vector.tensor_copy(w_bf3[:, :, t], w_planes[t][:].indirect(offsets[:]))
+        w_d = mx_operand("w_d")
+        quantize(w_d, E4, w_bf, 0, 512)
+
+        x_bf = sb.tile([P, R * PACK], BF16, name="x_bf", align_bytes=64)
+        x_dst = x_bf[:].rearrange("p (j m t) -> p m t j", j=PACK, t=PACK)
+        x_src = x_raw[:].rearrange("p t (m j) -> p m t j", j=PACK)
+        nc.vector.tensor_copy(x_dst[:, :, :, 0:2], x_src[:, :, :, 0:2])
+        nc.scalar.copy(x_dst[:, :, :, 2:4], x_src[:, :, :, 2:4])
+        x_d = mx_operand("x_d")
+        quantize(x_d, E4, x_bf, 0, 256)
+        quantize(x_d, E4, x_bf, 256, 512)
+
+        scaled = sb.tile([P, PACK, N], F32, name="scaled")
+        probs = sb.tile([P, PACK, N], F32, name="probs")
+        diff = sb.tile([P, PACK, N], F32, name="diff")
+        for j in range(PACK):
+            a_ps = bank("a%d" % j)
+            product(a_ps, x_d, E4, j, w_d, E4)
+            nc.vector.tensor_tensor(scaled[:, j, :], a_ps[:], ts_all[:], ALU.mult)
+            nc.scalar.activation(probs[:, j, :], scaled[:, j, :], ACT.Exp, bias=neg_lse[:, j:j + 1], scale=1.0)
+        for j in range(PACK):
+            nc.vector.tensor_tensor(diff[:, j, :], probs[:, j, :], y_sb[:, j, :], ALU.subtract)
+
+        xm_bf = sb.tile([P, D * PACK], BF16, name="xm_bf", align_bytes=64)
+        nc.scalar.copy(xm_bf[:].rearrange("p (c i t) -> p c t i", i=4, t=PACK),
+                       xm_raw[:].rearrange("p t (c i) -> p c t i", i=4))
+
+        w_i_bf = sb.tile([P, D * PACK], BF16, name="w_i_bf", align_bytes=64)
+        w_i_dst = w_i_bf[:].rearrange("q (p u e s) -> q u p e s", u=2, e=2, s=PACK)
+        for u, tag in ((0, "b2"), (1, "a3")):
+            turned = bank(tag)
+            turn_pairs(w_bf, u, turned)
+            nc.scalar.copy(w_i_dst[:, u], turned[:].bitcast(BF16).rearrange("q (s p e) -> q p e s", s=PACK, e=2))
+        w_i = mx_operand("w_i")
+
+        h_bf = sb.tile([P, N * PACK], BF16, name="h_bf", align_bytes=64)
+        h_dst = h_bf[:].rearrange("p (c i t) -> p c t i", i=4, t=PACK)
+        diff_src = diff[:].rearrange("p t (c i) -> p c t i", i=4)
+        wt_ts_src = wt_ts[:].rearrange("p t (c i) -> p c t i", i=4)
+        xm_r = mx_operand("xm_r")
+        h_r = mx_operand("h_r")
+        nc.vector.tensor_tensor(h_dst[:, 0:64], diff_src[:, 0:64], wt_ts_src[:, 0:64], ALU.mult)
+        quantize(xm_r, E4, xm_bf, 0, 512)
+        nc.vector.tensor_tensor(h_dst[:, 64:128], diff_src[:, 64:128], wt_ts_src[:, 64:128], ALU.mult)
+        quantize(h_r, E5, h_bf, 0, 256)
+        quantize(h_r, E5, h_bf, 256, 512)
+
+        quantize(w_i, E4, w_i_bf, 0, 512)
+
+        dw_sb = sb.tile([P, 4, N], F32, name="dw_sb")
+
+        def dw_block(j, copy):
+            dw_ps = bank("b0")
+            product(dw_ps, xm_r, E4, j, h_r, E5)
+            copy(dw_sb[:, j, :], dw_ps[:])
+
+        def place(j):
+            window = windows[j % WINDOWS]
+            nc.vector.tensor_copy(window[:].indirect(offsets[:]), dw_sb[:, j, :])
+            nc.sync.dma_start(out_0[j * P:(j + 1) * P, :], window[:])
+
+        dw_block(0, nc.vector.tensor_copy)
+        place(0)
+
+        h_i_bf = sb.tile([P, R * PACK], BF16, name="h_i_bf", align_bytes=64)
+        h_i_dst = h_i_bf[:].rearrange("q (u e p s) -> q u e p s", u=2, e=2, s=PACK)
+        for u, tag in ((0, "a0"), (1, "b0")):
+            turned = bank(tag)
+            turn_pairs(h_bf, u, turned)
+            nc.scalar.copy(h_i_dst[:, u], turned[:].bitcast(BF16).rearrange("q (s p e) -> q e p s", s=PACK, e=2))
+        h_i = mx_operand("h_i")
+        quantize(h_i, E5, h_i_bf, 0, 512)
+        dw_block(1, nc.scalar.copy)
+        place(1)
+        dw_block(2, nc.scalar.copy)
+        gx_sb = sb.tile([P, PACK, D], F32, name="gx_sb")
+        gx_rows = out_1[0].rearrange("(m j) d -> m j d", j=PACK)
+        for j in range(PACK):
+            gx_ps = bank("a%d" % j)
+            product(gx_ps, h_i, E5, j, w_i, E4)
+            nc.scalar.copy(gx_sb[:, j, :], gx_ps[:])
+            if j % 2 == 1:
+                nc.scalar.dma_start(gx_rows[:, j - 1:j + 1, :], gx_sb[:, j - 1:j + 1, :])
+        place(2)
+        dw_block(3, nc.scalar.copy)
+        place(3)

@@ -19,6 +19,7 @@ ACT = mybir.ActivationFunctionType
 P = 128
 PACK = 4
 WINDOWS = 3
+HALF = N // 2
 
 
 def tile_attend_glse_wx_ts_kernel(tc, xT, wT, y, lse, wt, ts, xm, offs, out_0, out_1):
@@ -40,24 +41,24 @@ def tile_attend_glse_wx_ts_kernel(tc, xT, wT, y, lse, wt, ts, xm, offs, out_0, o
             nc.vector.quantize_mx(out=codes[:, c0:c1].bitcast(fmt), scales=scales[:, c0:c1],
                                   in_=src[:, PACK * c0:PACK * c1])
 
-        def product(out, lhs, lhs_fmt, j, rhs, rhs_fmt):
+        def product(out, lhs, lhs_fmt, j, rhs, rhs_fmt, moving):
             cols = slice(j * P, (j + 1) * P)
-            nc.tensor.matmul_mx(out=out[:], lhsT=lhs[0][:, cols].bitcast(lhs_fmt), lhsT_scale=lhs[1][:, cols],
-                                rhs=rhs[0][:].bitcast(rhs_fmt), rhs_scale=rhs[1][:], start=True, stop=True)
+            nc.tensor.matmul_mx(out=out, lhsT=lhs[0][:, cols].bitcast(lhs_fmt), lhsT_scale=lhs[1][:, cols],
+                                rhs=rhs[0][:, moving].bitcast(rhs_fmt), rhs_scale=rhs[1][:, moving], start=True, stop=True)
 
         def turn_pairs(src, u, out_bank):
             words = src[:].bitcast(F32)
             for s in range(PACK):
                 nc.tensor.transpose(out_bank[:, s * P:(s + 1) * P], words[:, 2 * s + u:2 * 512:2 * PACK], ident[:])
 
-        offsets = sb.tile([P, N // 16], U16, name="offsets")
-        nc.sync.dma_start(offsets[:], offs)
         w_planes = [sb.tile([P, T], F32, name="w_plane%d" % t) for t in range(PACK)]
         wT_planes = wT.rearrange("(p t) c -> t p c", t=PACK)
-        ts_table = sb.tile([P, T], F32, name="ts_table")
-        nc.gpsimd.memset(ts_table[0:P - 1, :], 0.0)
-        nc.sync.dma_start(ts_table[P - 1:P, :], ts[0:1, :])
         nc.sync.dma_start(w_planes[0][:], wT_planes[0])
+        offsets = sb.tile([P, N // 16], U16, name="offsets")
+        nc.sync.dma_start(offsets[:], offs)
+        ts_table = sb.tile([P, T], F32, name="ts_table")
+        nc.vector.memset(ts_table[0:P - 1, :], 0.0)
+        nc.sync.dma_start(ts_table[P - 1:P, :], ts[0:1, :])
         wt_sb = sb.tile([P, PACK], F32, name="wt_sb")
         nc.sync.dma_start(wt_sb[:], wt[0].rearrange("(p t) o -> p (t o)", t=PACK))
         lse_sb = sb.tile([P, PACK], F32, name="lse_sb")
@@ -74,9 +75,12 @@ def tile_attend_glse_wx_ts_kernel(tc, xT, wT, y, lse, wt, ts, xm, offs, out_0, o
         make_identity(nc, ident[:])
         neg_lse = sb.tile([P, PACK], F32, name="neg_lse")
         nc.gpsimd.tensor_scalar(neg_lse[:], lse_sb[:], -1.0, 0.0, ALU.mult, ALU.add)
+        h_r = (sb.tile([P, HALF + N], U32, name="h_r_codes", align_bytes=64),
+               sb.tile([P, HALF + N], U8, name="h_r_scales", align_bytes=64))
+        nc.gpsimd.memset(h_r[0][:, 0:HALF], 0)
+        nc.gpsimd.memset(h_r[1][:, 0:HALF], 0)
         windows = [sb.tile([P, T], F32, name="window%d" % k) for k in range(WINDOWS)]
-        for k in range(WINDOWS):
-            nc.gpsimd.memset(windows[k][:], 0.0)
+        nc.gpsimd.memset(windows[2][:], 0.0)
 
         ts_row = sb.tile([P, N], F32, name="ts_row")
         nc.vector.tensor_copy(ts_row[:], ts_table[:].indirect(offsets[:]))
@@ -98,6 +102,9 @@ def tile_attend_glse_wx_ts_kernel(tc, xT, wT, y, lse, wt, ts, xm, offs, out_0, o
         w_bf3 = w_bf[:].rearrange("p (i t) -> p i t", t=PACK)
         for t in range(PACK):
             nc.vector.tensor_copy(w_bf3[:, :, t], w_planes[t][:].indirect(offsets[:]))
+        for k in range(2):
+            for c in range(2):
+                nc.vector.memset(windows[k][:, c * 1024:(c + 1) * 1024], 0.0)
         w_d = mx_operand("w_d")
         quantize(w_d, E4, w_bf, 0, 512)
 
@@ -110,20 +117,71 @@ def tile_attend_glse_wx_ts_kernel(tc, xT, wT, y, lse, wt, ts, xm, offs, out_0, o
         quantize(x_d, E4, x_bf, 0, 256)
         quantize(x_d, E4, x_bf, 256, 512)
 
-        scaled = sb.tile([P, PACK, N], F32, name="scaled")
-        probs = sb.tile([P, PACK, N], F32, name="probs")
-        diff = sb.tile([P, PACK, N], F32, name="diff")
-        for j in range(PACK):
-            a_ps = bank("a%d" % j)
-            product(a_ps, x_d, E4, j, w_d, E4)
-            nc.vector.tensor_tensor(scaled[:, j, :], a_ps[:], ts_all[:], ALU.mult)
-            nc.scalar.activation(probs[:, j, :], scaled[:, j, :], ACT.Exp, bias=neg_lse[:, j:j + 1], scale=1.0)
-        for j in range(PACK):
-            nc.vector.tensor_tensor(diff[:, j, :], probs[:, j, :], y_sb[:, j, :], ALU.subtract)
+        probs = []
+        for half in range(2):
+            slots = slice(half * HALF, (half + 1) * HALF)
+            scaled = sb.tile([P, PACK, HALF], F32, name="scaled%d" % half)
+            probs.append(sb.tile([P, PACK, HALF], F32, name="probs%d" % half))
+            for pair in range(2):
+                a_ps = bank("a%d" % (2 * half + pair))
+                for jj in range(2):
+                    product(a_ps[:, jj * HALF:(jj + 1) * HALF], x_d, E4, 2 * pair + jj, w_d, E4, slots)
+                nc.vector.tensor_tensor(scaled[:, 2 * pair:2 * pair + 2, :],
+                                        a_ps[:].rearrange("p (j i) -> p j i", j=2),
+                                        ts_all[:, slots].unsqueeze(1).to_broadcast([P, 2, HALF]), ALU.mult)
+                for j in range(2 * pair, 2 * pair + 2):
+                    nc.scalar.activation(probs[half][:, j, :], scaled[:, j, :], ACT.Exp,
+                                         bias=neg_lse[:, j:j + 1], scale=1.0)
 
         xm_bf = sb.tile([P, D * PACK], BF16, name="xm_bf", align_bytes=64)
-        nc.scalar.copy(xm_bf[:].rearrange("p (c i t) -> p c t i", i=4, t=PACK),
-                       xm_raw[:].rearrange("p t (c i) -> p c t i", i=4))
+        xm_dst = xm_bf[:].rearrange("p (c i t) -> p c t i", i=4, t=PACK)
+        xm_src = xm_raw[:].rearrange("p t (c i) -> p c t i", i=4)
+        for j in range(4):
+            nc.scalar.copy(xm_dst[:, 32 * j:32 * (j + 1)], xm_src[:, 32 * j:32 * (j + 1)])
+        xm_r = mx_operand("xm_r")
+
+        h_bf = sb.tile([P, N * PACK], BF16, name="h_bf", tag="h_bf", align_bytes=64)
+        h_dst = h_bf[:].rearrange("p (c i t) -> p c t i", i=4, t=PACK)
+        wt_ts_src = wt_ts[:].rearrange("p t (c i) -> p c t i", i=4)
+        diff = []
+        for half in range(2):
+            diff.append(sb.tile([P, PACK, HALF], F32, name="diff%d" % half))
+            nc.vector.tensor_tensor(diff[half][:], probs[half][:], y_sb[:, :, half * HALF:(half + 1) * HALF],
+                                    ALU.subtract)
+        dw_first = sb.tile([P, N], F32, name="dw_first")
+        for half in range(2):
+            slots = slice(half * HALF, (half + 1) * HALF)
+            quads = slice(half * HALF // 4, (half + 1) * HALF // 4)
+            nc.vector.tensor_tensor(h_dst[:, quads], diff[half][:].rearrange("p t (c i) -> p c t i", i=4),
+                                    wt_ts_src[:, quads], ALU.mult)
+            if half == 0:
+                quantize(xm_r, E4, xm_bf, 0, P)
+            else:
+                quantize(xm_r, E4, xm_bf, P, 2 * P)
+                quantize(xm_r, E4, xm_bf, 2 * P, 4 * P)
+            placed = slice((half + 1) * HALF, (half + 2) * HALF)
+            nc.vector.quantize_mx(out=h_r[0][:, placed].bitcast(E5), scales=h_r[1][:, placed],
+                                  in_=h_bf[:, PACK * half * HALF:PACK * (half + 1) * HALF])
+            dw_ps = bank("b%d" % half)
+            product(dw_ps[:], xm_r, E4, 0, h_r, E5, slice(half * HALF, half * HALF + N))
+            nc.scalar.copy(dw_first[:, slots], dw_ps[:, HALF:N])
+
+        for half in range(2):
+            nc.vector.tensor_copy(windows[0][:].indirect(offsets[:, half * HALF // 16:(half + 1) * HALF // 16]),
+                                  dw_first[:, half * HALF:(half + 1) * HALF])
+        nc.sync.dma_start(out_0[0:P, :], windows[0][:])
+
+        def dw_block(j, tag):
+            dw_ps = bank("b2")
+            product(dw_ps[:], xm_r, E4, j, h_r, E5, slice(HALF, HALF + N))
+            dw_sb = sb.tile([P, N], F32, name="dw_sb%d" % j, tag=tag, align_bytes=64)
+            nc.scalar.copy(dw_sb[:], dw_ps[:])
+            return dw_sb
+
+        def place(j, dw_sb):
+            window = windows[j % WINDOWS]
+            nc.vector.tensor_copy(window[:].indirect(offsets[:]), dw_sb[:])
+            nc.sync.dma_start(out_0[j * P:(j + 1) * P, :], window[:])
 
         w_i_bf = sb.tile([P, D * PACK], BF16, name="w_i_bf", align_bytes=64)
         w_i_dst = w_i_bf[:].rearrange("q (p u e s) -> q u p e s", u=2, e=2, s=PACK)
@@ -132,55 +190,25 @@ def tile_attend_glse_wx_ts_kernel(tc, xT, wT, y, lse, wt, ts, xm, offs, out_0, o
             turn_pairs(w_bf, u, turned)
             nc.scalar.copy(w_i_dst[:, u], turned[:].bitcast(BF16).rearrange("q (s p e) -> q p e s", s=PACK, e=2))
         w_i = mx_operand("w_i")
-
-        h_bf = sb.tile([P, N * PACK], BF16, name="h_bf", align_bytes=64)
-        h_dst = h_bf[:].rearrange("p (c i t) -> p c t i", i=4, t=PACK)
-        diff_src = diff[:].rearrange("p t (c i) -> p c t i", i=4)
-        wt_ts_src = wt_ts[:].rearrange("p t (c i) -> p c t i", i=4)
-        xm_r = mx_operand("xm_r")
-        h_r = mx_operand("h_r")
-        nc.vector.tensor_tensor(h_dst[:, 0:64], diff_src[:, 0:64], wt_ts_src[:, 0:64], ALU.mult)
-        quantize(xm_r, E4, xm_bf, 0, 512)
-        nc.vector.tensor_tensor(h_dst[:, 64:128], diff_src[:, 64:128], wt_ts_src[:, 64:128], ALU.mult)
-        quantize(h_r, E5, h_bf, 0, 256)
-        quantize(h_r, E5, h_bf, 256, 512)
-
         quantize(w_i, E4, w_i_bf, 0, 512)
-
-        dw_sb = sb.tile([P, 4, N], F32, name="dw_sb")
-
-        def dw_block(j, copy):
-            dw_ps = bank("b0")
-            product(dw_ps, xm_r, E4, j, h_r, E5)
-            copy(dw_sb[:, j, :], dw_ps[:])
-
-        def place(j):
-            window = windows[j % WINDOWS]
-            nc.vector.tensor_copy(window[:].indirect(offsets[:]), dw_sb[:, j, :])
-            nc.sync.dma_start(out_0[j * P:(j + 1) * P, :], window[:])
-
-        dw_block(0, nc.vector.tensor_copy)
-        place(0)
 
         h_i_bf = sb.tile([P, R * PACK], BF16, name="h_i_bf", align_bytes=64)
         h_i_dst = h_i_bf[:].rearrange("q (u e p s) -> q u e p s", u=2, e=2, s=PACK)
-        for u, tag in ((0, "a0"), (1, "b0")):
-            turned = bank(tag)
+        for u in range(2):
+            turned = bank("a%d" % u)
             turn_pairs(h_bf, u, turned)
             nc.scalar.copy(h_i_dst[:, u], turned[:].bitcast(BF16).rearrange("q (s p e) -> q e p s", s=PACK, e=2))
         h_i = mx_operand("h_i")
         quantize(h_i, E5, h_i_bf, 0, 512)
-        dw_block(1, nc.scalar.copy)
-        place(1)
-        dw_block(2, nc.scalar.copy)
+        place(1, dw_block(1, "h_bf"))
+        dw_2 = dw_block(2, "dw_2")
         gx_sb = sb.tile([P, PACK, D], F32, name="gx_sb")
         gx_rows = out_1[0].rearrange("(m j) d -> m j d", j=PACK)
-        for j in range(PACK):
-            gx_ps = bank("a%d" % j)
-            product(gx_ps, h_i, E5, j, w_i, E4)
+        for j, tag in enumerate(("b0", "b1", "a2", "b3")):
+            gx_ps = bank(tag)
+            product(gx_ps[:], h_i, E5, j, w_i, E4, slice(0, D))
             nc.scalar.copy(gx_sb[:, j, :], gx_ps[:])
             if j % 2 == 1:
                 nc.scalar.dma_start(gx_rows[:, j - 1:j + 1, :], gx_sb[:, j - 1:j + 1, :])
-        place(2)
-        dw_block(3, nc.scalar.copy)
-        place(3)
+        place(2, dw_2)
+        place(3, dw_block(3, "dw_3"))

@@ -51,13 +51,16 @@ def tile_attend_glse_wx_ts_kernel(tc, xT, wT, y, lse, wt, ts, xm, offs, out_0, o
             for s in range(PACK):
                 nc.tensor.transpose(out_bank[:, s * P:(s + 1) * P], words[:, 2 * s + u:2 * 512:2 * PACK], ident[:])
 
+        def list_half(half):
+            return offsets[:, half * HALF // 16:(half + 1) * HALF // 16]
+
         w_planes = [sb.tile([P, T], F32, name="w_plane%d" % t) for t in range(PACK)]
         wT_planes = wT.rearrange("(p t) c -> t p c", t=PACK)
         nc.sync.dma_start(w_planes[0][:], wT_planes[0])
         offsets = sb.tile([P, N // 16], U16, name="offsets")
         nc.sync.dma_start(offsets[:], offs)
         ts_table = sb.tile([P, T], F32, name="ts_table")
-        nc.vector.memset(ts_table[0:P - 1, :], 0.0)
+        nc.gpsimd.memset(ts_table[0:P - 1, :], 0.0)
         nc.sync.dma_start(ts_table[P - 1:P, :], ts[0:1, :])
         wt_sb = sb.tile([P, PACK], F32, name="wt_sb")
         nc.sync.dma_start(wt_sb[:], wt[0].rearrange("(p t) o -> p (t o)", t=PACK))
@@ -80,7 +83,6 @@ def tile_attend_glse_wx_ts_kernel(tc, xT, wT, y, lse, wt, ts, xm, offs, out_0, o
         nc.gpsimd.memset(h_r[0][:, 0:HALF], 0)
         nc.gpsimd.memset(h_r[1][:, 0:HALF], 0)
         windows = [sb.tile([P, T], F32, name="window%d" % k) for k in range(WINDOWS)]
-        nc.gpsimd.memset(windows[2][:], 0.0)
 
         ts_row = sb.tile([P, N], F32, name="ts_row")
         nc.vector.tensor_copy(ts_row[:], ts_table[:].indirect(offsets[:]))
@@ -100,13 +102,16 @@ def tile_attend_glse_wx_ts_kernel(tc, xT, wT, y, lse, wt, ts, xm, offs, out_0, o
 
         w_bf = sb.tile([P, N * PACK], BF16, name="w_bf", align_bytes=64)
         w_bf3 = w_bf[:].rearrange("p (i t) -> p i t", t=PACK)
-        for t in range(PACK):
+        for t in range(PACK - 1):
             nc.vector.tensor_copy(w_bf3[:, :, t], w_planes[t][:].indirect(offsets[:]))
-        for k in range(2):
+        for half in range(2):
+            nc.vector.tensor_copy(w_bf3[:, half * HALF:(half + 1) * HALF, PACK - 1],
+                                  w_planes[PACK - 1][:].indirect(list_half(half)))
+        for k in range(WINDOWS):
             for c in range(2):
                 nc.vector.memset(windows[k][:, c * 1024:(c + 1) * 1024], 0.0)
         w_d = mx_operand("w_d")
-        quantize(w_d, E4, w_bf, 0, 512)
+        quantize(w_d, E4, w_bf, 0, HALF)
 
         x_bf = sb.tile([P, R * PACK], BF16, name="x_bf", align_bytes=64)
         x_dst = x_bf[:].rearrange("p (j m t) -> p m t j", j=PACK, t=PACK)
@@ -114,22 +119,25 @@ def tile_attend_glse_wx_ts_kernel(tc, xT, wT, y, lse, wt, ts, xm, offs, out_0, o
         nc.vector.tensor_copy(x_dst[:, :, :, 0:2], x_src[:, :, :, 0:2])
         nc.scalar.copy(x_dst[:, :, :, 2:4], x_src[:, :, :, 2:4])
         x_d = mx_operand("x_d")
-        quantize(x_d, E4, x_bf, 0, 256)
-        quantize(x_d, E4, x_bf, 256, 512)
+        quantize(w_d, E4, w_bf, HALF, N)
+        quantize(x_d, E4, x_bf, 0, P)
+        quantize(x_d, E4, x_bf, P, 2 * P)
+        quantize(x_d, E4, x_bf, 2 * P, 4 * P)
 
         probs = []
+        score_banks = (((0, 1, "b3"), (1, 2, "a0"), (2, 4, "a1")), ((0, 2, "a2"), (2, 4, "a3")))
         for half in range(2):
             slots = slice(half * HALF, (half + 1) * HALF)
             scaled = sb.tile([P, PACK, HALF], F32, name="scaled%d" % half)
             probs.append(sb.tile([P, PACK, HALF], F32, name="probs%d" % half))
-            for pair in range(2):
-                a_ps = bank("a%d" % (2 * half + pair))
-                for jj in range(2):
-                    product(a_ps[:, jj * HALF:(jj + 1) * HALF], x_d, E4, 2 * pair + jj, w_d, E4, slots)
-                nc.vector.tensor_tensor(scaled[:, 2 * pair:2 * pair + 2, :],
-                                        a_ps[:].rearrange("p (j i) -> p j i", j=2),
-                                        ts_all[:, slots].unsqueeze(1).to_broadcast([P, 2, HALF]), ALU.mult)
-                for j in range(2 * pair, 2 * pair + 2):
+            for j0, j1, tag in score_banks[half]:
+                a_ps = bank(tag)
+                for j in range(j0, j1):
+                    product(a_ps[:, (j - j0) * HALF:(j - j0 + 1) * HALF], x_d, E4, j, w_d, E4, slots)
+                nc.vector.tensor_tensor(scaled[:, j0:j1, :],
+                                        a_ps[:, 0:(j1 - j0) * HALF].rearrange("p (j i) -> p j i", i=HALF),
+                                        ts_all[:, slots].unsqueeze(1).to_broadcast([P, j1 - j0, HALF]), ALU.mult)
+                for j in range(j0, j1):
                     nc.scalar.activation(probs[half][:, j, :], scaled[:, j, :], ACT.Exp,
                                          bias=neg_lse[:, j:j + 1], scale=1.0)
 
@@ -167,12 +175,12 @@ def tile_attend_glse_wx_ts_kernel(tc, xT, wT, y, lse, wt, ts, xm, offs, out_0, o
             nc.scalar.copy(dw_first[:, slots], dw_ps[:, HALF:N])
 
         for half in range(2):
-            nc.vector.tensor_copy(windows[0][:].indirect(offsets[:, half * HALF // 16:(half + 1) * HALF // 16]),
+            nc.vector.tensor_copy(windows[0][:].indirect(list_half(half)),
                                   dw_first[:, half * HALF:(half + 1) * HALF])
         nc.sync.dma_start(out_0[0:P, :], windows[0][:])
 
-        def dw_block(j, tag):
-            dw_ps = bank("b2")
+        def dw_block(j, bank_tag, tag):
+            dw_ps = bank(bank_tag)
             product(dw_ps[:], xm_r, E4, j, h_r, E5, slice(HALF, HALF + N))
             dw_sb = sb.tile([P, N], F32, name="dw_sb%d" % j, tag=tag, align_bytes=64)
             nc.scalar.copy(dw_sb[:], dw_ps[:])
@@ -182,6 +190,8 @@ def tile_attend_glse_wx_ts_kernel(tc, xT, wT, y, lse, wt, ts, xm, offs, out_0, o
             window = windows[j % WINDOWS]
             nc.vector.tensor_copy(window[:].indirect(offsets[:]), dw_sb[:])
             nc.sync.dma_start(out_0[j * P:(j + 1) * P, :], window[:])
+
+        place(1, dw_block(1, "a0", "dw_1"))
 
         w_i_bf = sb.tile([P, D * PACK], BF16, name="w_i_bf", align_bytes=64)
         w_i_dst = w_i_bf[:].rearrange("q (p u e s) -> q u p e s", u=2, e=2, s=PACK)
@@ -194,21 +204,21 @@ def tile_attend_glse_wx_ts_kernel(tc, xT, wT, y, lse, wt, ts, xm, offs, out_0, o
 
         h_i_bf = sb.tile([P, R * PACK], BF16, name="h_i_bf", align_bytes=64)
         h_i_dst = h_i_bf[:].rearrange("q (u e p s) -> q u e p s", u=2, e=2, s=PACK)
-        for u in range(2):
-            turned = bank("a%d" % u)
+        for u, tag in ((0, "b1"), (1, "a0")):
+            turned = bank(tag)
             turn_pairs(h_bf, u, turned)
             nc.scalar.copy(h_i_dst[:, u], turned[:].bitcast(BF16).rearrange("q (s p e) -> q e p s", s=PACK, e=2))
         h_i = mx_operand("h_i")
         quantize(h_i, E5, h_i_bf, 0, 512)
-        place(1, dw_block(1, "h_bf"))
-        dw_2 = dw_block(2, "dw_2")
+        dw_2 = dw_block(2, "a1", "h_bf")
+        dw_3 = dw_block(3, "a1", "dw_3")
         gx_sb = sb.tile([P, PACK, D], F32, name="gx_sb")
         gx_rows = out_1[0].rearrange("(m j) d -> m j d", j=PACK)
-        for j, tag in enumerate(("b0", "b1", "a2", "b3")):
+        for j, tag in enumerate(("b0", "b2", "a2", "b3")):
             gx_ps = bank(tag)
             product(gx_ps[:], h_i, E5, j, w_i, E4, slice(0, D))
             nc.scalar.copy(gx_sb[:, j, :], gx_ps[:])
             if j % 2 == 1:
                 nc.scalar.dma_start(gx_rows[:, j - 1:j + 1, :], gx_sb[:, j - 1:j + 1, :])
         place(2, dw_2)
-        place(3, dw_block(3, "dw_3"))
+        place(3, dw_3)

@@ -46,10 +46,12 @@ def tile_attend_glse_wx_ts_kernel(tc, xT, wT, y, lse, wt, ts, xm, offs, out_0, o
             nc.tensor.matmul_mx(out=out, lhsT=lhs[0][:, cols].bitcast(lhs_fmt), lhsT_scale=lhs[1][:, cols],
                                 rhs=rhs[0][:, moving].bitcast(rhs_fmt), rhs_scale=rhs[1][:, moving], start=True, stop=True)
 
-        def turn_pairs(src, u, out_bank):
+        def turn_words(out_bank, src, first_word, step):
             words = src[:].bitcast(F32)
             for s in range(PACK):
-                nc.tensor.transpose(out_bank[:, s * P:(s + 1) * P], words[:, 2 * s + u:2 * 512:2 * PACK], ident[:])
+                start = first_word(s)
+                nc.tensor.transpose(out_bank[:, s * P:(s + 1) * P],
+                                    words[:, start:start + (P - 1) * step + 1:step], ident[:])
 
         def list_half(half):
             return offsets[:, half * HALF // 16:(half + 1) * HALF // 16]
@@ -60,7 +62,7 @@ def tile_attend_glse_wx_ts_kernel(tc, xT, wT, y, lse, wt, ts, xm, offs, out_0, o
         offsets = sb.tile([P, N // 16], U16, name="offsets")
         nc.sync.dma_start(offsets[:], offs)
         ts_table = sb.tile([P, T], F32, name="ts_table")
-        nc.gpsimd.memset(ts_table[0:P - 1, :], 0.0)
+        nc.vector.memset(ts_table[0:P - 1, :], 0.0)
         nc.sync.dma_start(ts_table[P - 1:P, :], ts[0:1, :])
         wt_sb = sb.tile([P, PACK], F32, name="wt_sb")
         nc.sync.dma_start(wt_sb[:], wt[0].rearrange("(p t) o -> p (t o)", t=PACK))
@@ -72,7 +74,7 @@ def tile_attend_glse_wx_ts_kernel(tc, xT, wT, y, lse, wt, ts, xm, offs, out_0, o
         nc.sync.dma_start(x_raw[:], xT[0].rearrange("(p t) r -> p t r", t=PACK))
         y_sb = sb.tile([P, PACK, N], F32, name="y_sb")
         nc.sync.dma_start(y_sb[:], y[0].rearrange("(p t) i -> p t i", t=PACK))
-        xm_raw = sb.tile([P, PACK, D], F32, name="xm_raw")
+        xm_raw = sb.tile([P, PACK, D], F32, name="xm_raw", tag="xm_raw", align_bytes=64)
         nc.sync.dma_start(xm_raw[:], xm[0].rearrange("(p t) d -> p t d", t=PACK))
         ident = sb.tile([P, P], F32, name="ident")
         make_identity(nc, ident[:])
@@ -83,6 +85,7 @@ def tile_attend_glse_wx_ts_kernel(tc, xT, wT, y, lse, wt, ts, xm, offs, out_0, o
         nc.gpsimd.memset(h_r[0][:, 0:HALF], 0)
         nc.gpsimd.memset(h_r[1][:, 0:HALF], 0)
         windows = [sb.tile([P, T], F32, name="window%d" % k) for k in range(WINDOWS)]
+        nc.gpsimd.memset(windows[2][:], 0.0)
 
         ts_row = sb.tile([P, N], F32, name="ts_row")
         nc.vector.tensor_copy(ts_row[:], ts_table[:].indirect(offsets[:]))
@@ -102,12 +105,16 @@ def tile_attend_glse_wx_ts_kernel(tc, xT, wT, y, lse, wt, ts, xm, offs, out_0, o
 
         w_bf = sb.tile([P, N * PACK], BF16, name="w_bf", align_bytes=64)
         w_bf3 = w_bf[:].rearrange("p (i t) -> p i t", t=PACK)
-        for t in range(PACK - 1):
-            nc.vector.tensor_copy(w_bf3[:, :, t], w_planes[t][:].indirect(offsets[:]))
+        w_low = sb.tile([P, N * 2], BF16, name="w_low", align_bytes=64)
+        w_low3 = w_low[:].rearrange("p (i e) -> p i e", e=2)
+        for t in range(2):
+            nc.vector.tensor_copy(w_low3[:, :, t], w_planes[t][:].indirect(offsets[:]))
+        nc.vector.tensor_copy(w_bf3[:, :, 0:2], w_low3)
+        nc.vector.tensor_copy(w_bf3[:, :, 2], w_planes[2][:].indirect(offsets[:]))
         for half in range(2):
             nc.vector.tensor_copy(w_bf3[:, half * HALF:(half + 1) * HALF, PACK - 1],
                                   w_planes[PACK - 1][:].indirect(list_half(half)))
-        for k in range(WINDOWS):
+        for k in range(2):
             for c in range(2):
                 nc.vector.memset(windows[k][:, c * 1024:(c + 1) * 1024], 0.0)
         w_d = mx_operand("w_d")
@@ -149,41 +156,59 @@ def tile_attend_glse_wx_ts_kernel(tc, xT, wT, y, lse, wt, ts, xm, offs, out_0, o
         xm_r = mx_operand("xm_r")
 
         h_bf = sb.tile([P, N * PACK], BF16, name="h_bf", tag="h_bf", align_bytes=64)
-        h_dst = h_bf[:].rearrange("p (c i t) -> p c t i", i=4, t=PACK)
+        h_dst = h_bf[:].rearrange("p (s c t) -> p c t s", s=PACK, t=PACK)
         wt_ts_src = wt_ts[:].rearrange("p t (c i) -> p c t i", i=4)
-        diff = []
-        for half in range(2):
-            diff.append(sb.tile([P, PACK, HALF], F32, name="diff%d" % half))
-            nc.vector.tensor_tensor(diff[half][:], probs[half][:], y_sb[:, :, half * HALF:(half + 1) * HALF],
-                                    ALU.subtract)
-        dw_first = sb.tile([P, N], F32, name="dw_first")
-        for half in range(2):
-            slots = slice(half * HALF, (half + 1) * HALF)
-            quads = slice(half * HALF // 4, (half + 1) * HALF // 4)
-            nc.vector.tensor_tensor(h_dst[:, quads], diff[half][:].rearrange("p t (c i) -> p c t i", i=4),
-                                    wt_ts_src[:, quads], ALU.mult)
-            if half == 0:
-                quantize(xm_r, E4, xm_bf, 0, P)
-            else:
-                quantize(xm_r, E4, xm_bf, P, 2 * P)
-                quantize(xm_r, E4, xm_bf, 2 * P, 4 * P)
-            placed = slice((half + 1) * HALF, (half + 2) * HALF)
-            nc.vector.quantize_mx(out=h_r[0][:, placed].bitcast(E5), scales=h_r[1][:, placed],
-                                  in_=h_bf[:, PACK * half * HALF:PACK * (half + 1) * HALF])
-            dw_ps = bank("b%d" % half)
-            product(dw_ps[:], xm_r, E4, 0, h_r, E5, slice(half * HALF, half * HALF + N))
-            nc.scalar.copy(dw_first[:, slots], dw_ps[:, HALF:N])
+        dw_first_ps = []
+
+        def copy_first(half):
+            nc.scalar.copy(dw_first[:, half * HALF:(half + 1) * HALF].rearrange("p (c s) -> p c s", s=PACK),
+                           dw_first_ps[half][:, HALF:N].rearrange("p (s c) -> p c s", s=PACK))
 
         for half in range(2):
-            nc.vector.tensor_copy(windows[0][:].indirect(list_half(half)),
-                                  dw_first[:, half * HALF:(half + 1) * HALF])
+            slots = slice(half * HALF, (half + 1) * HALF)
+            if half == 0:
+                diff = sb.tile([P, PACK, HALF], F32, name="diff_first", tag="diff")
+                for j in range(2):
+                    nc.gpsimd.tensor_tensor(diff[:, j, :], probs[0][:, j, :], y_sb[:, j, slots], ALU.subtract)
+                nc.vector.tensor_tensor(diff[:, 2:4, :], probs[0][:, 2:4, :], y_sb[:, 2:4, slots], ALU.subtract)
+                parts = [(0, HALF, diff[:])]
+            else:
+                parts = []
+                diff = sb.tile([P, 2, PACK, P], F32, name="diff_second", tag="diff")
+                for part in range(2):
+                    i0 = HALF + part * P
+                    nc.vector.tensor_tensor(diff[:, part], probs[1][:, :, part * P:(part + 1) * P],
+                                            y_sb[:, :, i0:i0 + P], ALU.subtract)
+                    parts.append((i0, i0 + P, diff[:, part]))
+            for i0, i1, diff_part in parts:
+                quads = slice(i0 // 4, i1 // 4)
+                nc.vector.tensor_tensor(h_dst[:, quads], diff_part.rearrange("p t (c i) -> p c t i", i=4),
+                                        wt_ts_src[:, quads], ALU.mult)
+            if half == 1:
+                dw_first = sb.tile([P, N], F32, name="dw_first", tag="diff")
+                copy_first(0)
+            quantize(xm_r, E4, xm_bf, half * P, (half + 1) * P)
+            for s in range(PACK):
+                placed = slice((half + 1) * HALF + s * 64, (half + 1) * HALF + (s + 1) * 64)
+                first = s * N + half * HALF
+                nc.vector.quantize_mx(out=h_r[0][:, placed].bitcast(E5), scales=h_r[1][:, placed],
+                                      in_=h_bf[:, first:first + HALF])
+            dw_ps = bank("b%d" % half)
+            product(dw_ps[:], xm_r, E4, 0, h_r, E5, slice(half * HALF, half * HALF + N))
+            dw_first_ps.append(dw_ps)
+        copy_first(1)
+
+        quantize(xm_r, E4, xm_bf, 2 * P, 4 * P)
+        nc.vector.tensor_copy(windows[0][:].indirect(list_half(0)), dw_first[:, 0:HALF])
+        nc.vector.tensor_copy(windows[0][:].indirect(list_half(1)), dw_first[:, HALF:N])
         nc.sync.dma_start(out_0[0:P, :], windows[0][:])
 
         def dw_block(j, bank_tag, tag):
             dw_ps = bank(bank_tag)
             product(dw_ps[:], xm_r, E4, j, h_r, E5, slice(HALF, HALF + N))
             dw_sb = sb.tile([P, N], F32, name="dw_sb%d" % j, tag=tag, align_bytes=64)
-            nc.scalar.copy(dw_sb[:], dw_ps[:])
+            nc.scalar.copy(dw_sb[:].rearrange("p (g c s) -> p g c s", g=2, s=PACK),
+                           dw_ps[:].rearrange("p (g s c) -> p g c s", g=2, s=PACK))
             return dw_sb
 
         def place(j, dw_sb):
@@ -191,34 +216,37 @@ def tile_attend_glse_wx_ts_kernel(tc, xT, wT, y, lse, wt, ts, xm, offs, out_0, o
             nc.vector.tensor_copy(window[:].indirect(offsets[:]), dw_sb[:])
             nc.sync.dma_start(out_0[j * P:(j + 1) * P, :], window[:])
 
-        place(1, dw_block(1, "a0", "dw_1"))
-
-        w_i_bf = sb.tile([P, D * PACK], BF16, name="w_i_bf", align_bytes=64)
-        w_i_dst = w_i_bf[:].rearrange("q (p u e s) -> q u p e s", u=2, e=2, s=PACK)
-        for u, tag in ((0, "b2"), (1, "a3")):
-            turned = bank(tag)
-            turn_pairs(w_bf, u, turned)
-            nc.scalar.copy(w_i_dst[:, u], turned[:].bitcast(BF16).rearrange("q (s p e) -> q p e s", s=PACK, e=2))
         w_i = mx_operand("w_i")
-        quantize(w_i, E4, w_i_bf, 0, 512)
+        for u, bank_tag, tag in ((0, "b2", "w_i_low"), (1, "a3", "xm_raw")):
+            turned = bank(bank_tag)
+            if u == 0:
+                turn_words(turned, w_low, lambda s: s, PACK)
+            else:
+                turn_words(turned, w_bf, lambda s: 2 * s + 1, 2 * PACK)
+            w_i_bf = sb.tile([P, HALF * PACK], BF16, name="w_i_bf%d" % u, tag=tag, align_bytes=64)
+            nc.scalar.copy(w_i_bf[:].rearrange("q (p e s) -> q p e s", e=2, s=PACK),
+                           turned[:].bitcast(BF16).rearrange("q (s p e) -> q p e s", s=PACK, e=2))
+            placed = slice(u * HALF, (u + 1) * HALF)
+            nc.vector.quantize_mx(out=w_i[0][:, placed].bitcast(E4), scales=w_i[1][:, placed], in_=w_i_bf[:])
 
         h_i_bf = sb.tile([P, R * PACK], BF16, name="h_i_bf", align_bytes=64)
         h_i_dst = h_i_bf[:].rearrange("q (u e p s) -> q u e p s", u=2, e=2, s=PACK)
-        for u, tag in ((0, "b1"), (1, "a0")):
+        for u, tag in ((0, "a0"), (1, "a1")):
             turned = bank(tag)
-            turn_pairs(h_bf, u, turned)
+            turn_words(turned, h_bf, lambda s: 2 * P * s + u, 2)
             nc.scalar.copy(h_i_dst[:, u], turned[:].bitcast(BF16).rearrange("q (s p e) -> q e p s", s=PACK, e=2))
         h_i = mx_operand("h_i")
         quantize(h_i, E5, h_i_bf, 0, 512)
-        dw_2 = dw_block(2, "a1", "h_bf")
-        dw_3 = dw_block(3, "a1", "dw_3")
+        place(1, dw_block(1, "b2", "h_bf"))
+        dw_2 = dw_block(2, "b2", "dw_2")
         gx_sb = sb.tile([P, PACK, D], F32, name="gx_sb")
         gx_rows = out_1[0].rearrange("(m j) d -> m j d", j=PACK)
-        for j, tag in enumerate(("b0", "b2", "a2", "b3")):
+        for j, tag in enumerate(("b0", "b1", "a2", "b3")):
             gx_ps = bank(tag)
             product(gx_ps[:], h_i, E5, j, w_i, E4, slice(0, D))
-            nc.scalar.copy(gx_sb[:, j, :], gx_ps[:])
+            nc.scalar.copy(gx_sb[:, j, :].rearrange("m (p u e) -> m p u e", u=2, e=2),
+                           gx_ps[:].rearrange("m (u p e) -> m p u e", u=2, e=2))
             if j % 2 == 1:
                 nc.scalar.dma_start(gx_rows[:, j - 1:j + 1, :], gx_sb[:, j - 1:j + 1, :])
         place(2, dw_2)
-        place(3, dw_3)
+        place(3, dw_block(3, "b2", "dw_3"))

@@ -31,8 +31,8 @@ def tile_attend_glse_wx_ts_kernel(tc, xT, wT, y, lse, wt, ts, xm, offs, out_0, o
         def bank(tag):
             return ps.tile([P, 512], F32, name=tag, tag=tag)
 
-        def mx_operand(name):
-            codes = sb.tile([P, 512], U32, name=name + "_codes", align_bytes=64)
+        def mx_operand(name, tag=None):
+            codes = sb.tile([P, 512], U32, name=name + "_codes", tag=tag or name + "_codes", align_bytes=64)
             scales = sb.tile([P, 512], U8, name=name + "_scales", align_bytes=64)
             return codes, scales
 
@@ -56,26 +56,29 @@ def tile_attend_glse_wx_ts_kernel(tc, xT, wT, y, lse, wt, ts, xm, offs, out_0, o
         def list_half(half):
             return offsets[:, half * HALF // 16:(half + 1) * HALF // 16]
 
-        w_planes = [sb.tile([P, T], F32, name="w_plane%d" % t) for t in range(PACK)]
+        w_planes = [sb.tile([P, T], F32, name="w_plane%d" % t, tag="w_plane%d" % t, align_bytes=64) for t in range(PACK)]
         wT_planes = wT.rearrange("(p t) c -> t p c", t=PACK)
-        nc.sync.dma_start(w_planes[0][:], wT_planes[0])
         offsets = sb.tile([P, N // 16], U16, name="offsets")
         nc.sync.dma_start(offsets[:], offs)
+        nc.sync.dma_start(w_planes[0][:], wT_planes[0])
         ts_table = sb.tile([P, T], F32, name="ts_table")
-        nc.vector.memset(ts_table[0:P - 1, :], 0.0)
-        nc.sync.dma_start(ts_table[P - 1:P, :], ts[0:1, :])
+        nc.scalar.dma_start(ts_table[P - 1:P, :], ts[0:1, :])
         wt_sb = sb.tile([P, PACK], F32, name="wt_sb")
         nc.sync.dma_start(wt_sb[:], wt[0].rearrange("(p t) o -> p (t o)", t=PACK))
         lse_sb = sb.tile([P, PACK], F32, name="lse_sb")
         nc.sync.dma_start(lse_sb[:], lse[0].rearrange("(p t) o -> p (t o)", t=PACK))
         for t in range(1, PACK):
             nc.sync.dma_start(w_planes[t][:], wT_planes[t])
-        x_raw = sb.tile([P, PACK, R], F32, name="x_raw")
-        nc.sync.dma_start(x_raw[:], xT[0].rearrange("(p t) r -> p t r", t=PACK))
+        x_raw = []
+        for part in range(2):
+            x_raw.append(sb.tile([P, PACK, R // 2], F32, name="x_raw%d" % part))
+            nc.sync.dma_start(x_raw[part][:],
+                              xT[0].rearrange("(p t) r -> p t r", t=PACK)[:, :, part * R // 2:(part + 1) * R // 2])
         y_sb = sb.tile([P, PACK, N], F32, name="y_sb")
         nc.sync.dma_start(y_sb[:], y[0].rearrange("(p t) i -> p t i", t=PACK))
         xm_raw = sb.tile([P, PACK, D], F32, name="xm_raw", tag="xm_raw", align_bytes=64)
         nc.sync.dma_start(xm_raw[:], xm[0].rearrange("(p t) d -> p t d", t=PACK))
+        nc.vector.memset(ts_table[0:P - 1, :], 0.0)
         ident = sb.tile([P, P], F32, name="ident")
         make_identity(nc, ident[:])
         neg_lse = sb.tile([P, PACK], F32, name="neg_lse")
@@ -85,18 +88,17 @@ def tile_attend_glse_wx_ts_kernel(tc, xT, wT, y, lse, wt, ts, xm, offs, out_0, o
         nc.gpsimd.memset(h_r[0][:, 0:HALF], 0)
         nc.gpsimd.memset(h_r[1][:, 0:HALF], 0)
         windows = [sb.tile([P, T], F32, name="window%d" % k) for k in range(WINDOWS)]
-        nc.gpsimd.memset(windows[2][:], 0.0)
 
         ts_row = sb.tile([P, N], F32, name="ts_row")
         nc.vector.tensor_copy(ts_row[:], ts_table[:].indirect(offsets[:]))
-        ts_cols = bank("b0")
+        ts_cols_ps = bank("b0")
         for k in range(4):
-            nc.tensor.transpose(ts_cols[:, k * P:(k + 1) * P], ts_row[:, k * P:(k + 1) * P], ident[:])
-        ts_rep = sb.tile([P, 4, P], F32, name="ts_rep")
-        nc.scalar.copy(ts_rep[:], ts_cols[:].rearrange("q (k m) -> q k m", k=4)[:, :, P - 1:P].to_broadcast([P, 4, P]))
+            nc.tensor.transpose(ts_cols_ps[:, k * P:(k + 1) * P], ts_row[:, k * P:(k + 1) * P], ident[:])
+        ts_cols = sb.tile([P, 4], F32, name="ts_cols")
+        nc.scalar.copy(ts_cols[:], ts_cols_ps[:, P - 1:N:P])
         ts_all_ps = bank("b1")
         for k in range(4):
-            nc.tensor.transpose(ts_all_ps[:, k * P:(k + 1) * P], ts_rep[:, k, :], ident[:])
+            nc.tensor.transpose(ts_all_ps[:, k * P:(k + 1) * P], ts_cols[:, k:k + 1].to_broadcast([P, P]), ident[:])
         ts_all = sb.tile([P, N], F32, name="ts_all")
         nc.scalar.copy(ts_all[:], ts_all_ps[:])
         wt_ts = sb.tile([P, PACK, N], F32, name="wt_ts")
@@ -104,49 +106,46 @@ def tile_attend_glse_wx_ts_kernel(tc, xT, wT, y, lse, wt, ts, xm, offs, out_0, o
             nc.scalar.activation(wt_ts[:, t, :], ts_all_ps[:], ACT.Copy, scale=wt_sb[:, t:t + 1])
 
         w_bf = sb.tile([P, N * PACK], BF16, name="w_bf", align_bytes=64)
-        w_bf3 = w_bf[:].rearrange("p (i t) -> p i t", t=PACK)
+        w_dealt = w_bf[:].rearrange("p (s c t) -> p c s t", s=PACK, t=PACK)
         w_low = sb.tile([P, N * 2], BF16, name="w_low", align_bytes=64)
-        w_low3 = w_low[:].rearrange("p (i e) -> p i e", e=2)
+        w_low_dealt = w_low[:].rearrange("p (s c e) -> p c s e", s=PACK, e=2)
         for t in range(2):
-            nc.vector.tensor_copy(w_low3[:, :, t], w_planes[t][:].indirect(offsets[:]))
-        nc.vector.tensor_copy(w_bf3[:, :, 0:2], w_low3)
-        nc.vector.tensor_copy(w_bf3[:, :, 2], w_planes[2][:].indirect(offsets[:]))
-        for half in range(2):
-            nc.vector.tensor_copy(w_bf3[:, half * HALF:(half + 1) * HALF, PACK - 1],
-                                  w_planes[PACK - 1][:].indirect(list_half(half)))
-        for k in range(2):
-            for c in range(2):
-                nc.vector.memset(windows[k][:, c * 1024:(c + 1) * 1024], 0.0)
+            nc.vector.tensor_copy(w_low_dealt[:, :, :, t], w_planes[t][:].indirect(offsets[:]))
+        nc.vector.tensor_copy(w_bf[:].bitcast(F32)[:, 0:2 * N:2], w_low[:].bitcast(F32))
+        for t in range(2, PACK):
+            nc.vector.tensor_copy(w_dealt[:, :, :, t], w_planes[t][:].indirect(offsets[:]))
         w_d = mx_operand("w_d")
-        quantize(w_d, E4, w_bf, 0, HALF)
+        quantize(w_d, E4, w_bf, 0, N)
 
         x_bf = sb.tile([P, R * PACK], BF16, name="x_bf", align_bytes=64)
         x_dst = x_bf[:].rearrange("p (j m t) -> p m t j", j=PACK, t=PACK)
-        x_src = x_raw[:].rearrange("p t (m j) -> p m t j", j=PACK)
-        nc.vector.tensor_copy(x_dst[:, :, :, 0:2], x_src[:, :, :, 0:2])
-        nc.scalar.copy(x_dst[:, :, :, 2:4], x_src[:, :, :, 2:4])
+        x_src = [x_raw[part][:].rearrange("p t (m j) -> p m t j", j=PACK) for part in range(2)]
+        nc.scalar.copy(x_dst[:, 0:64, :, 0:2], x_src[0][:, :, :, 0:2])
+        nc.scalar.copy(x_dst[:, 0:64, :, 2:4], x_src[0][:, :, :, 2:4])
+        nc.vector.tensor_copy(x_dst[:, 64:128, :, 0:2], x_src[1][:, :, :, 0:2])
+        nc.scalar.copy(x_dst[:, 64:128, :, 2:4], x_src[1][:, :, :, 2:4])
         x_d = mx_operand("x_d")
-        quantize(w_d, E4, w_bf, HALF, N)
         quantize(x_d, E4, x_bf, 0, P)
         quantize(x_d, E4, x_bf, P, 2 * P)
         quantize(x_d, E4, x_bf, 2 * P, 4 * P)
+        for k in range(WINDOWS):
+            for c in range(2):
+                nc.vector.memset(windows[k][:, c * 1024:(c + 1) * 1024], 0.0)
 
-        probs = []
-        score_banks = (((0, 1, "b3"), (1, 2, "a0"), (2, 4, "a1")), ((0, 2, "a2"), (2, 4, "a3")))
+        scaled = [sb.tile([P, N], F32, name="scaled%d" % j) for j in range(PACK)]
+        probs = [sb.tile([P, PACK, HALF], F32, name="probs%d" % half) for half in range(2)]
+        for j, tag in enumerate(("a0", "a1", "a2", "a3")):
+            a_ps = bank(tag)
+            product(a_ps[:], x_d, E4, j, w_d, E4, slice(0, N))
+            a_slots = a_ps[:].rearrange("p (s c) -> p c s", s=PACK)
+            for i0, i1 in ((0, N),) if j < 3 else ((0, HALF), (HALF, N)):
+                nc.vector.tensor_tensor(scaled[j][:, i0:i1].rearrange("p (c s) -> p c s", s=PACK),
+                                        a_slots[:, i0 // 4:i1 // 4],
+                                        ts_all[:, i0:i1].rearrange("p (c s) -> p c s", s=PACK), ALU.mult)
         for half in range(2):
-            slots = slice(half * HALF, (half + 1) * HALF)
-            scaled = sb.tile([P, PACK, HALF], F32, name="scaled%d" % half)
-            probs.append(sb.tile([P, PACK, HALF], F32, name="probs%d" % half))
-            for j0, j1, tag in score_banks[half]:
-                a_ps = bank(tag)
-                for j in range(j0, j1):
-                    product(a_ps[:, (j - j0) * HALF:(j - j0 + 1) * HALF], x_d, E4, j, w_d, E4, slots)
-                nc.vector.tensor_tensor(scaled[:, j0:j1, :],
-                                        a_ps[:, 0:(j1 - j0) * HALF].rearrange("p (j i) -> p j i", i=HALF),
-                                        ts_all[:, slots].unsqueeze(1).to_broadcast([P, j1 - j0, HALF]), ALU.mult)
-                for j in range(j0, j1):
-                    nc.scalar.activation(probs[half][:, j, :], scaled[:, j, :], ACT.Exp,
-                                         bias=neg_lse[:, j:j + 1], scale=1.0)
+            for j in range(PACK):
+                nc.scalar.activation(probs[half][:, j, :], scaled[j][:, half * HALF:(half + 1) * HALF], ACT.Exp,
+                                     bias=neg_lse[:, j:j + 1], scale=1.0)
 
         xm_bf = sb.tile([P, D * PACK], BF16, name="xm_bf", align_bytes=64)
         xm_dst = xm_bf[:].rearrange("p (c i t) -> p c t i", i=4, t=PACK)
@@ -216,13 +215,13 @@ def tile_attend_glse_wx_ts_kernel(tc, xT, wT, y, lse, wt, ts, xm, offs, out_0, o
             nc.vector.tensor_copy(window[:].indirect(offsets[:]), dw_sb[:])
             nc.sync.dma_start(out_0[j * P:(j + 1) * P, :], window[:])
 
-        w_i = mx_operand("w_i")
-        for u, bank_tag, tag in ((0, "b2", "w_i_low"), (1, "a3", "xm_raw")):
+        w_i = mx_operand("w_i", "w_plane3")
+        for u, bank_tag, tag in ((0, "b2", "w_i_low"), (1, "b3", "xm_raw")):
             turned = bank(bank_tag)
             if u == 0:
-                turn_words(turned, w_low, lambda s: s, PACK)
+                turn_words(turned, w_low, lambda s: P * s, 1)
             else:
-                turn_words(turned, w_bf, lambda s: 2 * s + 1, 2 * PACK)
+                turn_words(turned, w_bf, lambda s: 2 * P * s + 1, 2)
             w_i_bf = sb.tile([P, HALF * PACK], BF16, name="w_i_bf%d" % u, tag=tag, align_bytes=64)
             nc.scalar.copy(w_i_bf[:].rearrange("q (p e s) -> q p e s", e=2, s=PACK),
                            turned[:].bitcast(BF16).rearrange("q (s p e) -> q p e s", s=PACK, e=2))

@@ -74,10 +74,15 @@ def tile_attend_glse_wx_ts_kernel(tc, xT, wT, y, lse, wt, ts, xm, offs, out_0, o
             x_raw.append(sb.tile([P, PACK, R // 2], F32, name="x_raw%d" % part))
             nc.sync.dma_start(x_raw[part][:],
                               xT[0].rearrange("(p t) r -> p t r", t=PACK)[:, :, part * R // 2:(part + 1) * R // 2])
-        y_sb = sb.tile([P, PACK, N], F32, name="y_sb")
-        nc.sync.dma_start(y_sb[:], y[0].rearrange("(p t) i -> p t i", t=PACK))
-        xm_raw = sb.tile([P, PACK, D], F32, name="xm_raw", tag="xm_raw", align_bytes=64)
-        nc.sync.dma_start(xm_raw[:], xm[0].rearrange("(p t) d -> p t d", t=PACK))
+        y_rows = y[0].rearrange("(p t) i -> p t i", t=PACK)
+        xm_rows = xm[0].rearrange("(p t) d -> p t d", t=PACK)
+        y_sb = [sb.tile([P, PACK, HALF], F32, name="y_sb%d" % half) for half in range(2)]
+        xm_raw_first = sb.tile([P, PACK, P], F32, name="xm_raw_first")
+        xm_raw = sb.tile([P, PACK, D - P], F32, name="xm_raw", tag="xm_raw", align_bytes=64)
+        nc.sync.dma_start(y_sb[1][:], y_rows[:, :, HALF:N])
+        nc.sync.dma_start(y_sb[0][:], y_rows[:, :, 0:HALF])
+        nc.sync.dma_start(xm_raw_first[:], xm_rows[:, :, 0:P])
+        nc.sync.dma_start(xm_raw[:], xm_rows[:, :, P:D])
         nc.vector.memset(ts_table[0:P - 1, :], 0.0)
         ident = sb.tile([P, P], F32, name="ident")
         make_identity(nc, ident[:])
@@ -85,8 +90,6 @@ def tile_attend_glse_wx_ts_kernel(tc, xT, wT, y, lse, wt, ts, xm, offs, out_0, o
         nc.gpsimd.tensor_scalar(neg_lse[:], lse_sb[:], -1.0, 0.0, ALU.mult, ALU.add)
         h_r = (sb.tile([P, HALF + N], U32, name="h_r_codes", align_bytes=64),
                sb.tile([P, HALF + N], U8, name="h_r_scales", align_bytes=64))
-        nc.gpsimd.memset(h_r[0][:, 0:HALF], 0)
-        nc.gpsimd.memset(h_r[1][:, 0:HALF], 0)
         windows = [sb.tile([P, T], F32, name="window%d" % k) for k in range(WINDOWS)]
 
         ts_row = sb.tile([P, N], F32, name="ts_row")
@@ -101,21 +104,29 @@ def tile_attend_glse_wx_ts_kernel(tc, xT, wT, y, lse, wt, ts, xm, offs, out_0, o
             nc.tensor.transpose(ts_all_ps[:, k * P:(k + 1) * P], ts_cols[:, k:k + 1].to_broadcast([P, P]), ident[:])
         ts_all = sb.tile([P, N], F32, name="ts_all")
         nc.scalar.copy(ts_all[:], ts_all_ps[:])
-        wt_ts = sb.tile([P, PACK, N], F32, name="wt_ts")
+        wt_ts = sb.tile([P, PACK, HALF], F32, name="wt_ts")
         for t in range(PACK):
-            nc.scalar.activation(wt_ts[:, t, :], ts_all_ps[:], ACT.Copy, scale=wt_sb[:, t:t + 1])
+            nc.scalar.activation(wt_ts[:, t, :], ts_all_ps[:, 0:HALF], ACT.Copy, scale=wt_sb[:, t:t + 1])
+        wt_all_ps = bank("a0")
+        for t in range(PACK):
+            nc.tensor.transpose(wt_all_ps[:, t * P:(t + 1) * P], wt_sb[:, t:t + 1].to_broadcast([P, P]), ident[:])
+        wt_all = sb.tile([P, R], F32, name="wt_all")
+        nc.scalar.copy(wt_all[:].rearrange("p (m t) -> p m t", t=PACK), wt_all_ps[:].rearrange("p (t m) -> p m t", t=PACK))
 
         w_bf = sb.tile([P, N * PACK], BF16, name="w_bf", align_bytes=64)
-        w_dealt = w_bf[:].rearrange("p (s c t) -> p c s t", s=PACK, t=PACK)
+        w_bf3 = w_bf[:].rearrange("p (i t) -> p i t", t=PACK)
         w_low = sb.tile([P, N * 2], BF16, name="w_low", align_bytes=64)
-        w_low_dealt = w_low[:].rearrange("p (s c e) -> p c s e", s=PACK, e=2)
+        w_low3 = w_low[:].rearrange("p (i e) -> p i e", e=2)
         for t in range(2):
-            nc.vector.tensor_copy(w_low_dealt[:, :, :, t], w_planes[t][:].indirect(offsets[:]))
+            nc.vector.tensor_copy(w_low3[:, :, t], w_planes[t][:].indirect(offsets[:]))
         nc.vector.tensor_copy(w_bf[:].bitcast(F32)[:, 0:2 * N:2], w_low[:].bitcast(F32))
-        for t in range(2, PACK):
-            nc.vector.tensor_copy(w_dealt[:, :, :, t], w_planes[t][:].indirect(offsets[:]))
+        nc.vector.tensor_copy(w_bf3[:, :, 2], w_planes[2][:].indirect(offsets[:]))
+        for half in range(2):
+            nc.vector.tensor_copy(w_bf3[:, half * HALF:(half + 1) * HALF, PACK - 1],
+                                  w_planes[PACK - 1][:].indirect(list_half(half)))
         w_d = mx_operand("w_d")
-        quantize(w_d, E4, w_bf, 0, N)
+        quantize(w_d, E4, w_bf, 0, HALF)
+        quantize(w_d, E4, w_bf, HALF, N)
 
         x_bf = sb.tile([P, R * PACK], BF16, name="x_bf", align_bytes=64)
         x_dst = x_bf[:].rearrange("p (j m t) -> p m t j", j=PACK, t=PACK)
@@ -131,76 +142,101 @@ def tile_attend_glse_wx_ts_kernel(tc, xT, wT, y, lse, wt, ts, xm, offs, out_0, o
         for k in range(WINDOWS):
             for c in range(2):
                 nc.vector.memset(windows[k][:, c * 1024:(c + 1) * 1024], 0.0)
+        nc.vector.memset(h_r[0][:, 0:HALF], 0)
+        nc.vector.memset(h_r[1][:, 0:HALF].bitcast(U32), 0)
 
-        scaled = [sb.tile([P, N], F32, name="scaled%d" % j) for j in range(PACK)]
-        probs = [sb.tile([P, PACK, HALF], F32, name="probs%d" % half) for half in range(2)]
-        for j, tag in enumerate(("a0", "a1", "a2", "a3")):
-            a_ps = bank(tag)
-            product(a_ps[:], x_d, E4, j, w_d, E4, slice(0, N))
-            a_slots = a_ps[:].rearrange("p (s c) -> p c s", s=PACK)
-            for i0, i1 in ((0, N),) if j < 3 else ((0, HALF), (HALF, N)):
-                nc.vector.tensor_tensor(scaled[j][:, i0:i1].rearrange("p (c s) -> p c s", s=PACK),
-                                        a_slots[:, i0 // 4:i1 // 4],
-                                        ts_all[:, i0:i1].rearrange("p (c s) -> p c s", s=PACK), ALU.mult)
+        neg_y = sb.tile([P, PACK, HALF], F32, name="neg_y")
+        nc.scalar.activation(neg_y[:], y_sb[1][:], ACT.Copy, scale=-1.0)
+        probs = []
+        score_banks = (((0, 1, "b3"), (1, 2, "a0"), (2, 4, "a1")), ((0, 2, "a2"), (2, 4, "a3")))
         for half in range(2):
-            for j in range(PACK):
-                nc.scalar.activation(probs[half][:, j, :], scaled[j][:, half * HALF:(half + 1) * HALF], ACT.Exp,
-                                     bias=neg_lse[:, j:j + 1], scale=1.0)
+            slots = slice(half * HALF, (half + 1) * HALF)
+            scaled = sb.tile([P, PACK, HALF], F32, name="scaled%d" % half, tag="scaled%d" % half, align_bytes=64)
+            probs.append(sb.tile([P, PACK, HALF], F32, name="probs%d" % half))
+            for j0, j1, tag in score_banks[half]:
+                a_ps = bank(tag)
+                for j in range(j0, j1):
+                    product(a_ps[:, (j - j0) * HALF:(j - j0 + 1) * HALF], x_d, E4, j, w_d, E4, slots)
+                nc.vector.tensor_tensor(scaled[:, j0:j1, :],
+                                        a_ps[:, 0:(j1 - j0) * HALF].rearrange("p (j i) -> p j i", i=HALF),
+                                        ts_all[:, slots].unsqueeze(1).to_broadcast([P, j1 - j0, HALF]), ALU.mult)
+                for j in range(j0, j1):
+                    nc.scalar.activation(probs[half][:, j, :], scaled[:, j, :], ACT.Exp,
+                                         bias=neg_lse[:, j:j + 1], scale=1.0)
 
-        xm_bf = sb.tile([P, D * PACK], BF16, name="xm_bf", align_bytes=64)
+        diff_turned = [bank("b0"), bank("b1")]
+        for term, src in enumerate((neg_y, probs[1])):
+            for j in range(PACK):
+                for b in range(2):
+                    nc.tensor.matmul(diff_turned[b][:, j * P:(j + 1) * P], src[:, j, b * P:(b + 1) * P], ident[:],
+                                     start=(term == 0 and j == 0), stop=(term == 1 and j == PACK - 1),
+                                     is_transpose=True)
+
+        xm_bf_first = sb.tile([P, P * PACK], BF16, name="xm_bf_first", tag="scaled1", align_bytes=64)
+        nc.scalar.copy(xm_bf_first[:].rearrange("p (c i t) -> p c t i", i=4, t=PACK),
+                       xm_raw_first[:].rearrange("p t (c i) -> p c t i", i=4))
+        xm_bf = sb.tile([P, (D - P) * PACK], BF16, name="xm_bf", tag="scaled0", align_bytes=64)
         xm_dst = xm_bf[:].rearrange("p (c i t) -> p c t i", i=4, t=PACK)
         xm_src = xm_raw[:].rearrange("p t (c i) -> p c t i", i=4)
-        for j in range(4):
+        for j in range(3):
             nc.scalar.copy(xm_dst[:, 32 * j:32 * (j + 1)], xm_src[:, 32 * j:32 * (j + 1)])
         xm_r = mx_operand("xm_r")
 
+        def quantize_xm(c0, c1, src):
+            nc.vector.quantize_mx(out=xm_r[0][:, c0:c1].bitcast(E4), scales=xm_r[1][:, c0:c1], in_=src)
+
         h_bf = sb.tile([P, N * PACK], BF16, name="h_bf", tag="h_bf", align_bytes=64)
         h_dst = h_bf[:].rearrange("p (s c t) -> p c t s", s=PACK, t=PACK)
-        wt_ts_src = wt_ts[:].rearrange("p t (c i) -> p c t i", i=4)
-        dw_first_ps = []
 
-        def copy_first(half):
-            nc.scalar.copy(dw_first[:, half * HALF:(half + 1) * HALF].rearrange("p (c s) -> p c s", s=PACK),
-                           dw_first_ps[half][:, HALF:N].rearrange("p (s c) -> p c s", s=PACK))
-
-        for half in range(2):
-            slots = slice(half * HALF, (half + 1) * HALF)
-            if half == 0:
-                diff = sb.tile([P, PACK, HALF], F32, name="diff_first", tag="diff")
-                for j in range(2):
-                    nc.gpsimd.tensor_tensor(diff[:, j, :], probs[0][:, j, :], y_sb[:, j, slots], ALU.subtract)
-                nc.vector.tensor_tensor(diff[:, 2:4, :], probs[0][:, 2:4, :], y_sb[:, 2:4, slots], ALU.subtract)
-                parts = [(0, HALF, diff[:])]
-            else:
-                parts = []
-                diff = sb.tile([P, 2, PACK, P], F32, name="diff_second", tag="diff")
-                for part in range(2):
-                    i0 = HALF + part * P
-                    nc.vector.tensor_tensor(diff[:, part], probs[1][:, :, part * P:(part + 1) * P],
-                                            y_sb[:, :, i0:i0 + P], ALU.subtract)
-                    parts.append((i0, i0 + P, diff[:, part]))
-            for i0, i1, diff_part in parts:
-                quads = slice(i0 // 4, i1 // 4)
-                nc.vector.tensor_tensor(h_dst[:, quads], diff_part.rearrange("p t (c i) -> p c t i", i=4),
-                                        wt_ts_src[:, quads], ALU.mult)
-            if half == 1:
-                dw_first = sb.tile([P, N], F32, name="dw_first", tag="diff")
-                copy_first(0)
-            quantize(xm_r, E4, xm_bf, half * P, (half + 1) * P)
+        def quantize_h(half):
             for s in range(PACK):
                 placed = slice((half + 1) * HALF + s * 64, (half + 1) * HALF + (s + 1) * 64)
                 first = s * N + half * HALF
                 nc.vector.quantize_mx(out=h_r[0][:, placed].bitcast(E5), scales=h_r[1][:, placed],
                                       in_=h_bf[:, first:first + HALF])
-            dw_ps = bank("b%d" % half)
-            product(dw_ps[:], xm_r, E4, 0, h_r, E5, slice(half * HALF, half * HALF + N))
-            dw_first_ps.append(dw_ps)
-        copy_first(1)
 
-        quantize(xm_r, E4, xm_bf, 2 * P, 4 * P)
-        nc.vector.tensor_copy(windows[0][:].indirect(list_half(0)), dw_first[:, 0:HALF])
-        nc.vector.tensor_copy(windows[0][:].indirect(list_half(1)), dw_first[:, HALF:N])
-        nc.sync.dma_start(out_0[0:P, :], windows[0][:])
+        def dw_half(j, half, bank_tag, tag):
+            dw_ps = bank(bank_tag)
+            product(dw_ps[:], xm_r, E4, j, h_r, E5, slice(half * HALF, half * HALF + N))
+            dw_sb = sb.tile([P, HALF], F32, name="dw_sb%d_%d" % (j, half), tag=tag, align_bytes=64)
+            nc.scalar.copy(dw_sb[:].rearrange("p (c s) -> p c s", s=PACK),
+                           dw_ps[:, HALF:N].rearrange("p (s c) -> p c s", s=PACK))
+            return dw_sb
+
+        def place_half(j, half, dw_sb):
+            nc.vector.tensor_copy(windows[j][:].indirect(list_half(half)), dw_sb[:])
+            if half == 1:
+                nc.sync.dma_start(out_0[j * P:(j + 1) * P, :], windows[j][:])
+
+        diff = sb.tile([P, PACK, HALF], F32, name="diff")
+        for pair in range(2):
+            rows = slice(2 * pair, 2 * pair + 2)
+            nc.vector.tensor_tensor(diff[:, rows, :], probs[0][:, rows, :], y_sb[0][:, rows, :], ALU.subtract)
+        nc.vector.tensor_tensor(h_dst[:, 0:64], diff[:].rearrange("p t (c i) -> p c t i", i=4),
+                                wt_ts[:].rearrange("p t (c i) -> p c t i", i=4), ALU.mult)
+        quantize_xm(0, P, xm_bf_first[:])
+        quantize_h(0)
+        h_turned = sb.tile([P, 2, R], BF16, name="h_turned", tag="h_turned", align_bytes=64)
+        for b in range(2):
+            nc.vector.scalar_tensor_tensor(h_turned[:, b, :].rearrange("q (m t) -> q m t", t=PACK),
+                                           diff_turned[b][:].rearrange("q (t m) -> q m t", t=PACK),
+                                           ts_cols[:, 2 + b:3 + b],
+                                           wt_all[:].rearrange("q (m t) -> q m t", t=PACK), ALU.mult, ALU.mult)
+        dw_00 = dw_half(0, 0, "b3", "dw_00")
+        back = bank("a2")
+        h_turned_words = h_turned[:].rearrange("q b r -> q (b r)").bitcast(F32)
+        for b in range(2):
+            for u in range(2):
+                nc.tensor.transpose(back[:, (2 * b + u) * P:(2 * b + u + 1) * P],
+                                    h_turned_words[:, b * HALF + u:(b + 1) * HALF:2], ident[:])
+        nc.scalar.copy(h_bf[:].bitcast(F32).rearrange("p (s g b c u) -> p g s b c u", s=PACK, g=2, b=2, u=2)[:, 1],
+                       back[:].rearrange("p (b u c s) -> p s b c u", b=2, u=2, s=PACK))
+        quantize_xm(P, 2 * P, xm_bf[:, 0:PACK * P])
+        place_half(0, 0, dw_00)
+        quantize_h(1)
+        place_half(1, 0, dw_half(1, 0, "a0", "h_turned"))
+        dw_second = [dw_half(j, 1, tag, "dw_%d1" % j) for j, tag in ((0, "b0"), (1, "b1"))]
+        quantize_xm(2 * P, 4 * P, xm_bf[:, PACK * P:])
 
         def dw_block(j, bank_tag, tag):
             dw_ps = bank(bank_tag)
@@ -216,31 +252,32 @@ def tile_attend_glse_wx_ts_kernel(tc, xT, wT, y, lse, wt, ts, xm, offs, out_0, o
             nc.sync.dma_start(out_0[j * P:(j + 1) * P, :], window[:])
 
         w_i = mx_operand("w_i", "w_plane3")
-        for u, bank_tag, tag in ((0, "b2", "w_i_low"), (1, "b3", "xm_raw")):
+        for u, bank_tag, tag in ((0, "b2", "w_i_low"), (1, "b2", "xm_raw")):
             turned = bank(bank_tag)
             if u == 0:
-                turn_words(turned, w_low, lambda s: P * s, 1)
+                turn_words(turned, w_low, lambda s: s, PACK)
             else:
-                turn_words(turned, w_bf, lambda s: 2 * P * s + 1, 2)
+                turn_words(turned, w_bf, lambda s: 2 * s + 1, 2 * PACK)
             w_i_bf = sb.tile([P, HALF * PACK], BF16, name="w_i_bf%d" % u, tag=tag, align_bytes=64)
             nc.scalar.copy(w_i_bf[:].rearrange("q (p e s) -> q p e s", e=2, s=PACK),
                            turned[:].bitcast(BF16).rearrange("q (s p e) -> q p e s", s=PACK, e=2))
             placed = slice(u * HALF, (u + 1) * HALF)
             nc.vector.quantize_mx(out=w_i[0][:, placed].bitcast(E4), scales=w_i[1][:, placed], in_=w_i_bf[:])
 
+        for j in range(2):
+            place_half(j, 1, dw_second[j])
         h_i_bf = sb.tile([P, R * PACK], BF16, name="h_i_bf", align_bytes=64)
         h_i_dst = h_i_bf[:].rearrange("q (u e p s) -> q u e p s", u=2, e=2, s=PACK)
-        for u, tag in ((0, "a0"), (1, "a1")):
+        for u, tag in ((0, "a1"), (1, "a3")):
             turned = bank(tag)
             turn_words(turned, h_bf, lambda s: 2 * P * s + u, 2)
             nc.scalar.copy(h_i_dst[:, u], turned[:].bitcast(BF16).rearrange("q (s p e) -> q e p s", s=PACK, e=2))
         h_i = mx_operand("h_i")
         quantize(h_i, E5, h_i_bf, 0, 512)
-        place(1, dw_block(1, "b2", "h_bf"))
-        dw_2 = dw_block(2, "b2", "dw_2")
+        dw_2 = dw_block(2, "b2", "h_bf")
         gx_sb = sb.tile([P, PACK, D], F32, name="gx_sb")
         gx_rows = out_1[0].rearrange("(m j) d -> m j d", j=PACK)
-        for j, tag in enumerate(("b0", "b1", "a2", "b3")):
+        for j, tag in enumerate(("b3", "a0", "a2", "b0")):
             gx_ps = bank(tag)
             product(gx_ps[:], h_i, E5, j, w_i, E4, slice(0, D))
             nc.scalar.copy(gx_sb[:, j, :].rearrange("m (p u e) -> m p u e", u=2, e=2),

@@ -59,14 +59,14 @@ def tile_attend_glse_wx_ts_kernel(tc, xT, wT, y, lse, wt, ts, xm, offs, out_0, o
         w_planes = [sb.tile([P, T], F32, name="w_plane%d" % t, tag="w_plane%d" % t, align_bytes=64) for t in range(PACK)]
         wT_planes = wT.rearrange("(p t) c -> t p c", t=PACK)
         offsets = sb.tile([P, N // 16], U16, name="offsets")
-        nc.sync.dma_start(offsets[:], offs)
-        nc.sync.dma_start(w_planes[0][:], wT_planes[0])
         ts_table = sb.tile([P, T], F32, name="ts_table")
         nc.scalar.dma_start(ts_table[P - 1:P, :], ts[0:1, :])
         wt_sb = sb.tile([P, PACK], F32, name="wt_sb")
-        nc.sync.dma_start(wt_sb[:], wt[0].rearrange("(p t) o -> p (t o)", t=PACK))
+        nc.scalar.dma_start(wt_sb[:], wt[0].rearrange("(p t) o -> p (t o)", t=PACK))
         lse_sb = sb.tile([P, PACK], F32, name="lse_sb")
-        nc.sync.dma_start(lse_sb[:], lse[0].rearrange("(p t) o -> p (t o)", t=PACK))
+        nc.scalar.dma_start(lse_sb[:], lse[0].rearrange("(p t) o -> p (t o)", t=PACK))
+        nc.sync.dma_start(offsets[:], offs)
+        nc.sync.dma_start(w_planes[0][:], wT_planes[0])
         for t in range(1, PACK):
             nc.sync.dma_start(w_planes[t][:], wT_planes[t])
         x_raw = []
@@ -90,7 +90,10 @@ def tile_attend_glse_wx_ts_kernel(tc, xT, wT, y, lse, wt, ts, xm, offs, out_0, o
         nc.gpsimd.tensor_scalar(neg_lse[:], lse_sb[:], -1.0, 0.0, ALU.mult, ALU.add)
         h_r = (sb.tile([P, HALF + N], U32, name="h_r_codes", align_bytes=64),
                sb.tile([P, HALF + N], U8, name="h_r_scales", align_bytes=64))
-        windows = [sb.tile([P, T], F32, name="window%d" % k) for k in range(WINDOWS)]
+        windows = [sb.tile([P, T], F32, name="window0")]
+        nc.vector.memset(windows[0][:], 0.0)
+        nc.vector.memset(h_r[0][:, 0:HALF], 0)
+        nc.vector.memset(h_r[1][:, 0:HALF].bitcast(U32), 0)
 
         ts_row = sb.tile([P, N], F32, name="ts_row")
         nc.vector.tensor_copy(ts_row[:], ts_table[:].indirect(offsets[:]))
@@ -128,7 +131,7 @@ def tile_attend_glse_wx_ts_kernel(tc, xT, wT, y, lse, wt, ts, xm, offs, out_0, o
         quantize(w_d, E4, w_bf, 0, HALF)
         quantize(w_d, E4, w_bf, HALF, N)
 
-        x_bf = sb.tile([P, R * PACK], BF16, name="x_bf", align_bytes=64)
+        x_bf = sb.tile([P, R * PACK], BF16, name="x_bf", tag="x_bf", align_bytes=64)
         x_dst = x_bf[:].rearrange("p (j m t) -> p m t j", j=PACK, t=PACK)
         x_src = [x_raw[part][:].rearrange("p t (m j) -> p m t j", j=PACK) for part in range(2)]
         nc.scalar.copy(x_dst[:, 0:64, :, 0:2], x_src[0][:, :, :, 0:2])
@@ -139,11 +142,8 @@ def tile_attend_glse_wx_ts_kernel(tc, xT, wT, y, lse, wt, ts, xm, offs, out_0, o
         quantize(x_d, E4, x_bf, 0, P)
         quantize(x_d, E4, x_bf, P, 2 * P)
         quantize(x_d, E4, x_bf, 2 * P, 4 * P)
-        for k in range(WINDOWS):
-            for c in range(2):
-                nc.vector.memset(windows[k][:, c * 1024:(c + 1) * 1024], 0.0)
-        nc.vector.memset(h_r[0][:, 0:HALF], 0)
-        nc.vector.memset(h_r[1][:, 0:HALF].bitcast(U32), 0)
+        windows.append(sb.tile([P, T], F32, name="window1", tag="x_bf", align_bytes=64))
+        nc.gpsimd.memset(windows[1][:], 0.0)
 
         neg_y = sb.tile([P, PACK, HALF], F32, name="neg_y")
         nc.scalar.activation(neg_y[:], y_sb[1][:], ACT.Copy, scale=-1.0)
@@ -163,6 +163,9 @@ def tile_attend_glse_wx_ts_kernel(tc, xT, wT, y, lse, wt, ts, xm, offs, out_0, o
                 for j in range(j0, j1):
                     nc.scalar.activation(probs[half][:, j, :], scaled[:, j, :], ACT.Exp,
                                          bias=neg_lse[:, j:j + 1], scale=1.0)
+
+        windows.append(sb.tile([P, T], F32, name="window2", tag="x_d_codes", align_bytes=64))
+        nc.gpsimd.memset(windows[2][:], 0.0)
 
         diff_turned = [bank("b0"), bank("b1")]
         for term, src in enumerate((neg_y, probs[1])):

@@ -69,20 +69,6 @@ def tile_attend_glse_wx_ts_kernel(tc, xT, wT, y, lse, wt, ts, xm, offs, out_0, o
         nc.sync.dma_start(w_planes[0][:], wT_planes[0])
         for t in range(1, PACK):
             nc.sync.dma_start(w_planes[t][:], wT_planes[t])
-        x_raw = []
-        for part in range(2):
-            x_raw.append(sb.tile([P, PACK, R // 2], F32, name="x_raw%d" % part))
-            nc.sync.dma_start(x_raw[part][:],
-                              xT[0].rearrange("(p t) r -> p t r", t=PACK)[:, :, part * R // 2:(part + 1) * R // 2])
-        y_rows = y[0].rearrange("(p t) i -> p t i", t=PACK)
-        xm_rows = xm[0].rearrange("(p t) d -> p t d", t=PACK)
-        y_sb = [sb.tile([P, PACK, HALF], F32, name="y_sb%d" % half) for half in range(2)]
-        xm_raw_first = sb.tile([P, PACK, P], F32, name="xm_raw_first")
-        xm_raw = sb.tile([P, PACK, D - P], F32, name="xm_raw", tag="xm_raw", align_bytes=64)
-        nc.sync.dma_start(y_sb[1][:], y_rows[:, :, HALF:N])
-        nc.sync.dma_start(y_sb[0][:], y_rows[:, :, 0:HALF])
-        nc.sync.dma_start(xm_raw_first[:], xm_rows[:, :, 0:P])
-        nc.sync.dma_start(xm_raw[:], xm_rows[:, :, P:D])
         nc.vector.memset(ts_table[0:P - 1, :], 0.0)
         ident = sb.tile([P, P], F32, name="ident")
         make_identity(nc, ident[:])
@@ -131,6 +117,11 @@ def tile_attend_glse_wx_ts_kernel(tc, xT, wT, y, lse, wt, ts, xm, offs, out_0, o
         quantize(w_d, E4, w_bf, 0, HALF)
         quantize(w_d, E4, w_bf, HALF, N)
 
+        x_raw = []
+        for part in range(2):
+            x_raw.append(sb.tile([P, PACK, R // 2], F32, name="x_raw%d" % part, tag="w_plane%d" % part, align_bytes=64))
+            nc.sync.dma_start(x_raw[part][:],
+                              xT[0].rearrange("(p t) r -> p t r", t=PACK)[:, :, part * R // 2:(part + 1) * R // 2])
         x_bf = sb.tile([P, R * PACK], BF16, name="x_bf", tag="x_bf", align_bytes=64)
         x_dst = x_bf[:].rearrange("p (j m t) -> p m t j", j=PACK, t=PACK)
         x_src = [x_raw[part][:].rearrange("p t (m j) -> p m t j", j=PACK) for part in range(2)]
@@ -145,8 +136,20 @@ def tile_attend_glse_wx_ts_kernel(tc, xT, wT, y, lse, wt, ts, xm, offs, out_0, o
         windows.append(sb.tile([P, T], F32, name="window1", tag="x_bf", align_bytes=64))
         nc.gpsimd.memset(windows[1][:], 0.0)
 
+        y_rows = y[0].rearrange("(p t) i -> p t i", t=PACK)
+        xm_rows = xm[0].rearrange("(p t) d -> p t d", t=PACK)
+        y_both = sb.tile([P, 2 * PACK * HALF], F32, name="y_both", tag="w_plane2", align_bytes=64)
+        y_sb = [y_both[:, half * PACK * HALF:(half + 1) * PACK * HALF].rearrange("p (t i) -> p t i", t=PACK)
+                for half in range(2)]
+        xm_raw_first = sb.tile([P, PACK, P], F32, name="xm_raw_first", tag="w_plane0", align_bytes=64)
+        xm_raw = sb.tile([P, PACK, D - P], F32, name="xm_raw", tag="w_plane1", align_bytes=64)
+        nc.sync.dma_start(y_sb[1], y_rows[:, :, HALF:N])
+        nc.sync.dma_start(y_sb[0], y_rows[:, :, 0:HALF])
+        nc.sync.dma_start(xm_raw_first[:], xm_rows[:, :, 0:P])
+        nc.sync.dma_start(xm_raw[:], xm_rows[:, :, P:D])
+
         neg_y = sb.tile([P, PACK, HALF], F32, name="neg_y")
-        nc.scalar.activation(neg_y[:], y_sb[1][:], ACT.Copy, scale=-1.0)
+        nc.scalar.activation(neg_y[:], y_sb[1], ACT.Copy, scale=-1.0)
         probs = []
         score_banks = (((0, 1, "b3"), (1, 2, "a0"), (2, 4, "a1")), ((0, 2, "a2"), (2, 4, "a3")))
         for half in range(2):
@@ -255,7 +258,7 @@ def tile_attend_glse_wx_ts_kernel(tc, xT, wT, y, lse, wt, ts, xm, offs, out_0, o
             nc.sync.dma_start(out_0[j * P:(j + 1) * P, :], window[:])
 
         w_i = mx_operand("w_i", "w_plane3")
-        for u, bank_tag, tag in ((0, "b2", "w_i_low"), (1, "b2", "xm_raw")):
+        for u, bank_tag, tag in ((0, "b2", "w_i_low"), (1, "b2", "w_plane1")):
             turned = bank(bank_tag)
             if u == 0:
                 turn_words(turned, w_low, lambda s: s, PACK)

@@ -26,6 +26,7 @@ def tile_attend_glse_wx_ts_kernel(tc, xT, wT, y, lse, wt, ts, xm, offs, out_0, o
     nc = tc.nc
     with ExitStack() as ctx:
         sb = ctx.enter_context(tc.tile_pool(name="sb", bufs=1))
+        shared = ctx.enter_context(tc.tile_pool(name="shared", bufs=1))
         ps = ctx.enter_context(tc.psum_pool(name="ps", bufs=1))
 
         def bank(tag):
@@ -113,16 +114,40 @@ def tile_attend_glse_wx_ts_kernel(tc, xT, wT, y, lse, wt, ts, xm, offs, out_0, o
         for half in range(2):
             nc.vector.tensor_copy(w_bf3[:, half * HALF:(half + 1) * HALF, PACK - 1],
                                   w_planes[PACK - 1][:].indirect(list_half(half)))
-        w_d = mx_operand("w_d")
-        quantize(w_d, E4, w_bf, 0, HALF)
-        quantize(w_d, E4, w_bf, HALF, N)
+        w_d = []
+
+        def quantize_w_d(half, tag):
+            w_d.append((sb.tile([P, HALF], U32, name="w_d_codes%d" % half, tag=tag, align_bytes=64),
+                        sb.tile([P, HALF], U8, name="w_d_scales%d" % half, align_bytes=64)))
+            nc.vector.quantize_mx(out=w_d[half][0][:].bitcast(E4), scales=w_d[half][1][:],
+                                  in_=w_bf[:, half * PACK * HALF:(half + 1) * PACK * HALF])
+
+        quantize_w_d(0, "w_d_codes0")
+        w_i = (shared.tile([P, D], U32, name="w_i_codes", offset=4096, align_bytes=64),
+               sb.tile([P, D], U8, name="w_i_scales", align_bytes=64))
+
+        def w_along_slots(u, w_i_bf):
+            turned = bank("b2")
+            if u == 0:
+                turn_words(turned, w_low, lambda s: s, PACK)
+            else:
+                turn_words(turned, w_bf, lambda s: 2 * s + 1, 2 * PACK)
+            nc.scalar.copy(w_i_bf[:].rearrange("q (p e s) -> q p e s", e=2, s=PACK),
+                           turned[:].bitcast(BF16).rearrange("q (s p e) -> q p e s", s=PACK, e=2))
+            return w_i_bf
+
+        def quantize_w_i(u, w_i_bf):
+            placed = slice(u * HALF, (u + 1) * HALF)
+            nc.vector.quantize_mx(out=w_i[0][:, placed].bitcast(E4), scales=w_i[1][:, placed], in_=w_i_bf[:])
+
+        w_i_low = w_along_slots(0, sb.tile([P, HALF * PACK], BF16, name="w_i_low", align_bytes=64))
 
         x_raw = []
         for part in range(2):
             x_raw.append(sb.tile([P, PACK, R // 2], F32, name="x_raw%d" % part, tag="w_plane%d" % part, align_bytes=64))
             nc.sync.dma_start(x_raw[part][:],
                               xT[0].rearrange("(p t) r -> p t r", t=PACK)[:, :, part * R // 2:(part + 1) * R // 2])
-        x_bf = sb.tile([P, R * PACK], BF16, name="x_bf", tag="x_bf", align_bytes=64)
+        x_bf = shared.tile([P, R * PACK], BF16, name="x_bf", offset=3072, align_bytes=64)
         x_dst = x_bf[:].rearrange("p (j m t) -> p m t j", j=PACK, t=PACK)
         x_src = [x_raw[part][:].rearrange("p t (m j) -> p m t j", j=PACK) for part in range(2)]
         nc.scalar.copy(x_dst[:, 0:64, :, 0:2], x_src[0][:, :, :, 0:2])
@@ -133,7 +158,9 @@ def tile_attend_glse_wx_ts_kernel(tc, xT, wT, y, lse, wt, ts, xm, offs, out_0, o
         quantize(x_d, E4, x_bf, 0, P)
         quantize(x_d, E4, x_bf, P, 2 * P)
         quantize(x_d, E4, x_bf, 2 * P, 4 * P)
-        windows.append(sb.tile([P, T], F32, name="window1", tag="x_bf", align_bytes=64))
+        quantize_w_d(1, "w_plane1")
+        quantize_w_i(0, w_i_low)
+        windows.append(shared.tile([P, T], F32, name="window1", offset=6144, align_bytes=64))
         nc.gpsimd.memset(windows[1][:], 0.0)
 
         y_rows = y[0].rearrange("(p t) i -> p t i", t=PACK)
@@ -141,12 +168,10 @@ def tile_attend_glse_wx_ts_kernel(tc, xT, wT, y, lse, wt, ts, xm, offs, out_0, o
         y_both = sb.tile([P, 2 * PACK * HALF], F32, name="y_both", tag="w_plane2", align_bytes=64)
         y_sb = [y_both[:, half * PACK * HALF:(half + 1) * PACK * HALF].rearrange("p (t i) -> p t i", t=PACK)
                 for half in range(2)]
-        xm_raw_first = sb.tile([P, PACK, P], F32, name="xm_raw_first", tag="w_plane0", align_bytes=64)
-        xm_raw = sb.tile([P, PACK, D - P], F32, name="xm_raw", tag="w_plane1", align_bytes=64)
+        xm_raw = sb.tile([P, PACK, D], F32, name="xm_raw", tag="w_plane0", align_bytes=64)
         nc.sync.dma_start(y_sb[1], y_rows[:, :, HALF:N])
         nc.sync.dma_start(y_sb[0], y_rows[:, :, 0:HALF])
-        nc.sync.dma_start(xm_raw_first[:], xm_rows[:, :, 0:P])
-        nc.sync.dma_start(xm_raw[:], xm_rows[:, :, P:D])
+        nc.sync.dma_start(xm_raw[:], xm_rows)
 
         neg_y = sb.tile([P, PACK, HALF], F32, name="neg_y")
         nc.scalar.activation(neg_y[:], y_sb[1], ACT.Copy, scale=-1.0)
@@ -154,12 +179,15 @@ def tile_attend_glse_wx_ts_kernel(tc, xT, wT, y, lse, wt, ts, xm, offs, out_0, o
         score_banks = (((0, 1, "b3"), (1, 2, "a0"), (2, 4, "a1")), ((0, 2, "a2"), (2, 4, "a3")))
         for half in range(2):
             slots = slice(half * HALF, (half + 1) * HALF)
-            scaled = sb.tile([P, PACK, HALF], F32, name="scaled%d" % half, tag="scaled%d" % half, align_bytes=64)
+            if half == 0:
+                scaled = shared.tile([P, PACK, HALF], F32, name="scaled0", offset=0, align_bytes=64)
+            else:
+                scaled = shared.tile([P, PACK, HALF], F32, name="scaled1", offset=14336, align_bytes=64)
             probs.append(sb.tile([P, PACK, HALF], F32, name="probs%d" % half))
             for j0, j1, tag in score_banks[half]:
                 a_ps = bank(tag)
                 for j in range(j0, j1):
-                    product(a_ps[:, (j - j0) * HALF:(j - j0 + 1) * HALF], x_d, E4, j, w_d, E4, slots)
+                    product(a_ps[:, (j - j0) * HALF:(j - j0 + 1) * HALF], x_d, E4, j, w_d[half], E4, slice(0, HALF))
                 nc.vector.tensor_tensor(scaled[:, j0:j1, :],
                                         a_ps[:, 0:(j1 - j0) * HALF].rearrange("p (j i) -> p j i", i=HALF),
                                         ts_all[:, slots].unsqueeze(1).to_broadcast([P, j1 - j0, HALF]), ALU.mult)
@@ -178,35 +206,40 @@ def tile_attend_glse_wx_ts_kernel(tc, xT, wT, y, lse, wt, ts, xm, offs, out_0, o
                                      start=(term == 0 and j == 0), stop=(term == 1 and j == PACK - 1),
                                      is_transpose=True)
 
-        xm_bf_first = sb.tile([P, P * PACK], BF16, name="xm_bf_first", tag="scaled1", align_bytes=64)
-        nc.scalar.copy(xm_bf_first[:].rearrange("p (c i t) -> p c t i", i=4, t=PACK),
-                       xm_raw_first[:].rearrange("p t (c i) -> p c t i", i=4))
-        xm_bf = sb.tile([P, (D - P) * PACK], BF16, name="xm_bf", tag="scaled0", align_bytes=64)
-        xm_dst = xm_bf[:].rearrange("p (c i t) -> p c t i", i=4, t=PACK)
-        xm_src = xm_raw[:].rearrange("p t (c i) -> p c t i", i=4)
-        for j in range(3):
-            nc.scalar.copy(xm_dst[:, 32 * j:32 * (j + 1)], xm_src[:, 32 * j:32 * (j + 1)])
-        xm_r = mx_operand("xm_r")
+        xm_bf = []
 
-        def quantize_xm(c0, c1, src):
-            nc.vector.quantize_mx(out=xm_r[0][:, c0:c1].bitcast(E4), scales=xm_r[1][:, c0:c1], in_=src)
+        def round_xm(pair, tile):
+            xm_bf.append(tile)
+            dst = tile[:].rearrange("p (c i t) -> p c t i", i=4, t=PACK)
+            for k in range(2):
+                j = 2 * pair + k
+                nc.scalar.copy(dst[:, 32 * k:32 * (k + 1)],
+                               xm_raw[:, :, j * P:(j + 1) * P].rearrange("p t (c i) -> p c t i", i=4))
+
+        round_xm(0, shared.tile([P, 2 * P * PACK], BF16, name="xm_bf0", offset=14336, align_bytes=64))
+        w_i_high = w_along_slots(1, shared.tile([P, HALF * PACK], BF16, name="w_i_high", offset=16384, align_bytes=64))
+        xm_r = [(sb.tile([P, 2 * P], U32, name="xm_r_codes%d" % pair, tag="xm_r_codes%d" % pair, align_bytes=64),
+                 sb.tile([P, 2 * P], U8, name="xm_r_scales%d" % pair, align_bytes=64)) for pair in range(2)]
+
+        def quantize_xm(j0, j1):
+            codes, scales = xm_r[j0 // 2]
+            placed = slice((j0 % 2) * P, (j0 % 2 + j1 - j0) * P)
+            nc.vector.quantize_mx(out=codes[:, placed].bitcast(E4), scales=scales[:, placed],
+                                  in_=xm_bf[j0 // 2][:, PACK * placed.start:PACK * placed.stop])
 
         h_bf = sb.tile([P, N * PACK], BF16, name="h_bf", tag="h_bf", align_bytes=64)
-        h_dst = h_bf[:].rearrange("p (s c t) -> p c t s", s=PACK, t=PACK)
+        h_dst = h_bf[:].rearrange("p (c i t) -> p c t i", i=4, t=PACK)
 
-        def quantize_h(half):
-            for s in range(PACK):
-                placed = slice((half + 1) * HALF + s * 64, (half + 1) * HALF + (s + 1) * 64)
-                first = s * N + half * HALF
-                nc.vector.quantize_mx(out=h_r[0][:, placed].bitcast(E5), scales=h_r[1][:, placed],
-                                      in_=h_bf[:, first:first + HALF])
+        def quantize_h(c0, c1):
+            placed = slice(HALF + c0, HALF + c1)
+            nc.vector.quantize_mx(out=h_r[0][:, placed].bitcast(E5), scales=h_r[1][:, placed],
+                                  in_=h_bf[:, PACK * c0:PACK * c1])
 
         def dw_half(j, half, bank_tag, tag):
             dw_ps = bank(bank_tag)
-            product(dw_ps[:], xm_r, E4, j, h_r, E5, slice(half * HALF, half * HALF + N))
+            product(dw_ps[:], xm_r[j // 2], E4, j % 2, h_r, E5, slice(half * HALF, half * HALF + N))
             dw_sb = sb.tile([P, HALF], F32, name="dw_sb%d_%d" % (j, half), tag=tag, align_bytes=64)
-            nc.scalar.copy(dw_sb[:].rearrange("p (c s) -> p c s", s=PACK),
-                           dw_ps[:, HALF:N].rearrange("p (s c) -> p c s", s=PACK))
+            nc.scalar.copy(dw_sb[:], dw_ps[:, HALF:N])
             return dw_sb
 
         def place_half(j, half, dw_sb):
@@ -214,42 +247,43 @@ def tile_attend_glse_wx_ts_kernel(tc, xT, wT, y, lse, wt, ts, xm, offs, out_0, o
             if half == 1:
                 nc.sync.dma_start(out_0[j * P:(j + 1) * P, :], windows[j][:])
 
-        diff = sb.tile([P, PACK, HALF], F32, name="diff")
-        for pair in range(2):
-            rows = slice(2 * pair, 2 * pair + 2)
-            nc.vector.tensor_tensor(diff[:, rows, :], probs[0][:, rows, :], y_sb[0][:, rows, :], ALU.subtract)
-        nc.vector.tensor_tensor(h_dst[:, 0:64], diff[:].rearrange("p t (c i) -> p c t i", i=4),
-                                wt_ts[:].rearrange("p t (c i) -> p c t i", i=4), ALU.mult)
-        quantize_xm(0, P, xm_bf_first[:])
-        quantize_h(0)
-        h_turned = sb.tile([P, 2, R], BF16, name="h_turned", tag="h_turned", align_bytes=64)
+        diff = [sb.tile([P, PACK, P], F32, name="diff%d" % b) for b in range(2)]
         for b in range(2):
-            nc.vector.scalar_tensor_tensor(h_turned[:, b, :].rearrange("q (m t) -> q m t", t=PACK),
+            cols = slice(b * P, (b + 1) * P)
+            nc.vector.tensor_tensor(diff[b][:], probs[0][:, :, cols], y_sb[0][:, :, cols], ALU.subtract)
+        for b in range(2):
+            nc.vector.tensor_tensor(h_dst[:, 32 * b:32 * (b + 1)], diff[b][:].rearrange("p t (c i) -> p c t i", i=4),
+                                    wt_ts[:, :, b * P:(b + 1) * P].rearrange("p t (c i) -> p c t i", i=4), ALU.mult)
+        quantize_h(0, P)
+        quantize_xm(0, 1)
+        quantize_h(P, HALF)
+        h_turned = [sb.tile([P, R], BF16, name="h_turned%d" % b, tag="h_turned%d" % b, align_bytes=64) for b in range(2)]
+        for b in range(2):
+            nc.vector.scalar_tensor_tensor(h_turned[b][:].rearrange("q (m t) -> q m t", t=PACK),
                                            diff_turned[b][:].rearrange("q (t m) -> q m t", t=PACK),
                                            ts_cols[:, 2 + b:3 + b],
                                            wt_all[:].rearrange("q (m t) -> q m t", t=PACK), ALU.mult, ALU.mult)
         dw_00 = dw_half(0, 0, "b3", "dw_00")
-        back = bank("a2")
-        h_turned_words = h_turned[:].rearrange("q b r -> q (b r)").bitcast(F32)
-        for b in range(2):
+        for b, tag in enumerate(("a2", "a3")):
+            back = bank(tag)
+            words = h_turned[b][:].bitcast(F32)
             for u in range(2):
-                nc.tensor.transpose(back[:, (2 * b + u) * P:(2 * b + u + 1) * P],
-                                    h_turned_words[:, b * HALF + u:(b + 1) * HALF:2], ident[:])
-        nc.scalar.copy(h_bf[:].bitcast(F32).rearrange("p (s g b c u) -> p g s b c u", s=PACK, g=2, b=2, u=2)[:, 1],
-                       back[:].rearrange("p (b u c s) -> p s b c u", b=2, u=2, s=PACK))
-        quantize_xm(P, 2 * P, xm_bf[:, 0:PACK * P])
+                nc.tensor.transpose(back[:, u * P:(u + 1) * P], words[:, u:HALF:2], ident[:])
+            nc.scalar.copy(h_bf[:].bitcast(F32)[:, N + b * HALF:N + (b + 1) * HALF].rearrange("p (q u) -> p q u", u=2),
+                           back[:, 0:HALF].rearrange("p (u q) -> p q u", u=2))
+        quantize_xm(1, 2)
         place_half(0, 0, dw_00)
-        quantize_h(1)
-        place_half(1, 0, dw_half(1, 0, "a0", "h_turned"))
+        quantize_h(HALF, N)
+        place_half(1, 0, dw_half(1, 0, "a2", "dw_10"))
         dw_second = [dw_half(j, 1, tag, "dw_%d1" % j) for j, tag in ((0, "b0"), (1, "b1"))]
-        quantize_xm(2 * P, 4 * P, xm_bf[:, PACK * P:])
+        round_xm(1, sb.tile([P, 2 * P * PACK], BF16, name="xm_bf1", tag="h_turned1", align_bytes=64))
+        quantize_xm(2, 4)
 
         def dw_block(j, bank_tag, tag):
             dw_ps = bank(bank_tag)
-            product(dw_ps[:], xm_r, E4, j, h_r, E5, slice(HALF, HALF + N))
+            product(dw_ps[:], xm_r[j // 2], E4, j % 2, h_r, E5, slice(HALF, HALF + N))
             dw_sb = sb.tile([P, N], F32, name="dw_sb%d" % j, tag=tag, align_bytes=64)
-            nc.scalar.copy(dw_sb[:].rearrange("p (g c s) -> p g c s", g=2, s=PACK),
-                           dw_ps[:].rearrange("p (g s c) -> p g c s", g=2, s=PACK))
+            nc.scalar.copy(dw_sb[:], dw_ps[:])
             return dw_sb
 
         def place(j, dw_sb):
@@ -257,33 +291,23 @@ def tile_attend_glse_wx_ts_kernel(tc, xT, wT, y, lse, wt, ts, xm, offs, out_0, o
             nc.vector.tensor_copy(window[:].indirect(offsets[:]), dw_sb[:])
             nc.sync.dma_start(out_0[j * P:(j + 1) * P, :], window[:])
 
-        w_i = mx_operand("w_i", "w_plane3")
-        for u, bank_tag, tag in ((0, "b2", "w_i_low"), (1, "b2", "w_plane1")):
-            turned = bank(bank_tag)
-            if u == 0:
-                turn_words(turned, w_low, lambda s: s, PACK)
-            else:
-                turn_words(turned, w_bf, lambda s: 2 * s + 1, 2 * PACK)
-            w_i_bf = sb.tile([P, HALF * PACK], BF16, name="w_i_bf%d" % u, tag=tag, align_bytes=64)
-            nc.scalar.copy(w_i_bf[:].rearrange("q (p e s) -> q p e s", e=2, s=PACK),
-                           turned[:].bitcast(BF16).rearrange("q (s p e) -> q p e s", s=PACK, e=2))
-            placed = slice(u * HALF, (u + 1) * HALF)
-            nc.vector.quantize_mx(out=w_i[0][:, placed].bitcast(E4), scales=w_i[1][:, placed], in_=w_i_bf[:])
+        quantize_w_i(1, w_i_high)
 
         for j in range(2):
             place_half(j, 1, dw_second[j])
         h_i_bf = sb.tile([P, R * PACK], BF16, name="h_i_bf", align_bytes=64)
         h_i_dst = h_i_bf[:].rearrange("q (u e p s) -> q u e p s", u=2, e=2, s=PACK)
-        for u, tag in ((0, "a1"), (1, "a3")):
+        for u, tag in ((0, "b0"), (1, "b1")):
             turned = bank(tag)
-            turn_words(turned, h_bf, lambda s: 2 * P * s + u, 2)
+            turn_words(turned, h_bf, lambda s: 2 * s + u, 2 * PACK)
             nc.scalar.copy(h_i_dst[:, u], turned[:].bitcast(BF16).rearrange("q (s p e) -> q e p s", s=PACK, e=2))
         h_i = mx_operand("h_i")
         quantize(h_i, E5, h_i_bf, 0, 512)
-        dw_2 = dw_block(2, "b2", "h_bf")
+        dw_2 = dw_block(2, "a1", "h_bf")
+        dw_3 = dw_block(3, "a1", "dw_3")
         gx_sb = sb.tile([P, PACK, D], F32, name="gx_sb")
         gx_rows = out_1[0].rearrange("(m j) d -> m j d", j=PACK)
-        for j, tag in enumerate(("b3", "a0", "a2", "b0")):
+        for j, tag in enumerate(("b3", "a0", "a2", "a3")):
             gx_ps = bank(tag)
             product(gx_ps[:], h_i, E5, j, w_i, E4, slice(0, D))
             nc.scalar.copy(gx_sb[:, j, :].rearrange("m (p u e) -> m p u e", u=2, e=2),
@@ -291,4 +315,4 @@ def tile_attend_glse_wx_ts_kernel(tc, xT, wT, y, lse, wt, ts, xm, offs, out_0, o
             if j % 2 == 1:
                 nc.scalar.dma_start(gx_rows[:, j - 1:j + 1, :], gx_sb[:, j - 1:j + 1, :])
         place(2, dw_2)
-        place(3, dw_block(3, "b2", "dw_3"))
+        place(3, dw_3)

@@ -101,7 +101,8 @@ def tile_attend_glse_wx_ts_kernel(tc, xT, wT, y, lse, wt, ts, xm, offs, out_0, o
         for t in range(PACK):
             nc.tensor.transpose(wt_all_ps[:, t * P:(t + 1) * P], wt_sb[:, t:t + 1].to_broadcast([P, P]), ident[:])
         wt_all = sb.tile([P, R], F32, name="wt_all")
-        nc.scalar.copy(wt_all[:].rearrange("p (m t) -> p m t", t=PACK), wt_all_ps[:].rearrange("p (t m) -> p m t", t=PACK))
+        nc.scalar.copy(wt_all[:].rearrange("p (u m e) -> p u m e", u=2, e=2),
+                       wt_all_ps[:].rearrange("p (u e m) -> p u m e", u=2, e=2))
 
         w_bf = sb.tile([P, N * PACK], BF16, name="w_bf", align_bytes=64)
         w_bf3 = w_bf[:].rearrange("p (i t) -> p i t", t=PACK)
@@ -259,16 +260,18 @@ def tile_attend_glse_wx_ts_kernel(tc, xT, wT, y, lse, wt, ts, xm, offs, out_0, o
         quantize_h(P, HALF)
         h_turned = [sb.tile([P, R], BF16, name="h_turned%d" % b, tag="h_turned%d" % b, align_bytes=64) for b in range(2)]
         for b in range(2):
-            nc.vector.scalar_tensor_tensor(h_turned[b][:].rearrange("q (m t) -> q m t", t=PACK),
-                                           diff_turned[b][:].rearrange("q (t m) -> q m t", t=PACK),
-                                           ts_cols[:, 2 + b:3 + b],
-                                           wt_all[:].rearrange("q (m t) -> q m t", t=PACK), ALU.mult, ALU.mult)
+            for u in range(2):
+                rows = slice(u * 2 * P, (u + 1) * 2 * P)
+                nc.vector.scalar_tensor_tensor(h_turned[b][:, rows].rearrange("q (m e) -> q m e", e=2),
+                                               diff_turned[b][:, rows].rearrange("q (e m) -> q m e", e=2),
+                                               ts_cols[:, 2 + b:3 + b],
+                                               wt_all[:, rows].rearrange("q (m e) -> q m e", e=2), ALU.mult, ALU.mult)
         dw_00 = dw_half(0, 0, "b3", "dw_00")
         for b, tag in enumerate(("a2", "a3")):
             back = bank(tag)
             words = h_turned[b][:].bitcast(F32)
             for u in range(2):
-                nc.tensor.transpose(back[:, u * P:(u + 1) * P], words[:, u:HALF:2], ident[:])
+                nc.tensor.transpose(back[:, u * P:(u + 1) * P], words[:, u * P:(u + 1) * P], ident[:])
             nc.scalar.copy(h_bf[:].bitcast(F32)[:, N + b * HALF:N + (b + 1) * HALF].rearrange("p (q u) -> p q u", u=2),
                            back[:, 0:HALF].rearrange("p (u q) -> p q u", u=2))
         quantize_xm(1, 2)

@@ -66,8 +66,8 @@ def tile_attend_glse_wx_ts_kernel(tc, xT, wT, y, lse, wt, ts, xm, offs, out_0, o
         nc.scalar.dma_start(wt_sb[:], wt[0].rearrange("(p t) o -> p (t o)", t=PACK))
         lse_sb = sb.tile([P, PACK], F32, name="lse_sb")
         nc.scalar.dma_start(lse_sb[:], lse[0].rearrange("(p t) o -> p (t o)", t=PACK))
-        nc.sync.dma_start(offsets[:], offs)
         nc.sync.dma_start(w_planes[0][:], wT_planes[0])
+        nc.sync.dma_start(offsets[:], offs)
         for t in range(1, PACK):
             nc.sync.dma_start(w_planes[t][:], wT_planes[t])
         nc.vector.memset(ts_table[0:P - 1, :], 0.0)
@@ -128,7 +128,7 @@ def tile_attend_glse_wx_ts_kernel(tc, xT, wT, y, lse, wt, ts, xm, offs, out_0, o
                sb.tile([P, D], U8, name="w_i_scales", align_bytes=64))
 
         def w_along_slots(u, w_i_bf):
-            turned = bank("b2")
+            turned = bank(("b2", "a1")[u])
             if u == 0:
                 turn_words(turned, w_low, lambda s: s, PACK)
             else:

@@ -18,7 +18,6 @@ ACT = mybir.ActivationFunctionType
 
 P = 128
 PACK = 4
-WINDOWS = 3
 HALF = N // 2
 
 
@@ -32,10 +31,11 @@ def tile_attend_glse_wx_ts_kernel(tc, xT, wT, y, lse, wt, ts, xm, offs, out_0, o
         def bank(tag):
             return ps.tile([P, 512], F32, name=tag, tag=tag)
 
-        def mx_operand(name, tag=None):
-            codes = sb.tile([P, 512], U32, name=name + "_codes", tag=tag or name + "_codes", align_bytes=64)
-            scales = sb.tile([P, 512], U8, name=name + "_scales", align_bytes=64)
-            return codes, scales
+        def tile(name, shape, dtype, tag=None):
+            return sb.tile(shape, dtype, name=name, tag=tag or name, align_bytes=64)
+
+        def mx_operand(name, width, tag=None):
+            return tile(name + "_codes", [P, width], U32, tag), tile(name + "_scales", [P, width], U8)
 
         def quantize(operand, fmt, src, c0, c1):
             codes, scales = operand
@@ -47,275 +47,235 @@ def tile_attend_glse_wx_ts_kernel(tc, xT, wT, y, lse, wt, ts, xm, offs, out_0, o
             nc.tensor.matmul_mx(out=out, lhsT=lhs[0][:, cols].bitcast(lhs_fmt), lhsT_scale=lhs[1][:, cols],
                                 rhs=rhs[0][:, moving].bitcast(rhs_fmt), rhs_scale=rhs[1][:, moving], start=True, stop=True)
 
-        def turn_words(out_bank, src, first_word, step):
-            words = src[:].bitcast(F32)
-            for s in range(PACK):
-                start = first_word(s)
-                nc.tensor.transpose(out_bank[:, s * P:(s + 1) * P],
-                                    words[:, start:start + (P - 1) * step + 1:step], ident[:])
+        def half_cols(half):
+            return slice(half * HALF, (half + 1) * HALF)
 
         def list_half(half):
             return offsets[:, half * HALF // 16:(half + 1) * HALF // 16]
 
-        w_planes = [sb.tile([P, T], F32, name="w_plane%d" % t, tag="w_plane%d" % t, align_bytes=64) for t in range(PACK)]
+        w_planes = [tile("w_plane%d" % t, [P, T], F32) for t in range(PACK)]
         wT_planes = wT.rearrange("(p t) c -> t p c", t=PACK)
         offsets = sb.tile([P, N // 16], U16, name="offsets")
-        ts_table = sb.tile([P, T], F32, name="ts_table")
+        ts_table = tile("ts_table", [P, T], F32)
         nc.scalar.dma_start(ts_table[P - 1:P, :], ts[0:1, :])
-        wt_sb = sb.tile([P, PACK], F32, name="wt_sb")
+        wt_sb = tile("wt_sb", [P, PACK], F32)
         nc.scalar.dma_start(wt_sb[:], wt[0].rearrange("(p t) o -> p (t o)", t=PACK))
-        lse_sb = sb.tile([P, PACK], F32, name="lse_sb")
+        lse_sb = tile("lse_sb", [P, PACK], F32)
         nc.scalar.dma_start(lse_sb[:], lse[0].rearrange("(p t) o -> p (t o)", t=PACK))
-        nc.sync.dma_start(w_planes[0][:], wT_planes[0])
         nc.sync.dma_start(offsets[:], offs)
-        for t in range(1, PACK):
+        for t in range(PACK):
             nc.sync.dma_start(w_planes[t][:], wT_planes[t])
-        nc.vector.memset(ts_table[0:P - 1, :], 0.0)
-        ident = sb.tile([P, P], F32, name="ident")
-        make_identity(nc, ident[:])
-        neg_lse = sb.tile([P, PACK], F32, name="neg_lse")
-        nc.gpsimd.tensor_scalar(neg_lse[:], lse_sb[:], -1.0, 0.0, ALU.mult, ALU.add)
-        h_r = (sb.tile([P, HALF + N], U32, name="h_r_codes", align_bytes=64),
-               sb.tile([P, HALF + N], U8, name="h_r_scales", align_bytes=64))
-        windows = [sb.tile([P, T], F32, name="window0")]
-        nc.vector.memset(windows[0][:], 0.0)
-        nc.vector.memset(h_r[0][:, 0:HALF], 0)
-        nc.vector.memset(h_r[1][:, 0:HALF].bitcast(U32), 0)
+        x_raw = [tile("x_raw0", [P, PACK, R // 2], F32),
+                 shared.tile([P, PACK, R // 2], F32, name="x_raw1", offset=0, align_bytes=64)]
+        for part in range(2):
+            nc.sync.dma_start(x_raw[part][:],
+                              xT[0].rearrange("(p t) r -> p t r", t=PACK)[:, :, part * R // 2:(part + 1) * R // 2])
+        y_rows = y[0].rearrange("(p t) i -> p t i", t=PACK)
+        y_sb = [tile("y_sb%d" % half, [P, PACK, HALF], F32) for half in range(2)]
+        xm_rows = xm[0].rearrange("(p t) d -> p t d", t=PACK)
+        xm_raw = [tile("xm_raw%d" % pair, [P, PACK, D // 2], F32) for pair in range(2)]
+        for pair in range(2):
+            nc.sync.dma_start(xm_raw[pair][:], xm_rows[:, :, pair * D // 2:(pair + 1) * D // 2])
+        for half in range(2):
+            nc.sync.dma_start(y_sb[half][:], y_rows[:, :, half_cols(half)])
 
-        ts_row = sb.tile([P, N], F32, name="ts_row")
-        nc.vector.tensor_copy(ts_row[:], ts_table[:].indirect(offsets[:]))
+        nc.vector.memset(ts_table[0:P - 1, :], 0.0)
+        ident = tile("ident", [P, P], F32)
+        make_identity(nc, ident[:])
+        windows = [tile("window%d" % j, [P, T], F32) for j in range(2)]
+        for window in windows:
+            nc.vector.memset(window[:], 0.0)
+        neg_lse = tile("neg_lse", [P, PACK], F32)
+        nc.gpsimd.tensor_scalar(neg_lse[:], lse_sb[:], -1.0, 0.0, ALU.mult, ALU.add)
+
+        ts_row = tile("ts_row", [P, N], F32)
+        nc.scalar.activation(ts_row[:], ts_table[:].indirect(offsets[:]), ACT.Copy)
+        w_rows = [tile("w_rows%d" % pair, [P, 2, N], BF16) for pair in range(2)]
+        nc.scalar.activation(w_rows[0][:, 0, :], w_planes[0][:].indirect(offsets[:]), ACT.Copy)
         ts_cols_ps = bank("b0")
         for k in range(4):
             nc.tensor.transpose(ts_cols_ps[:, k * P:(k + 1) * P], ts_row[:, k * P:(k + 1) * P], ident[:])
-        ts_cols = sb.tile([P, 4], F32, name="ts_cols")
+        ts_cols = tile("ts_cols", [P, 4], F32, "w_plane0")
         nc.scalar.copy(ts_cols[:], ts_cols_ps[:, P - 1:N:P])
         ts_all_ps = bank("b1")
         for k in range(4):
             nc.tensor.transpose(ts_all_ps[:, k * P:(k + 1) * P], ts_cols[:, k:k + 1].to_broadcast([P, P]), ident[:])
-        ts_all = sb.tile([P, N], F32, name="ts_all")
+        ts_all = tile("ts_all", [P, N], F32)
         nc.scalar.copy(ts_all[:], ts_all_ps[:])
-        wt_ts = sb.tile([P, PACK, HALF], F32, name="wt_ts")
+        wt_ts = tile("wt_ts", [P, PACK, N], F32)
         for t in range(PACK):
-            nc.scalar.activation(wt_ts[:, t, :], ts_all_ps[:, 0:HALF], ACT.Copy, scale=wt_sb[:, t:t + 1])
-        wt_all_ps = bank("a0")
-        for t in range(PACK):
-            nc.tensor.transpose(wt_all_ps[:, t * P:(t + 1) * P], wt_sb[:, t:t + 1].to_broadcast([P, P]), ident[:])
-        wt_all = sb.tile([P, R], F32, name="wt_all")
-        nc.scalar.copy(wt_all[:].rearrange("p (u m e) -> p u m e", u=2, e=2),
-                       wt_all_ps[:].rearrange("p (u e m) -> p u m e", u=2, e=2))
+            nc.scalar.activation(wt_ts[:, t, :], ts_all_ps[:], ACT.Copy, scale=wt_sb[:, t:t + 1])
 
-        w_bf = sb.tile([P, N * PACK], BF16, name="w_bf", align_bytes=64)
+        w_bf = tile("w_bf", [P, N * PACK], BF16)
         w_bf3 = w_bf[:].rearrange("p (i t) -> p i t", t=PACK)
-        w_low = sb.tile([P, N * 2], BF16, name="w_low", align_bytes=64)
-        w_low3 = w_low[:].rearrange("p (i e) -> p i e", e=2)
-        for t in range(2):
-            nc.vector.tensor_copy(w_low3[:, :, t], w_planes[t][:].indirect(offsets[:]))
-        nc.vector.tensor_copy(w_bf[:].bitcast(F32)[:, 0:2 * N:2], w_low[:].bitcast(F32))
-        nc.vector.tensor_copy(w_bf3[:, :, 2], w_planes[2][:].indirect(offsets[:]))
+        nc.vector.tensor_copy(w_rows[0][:, 1, :], w_planes[1][:].indirect(offsets[:]))
+
+        def weave(pair, slots):
+            planes = slice(2 * pair, 2 * pair + 2)
+            nc.vector.tensor_copy(w_bf3[:, slots, planes], w_rows[pair][:, :, slots].rearrange("p t i -> p i t"))
+
+        w_i_bf = []
+
+        def turn_w(pair, tag, dst):
+            w_i_bf.append(dst)
+            turned = bank(tag)
+            for k in range(2):
+                words = w_rows[pair][:, k, :].bitcast(F32)
+                for u in range(2):
+                    nc.tensor.transpose(turned[:, (2 * k + u) * P:(2 * k + u + 1) * P], words[:, u:HALF:2], ident[:])
+            nc.scalar.copy(dst[:].bitcast(F32).rearrange("q (p k u) -> q p k u", k=2, u=2),
+                           turned[:].rearrange("q (k u p) -> q p k u", k=2, u=2))
+
+        weave(0, slice(0, N))
+        turn_w(0, "b0", tile("w_i_low", [P, HALF * PACK], BF16))
+        nc.vector.tensor_copy(w_rows[1][:, 0, :], w_planes[2][:].indirect(offsets[:]))
+        nc.vector.tensor_copy(w_rows[1][:, 1, half_cols(0)], w_planes[3][:].indirect(list_half(0)))
+        nc.scalar.activation(w_rows[1][:, 1, half_cols(1)], w_planes[3][:].indirect(list_half(1)), ACT.Copy)
         for half in range(2):
-            nc.vector.tensor_copy(w_bf3[:, half * HALF:(half + 1) * HALF, PACK - 1],
-                                  w_planes[PACK - 1][:].indirect(list_half(half)))
-        w_d = []
+            weave(1, half_cols(half))
+        w_d = mx_operand("w_d", N)
+        quantize(w_d, E4, w_bf, 0, N)
 
-        def quantize_w_d(half, tag):
-            w_d.append((sb.tile([P, HALF], U32, name="w_d_codes%d" % half, tag=tag, align_bytes=64),
-                        sb.tile([P, HALF], U8, name="w_d_scales%d" % half, align_bytes=64)))
-            nc.vector.quantize_mx(out=w_d[half][0][:].bitcast(E4), scales=w_d[half][1][:],
-                                  in_=w_bf[:, half * PACK * HALF:(half + 1) * PACK * HALF])
+        def turn_pairs(tag, src, u):
+            pairs = bank(tag)
+            words = src[:].bitcast(F32)
+            for s in range(PACK):
+                start = 2 * s + u
+                nc.tensor.transpose(pairs[:, s * P:(s + 1) * P], words[:, start:start + (P - 1) * 8 + 1:8], ident[:])
+            return pairs[:].bitcast(BF16)
 
-        quantize_w_d(0, "w_d_codes0")
-        w_i = (shared.tile([P, D], U32, name="w_i_codes", offset=4096, align_bytes=64),
-               sb.tile([P, D], U8, name="w_i_scales", align_bytes=64))
-
-        def w_along_slots(u, w_i_bf):
-            turned = bank(("b2", "a1")[u])
-            if u == 0:
-                turn_words(turned, w_low, lambda s: s, PACK)
-            else:
-                turn_words(turned, w_bf, lambda s: 2 * s + 1, 2 * PACK)
-            nc.scalar.copy(w_i_bf[:].rearrange("q (p e s) -> q p e s", e=2, s=PACK),
-                           turned[:].bitcast(BF16).rearrange("q (s p e) -> q p e s", s=PACK, e=2))
-            return w_i_bf
-
-        def quantize_w_i(u, w_i_bf):
-            placed = slice(u * HALF, (u + 1) * HALF)
-            nc.vector.quantize_mx(out=w_i[0][:, placed].bitcast(E4), scales=w_i[1][:, placed], in_=w_i_bf[:])
-
-        w_i_low = w_along_slots(0, sb.tile([P, HALF * PACK], BF16, name="w_i_low", align_bytes=64))
-
-        x_raw = []
-        for part in range(2):
-            x_raw.append(sb.tile([P, PACK, R // 2], F32, name="x_raw%d" % part, tag="w_plane%d" % part, align_bytes=64))
-            nc.sync.dma_start(x_raw[part][:],
-                              xT[0].rearrange("(p t) r -> p t r", t=PACK)[:, :, part * R // 2:(part + 1) * R // 2])
-        x_bf = shared.tile([P, R * PACK], BF16, name="x_bf", offset=3072, align_bytes=64)
+        x_bf = tile("x_bf", [P, R * PACK], BF16, "w_plane3")
         x_dst = x_bf[:].rearrange("p (j m t) -> p m t j", j=PACK, t=PACK)
         x_src = [x_raw[part][:].rearrange("p t (m j) -> p m t j", j=PACK) for part in range(2)]
         nc.scalar.copy(x_dst[:, 0:64, :, 0:2], x_src[0][:, :, :, 0:2])
         nc.scalar.copy(x_dst[:, 0:64, :, 2:4], x_src[0][:, :, :, 2:4])
         nc.vector.tensor_copy(x_dst[:, 64:128, :, 0:2], x_src[1][:, :, :, 0:2])
         nc.scalar.copy(x_dst[:, 64:128, :, 2:4], x_src[1][:, :, :, 2:4])
-        x_d = mx_operand("x_d")
+        x_d = mx_operand("x_d", R)
         quantize(x_d, E4, x_bf, 0, P)
         quantize(x_d, E4, x_bf, P, 2 * P)
         quantize(x_d, E4, x_bf, 2 * P, 4 * P)
-        quantize_w_d(1, "w_plane1")
-        quantize_w_i(0, w_i_low)
-        windows.append(shared.tile([P, T], F32, name="window1", offset=6144, align_bytes=64))
-        nc.gpsimd.memset(windows[1][:], 0.0)
+        turn_w(1, "b1", shared.tile([P, HALF * PACK], BF16, name="w_i_high", offset=0, align_bytes=64))
+        xm_bf = []
 
-        y_rows = y[0].rearrange("(p t) i -> p t i", t=PACK)
-        xm_rows = xm[0].rearrange("(p t) d -> p t d", t=PACK)
-        y_both = sb.tile([P, 2 * PACK * HALF], F32, name="y_both", tag="w_plane2", align_bytes=64)
-        y_sb = [y_both[:, half * PACK * HALF:(half + 1) * PACK * HALF].rearrange("p (t i) -> p t i", t=PACK)
-                for half in range(2)]
-        xm_raw = sb.tile([P, PACK, D], F32, name="xm_raw", tag="w_plane0", align_bytes=64)
-        nc.sync.dma_start(y_sb[1], y_rows[:, :, HALF:N])
-        nc.sync.dma_start(y_sb[0], y_rows[:, :, 0:HALF])
-        nc.sync.dma_start(xm_raw[:], xm_rows)
+        def round_xm(pair, dst, copy):
+            xm_bf.append(dst)
+            copy(xm_bf[pair][:].rearrange("p (c i t) -> p c t i", i=4, t=PACK),
+                           xm_raw[pair][:].rearrange("p t (c i) -> p c t i", i=4))
 
-        neg_y = sb.tile([P, PACK, HALF], F32, name="neg_y")
-        nc.scalar.activation(neg_y[:], y_sb[1], ACT.Copy, scale=-1.0)
+        xm_r = []
+
+        def quantize_xm(pair, tag):
+            xm_r.append(mx_operand("xm_r%d" % pair, 2 * P, tag))
+            quantize(xm_r[pair], E4, xm_bf[pair], 0, 2 * P)
+
+        round_xm(0, shared.tile([P, HALF * PACK], BF16, name="xm_bf0", offset=2048, align_bytes=64), nc.scalar.copy)
+        xm_bf.append(tile("xm_bf1", [P, HALF * PACK], BF16, "w_plane3"))
+        nc.gpsimd.tensor_scalar(xm_bf[1][:].rearrange("p (c t) -> p c t", t=PACK), xm_raw[1][:].rearrange("p t c -> p c t"),
+                                1.0, 0.0, ALU.mult, ALU.add)
+        windows.append(tile("window2", [P, T], F32, "xm_raw1"))
+        windows.append(tile("window3", [P, T], F32, "xm_raw0"))
+        for window in windows[2:]:
+            nc.gpsimd.memset(window[:], 0.0)
+
         probs = []
-        score_banks = (((0, 1, "b3"), (1, 2, "a0"), (2, 4, "a1")), ((0, 2, "a2"), (2, 4, "a3")))
         for half in range(2):
-            slots = slice(half * HALF, (half + 1) * HALF)
-            if half == 0:
-                scaled = shared.tile([P, PACK, HALF], F32, name="scaled0", offset=0, align_bytes=64)
-            else:
-                scaled = shared.tile([P, PACK, HALF], F32, name="scaled1", offset=14336, align_bytes=64)
-            probs.append(sb.tile([P, PACK, HALF], F32, name="probs%d" % half))
-            for j0, j1, tag in score_banks[half]:
-                a_ps = bank(tag)
-                for j in range(j0, j1):
-                    product(a_ps[:, (j - j0) * HALF:(j - j0 + 1) * HALF], x_d, E4, j, w_d[half], E4, slice(0, HALF))
-                nc.vector.tensor_tensor(scaled[:, j0:j1, :],
-                                        a_ps[:, 0:(j1 - j0) * HALF].rearrange("p (j i) -> p j i", i=HALF),
-                                        ts_all[:, slots].unsqueeze(1).to_broadcast([P, j1 - j0, HALF]), ALU.mult)
-                for j in range(j0, j1):
+            scaled = tile("scaled%d" % half, [P, PACK, HALF], F32)
+            probs.append(tile("probs%d" % half, [P, PACK, HALF], F32))
+            for pair in range(2):
+                a_ps = bank("a%d" % (2 * half + pair))
+                for k in range(2):
+                    product(a_ps[:, half_cols(k)], x_d, E4, 2 * pair + k, w_d, E4, half_cols(half))
+                nc.vector.tensor_tensor(scaled[:, 2 * pair:2 * pair + 2, :], a_ps[:].rearrange("p (j i) -> p j i", i=HALF),
+                                        ts_all[:, half_cols(half)].unsqueeze(1).to_broadcast([P, 2, HALF]), ALU.mult)
+                for j in range(2 * pair, 2 * pair + 2):
                     nc.scalar.activation(probs[half][:, j, :], scaled[:, j, :], ACT.Exp,
                                          bias=neg_lse[:, j:j + 1], scale=1.0)
 
-        windows.append(sb.tile([P, T], F32, name="window2", tag="x_d_codes", align_bytes=64))
-        nc.gpsimd.memset(windows[2][:], 0.0)
 
-        diff_turned = [bank("b0"), bank("b1")]
-        for term, src in enumerate((neg_y, probs[1])):
-            for j in range(PACK):
-                for b in range(2):
-                    nc.tensor.matmul(diff_turned[b][:, j * P:(j + 1) * P], src[:, j, b * P:(b + 1) * P], ident[:],
-                                     start=(term == 0 and j == 0), stop=(term == 1 and j == PACK - 1),
-                                     is_transpose=True)
-
-        xm_bf = []
-
-        def round_xm(pair, tile):
-            xm_bf.append(tile)
-            dst = tile[:].rearrange("p (c i t) -> p c t i", i=4, t=PACK)
-            for k in range(2):
-                j = 2 * pair + k
-                nc.scalar.copy(dst[:, 32 * k:32 * (k + 1)],
-                               xm_raw[:, :, j * P:(j + 1) * P].rearrange("p t (c i) -> p c t i", i=4))
-
-        round_xm(0, shared.tile([P, 2 * P * PACK], BF16, name="xm_bf0", offset=14336, align_bytes=64))
-        w_i_high = w_along_slots(1, shared.tile([P, HALF * PACK], BF16, name="w_i_high", offset=16384, align_bytes=64))
-        xm_r = [(sb.tile([P, 2 * P], U32, name="xm_r_codes%d" % pair, tag="xm_r_codes%d" % pair, align_bytes=64),
-                 sb.tile([P, 2 * P], U8, name="xm_r_scales%d" % pair, align_bytes=64)) for pair in range(2)]
-
-        def quantize_xm(j0, j1):
-            codes, scales = xm_r[j0 // 2]
-            placed = slice((j0 % 2) * P, (j0 % 2 + j1 - j0) * P)
-            nc.vector.quantize_mx(out=codes[:, placed].bitcast(E4), scales=scales[:, placed],
-                                  in_=xm_bf[j0 // 2][:, PACK * placed.start:PACK * placed.stop])
-
-        h_bf = sb.tile([P, N * PACK], BF16, name="h_bf", tag="h_bf", align_bytes=64)
+        h_bf = tile("h_bf", [P, N * PACK], BF16)
         h_dst = h_bf[:].rearrange("p (c i t) -> p c t i", i=4, t=PACK)
+        h_r = mx_operand("h_r", N)
 
-        def quantize_h(c0, c1):
-            placed = slice(HALF + c0, HALF + c1)
-            nc.vector.quantize_mx(out=h_r[0][:, placed].bitcast(E5), scales=h_r[1][:, placed],
-                                  in_=h_bf[:, PACK * c0:PACK * c1])
+        def subtract(c0, c1, tag):
+            half = c0 // HALF
+            cols = slice(c0 - half * HALF, c1 - half * HALF)
+            diff = tile("diff%d" % c0, [P, PACK, c1 - c0], F32, tag)
+            nc.vector.tensor_tensor(diff[:], probs[half][:, :, cols], y_sb[half][:, :, cols], ALU.subtract)
+            return diff
 
-        def dw_half(j, half, bank_tag, tag):
-            dw_ps = bank(bank_tag)
-            product(dw_ps[:], xm_r[j // 2], E4, j % 2, h_r, E5, slice(half * HALF, half * HALF + N))
-            dw_sb = sb.tile([P, HALF], F32, name="dw_sb%d_%d" % (j, half), tag=tag, align_bytes=64)
-            nc.scalar.copy(dw_sb[:], dw_ps[:, HALF:N])
-            return dw_sb
+        def weigh(c0, diff):
+            nc.vector.tensor_tensor(h_dst[:, c0 // 4:(c0 + P) // 4], diff.rearrange("p t (c i) -> p c t i", i=4),
+                                    wt_ts[:, :, c0:c0 + P].rearrange("p t (c i) -> p c t i", i=4), ALU.mult)
 
-        def place_half(j, half, dw_sb):
-            nc.vector.tensor_copy(windows[j][:].indirect(list_half(half)), dw_sb[:])
-            if half == 1:
-                nc.sync.dma_start(out_0[j * P:(j + 1) * P, :], windows[j][:])
+        def store_window(j):
+            nc.sync.dma_start(out_0[j * P:(j + 1) * P, :], windows[j][:])
 
-        diff = [sb.tile([P, PACK, P], F32, name="diff%d" % b) for b in range(2)]
+        def scatter_on_scalar(j, half, src):
+            nc.scalar.activation(windows[j][:].indirect(list_half(half)), src, ACT.Copy)
+
+        diff_first = [subtract(b * P, (b + 1) * P, "diff%d" % b) for b in range(2)]
         for b in range(2):
-            cols = slice(b * P, (b + 1) * P)
-            nc.vector.tensor_tensor(diff[b][:], probs[0][:, :, cols], y_sb[0][:, :, cols], ALU.subtract)
+            weigh(b * P, diff_first[b][:])
+        quantize(h_r, E5, h_bf, 0, P)
+        quantize_xm(0, "diff0")
+        quantize(h_r, E5, h_bf, P, HALF)
+        diff_second = [subtract(HALF, HALF + P, "diff1"), subtract(HALF + P, N, "probs0")]
+        dw_first_ps = bank("b0")
+        for j in range(2):
+            product(dw_first_ps[:, half_cols(j)], xm_r[0], E4, j, h_r, E5, half_cols(0))
+        dw_first = tile("dw_first", [P, N], F32)
+        nc.scalar.copy(dw_first[:], dw_first_ps[:])
+        for j in range(2):
+            scatter_on_scalar(j, 0, dw_first[:, half_cols(j)])
+
         for b in range(2):
-            nc.vector.tensor_tensor(h_dst[:, 32 * b:32 * (b + 1)], diff[b][:].rearrange("p t (c i) -> p c t i", i=4),
-                                    wt_ts[:, :, b * P:(b + 1) * P].rearrange("p t (c i) -> p c t i", i=4), ALU.mult)
-        quantize_h(0, P)
-        quantize_xm(0, 1)
-        quantize_h(P, HALF)
-        h_turned = [sb.tile([P, R], BF16, name="h_turned%d" % b, tag="h_turned%d" % b, align_bytes=64) for b in range(2)]
-        for b in range(2):
-            for u in range(2):
-                rows = slice(u * 2 * P, (u + 1) * 2 * P)
-                nc.vector.scalar_tensor_tensor(h_turned[b][:, rows].rearrange("q (m e) -> q m e", e=2),
-                                               diff_turned[b][:, rows].rearrange("q (e m) -> q m e", e=2),
-                                               ts_cols[:, 2 + b:3 + b],
-                                               wt_all[:, rows].rearrange("q (m e) -> q m e", e=2), ALU.mult, ALU.mult)
-        dw_00 = dw_half(0, 0, "b3", "dw_00")
-        for b, tag in enumerate(("a2", "a3")):
-            back = bank(tag)
-            words = h_turned[b][:].bitcast(F32)
-            for u in range(2):
-                nc.tensor.transpose(back[:, u * P:(u + 1) * P], words[:, u * P:(u + 1) * P], ident[:])
-            nc.scalar.copy(h_bf[:].bitcast(F32)[:, N + b * HALF:N + (b + 1) * HALF].rearrange("p (q u) -> p q u", u=2),
-                           back[:, 0:HALF].rearrange("p (u q) -> p q u", u=2))
-        quantize_xm(1, 2)
-        place_half(0, 0, dw_00)
-        quantize_h(HALF, N)
-        place_half(1, 0, dw_half(1, 0, "a2", "dw_10"))
-        dw_second = [dw_half(j, 1, tag, "dw_%d1" % j) for j, tag in ((0, "b0"), (1, "b1"))]
-        round_xm(1, sb.tile([P, 2 * P * PACK], BF16, name="xm_bf1", tag="h_turned1", align_bytes=64))
-        quantize_xm(2, 4)
+            weigh(HALF + b * P, diff_second[b][:])
+        quantize(h_r, E5, h_bf, HALF, HALF + P)
+        quantize(h_r, E5, h_bf, HALF + P, N)
+        quantize_xm(1, "diff1")
+        dw_second = []
+        for j in range(2):
+            dw_ps = bank("b1")
+            product(dw_ps[:, 0:HALF], xm_r[0], E4, j, h_r, E5, half_cols(1))
+            dw_second.append(tile("dw_second%d" % j, [P, HALF], F32))
+            (nc.vector.tensor_copy, nc.scalar.copy)[j](dw_second[j][:], dw_ps[:, 0:HALF])
 
         def dw_block(j, bank_tag, tag):
             dw_ps = bank(bank_tag)
-            product(dw_ps[:], xm_r[j // 2], E4, j % 2, h_r, E5, slice(HALF, HALF + N))
-            dw_sb = sb.tile([P, N], F32, name="dw_sb%d" % j, tag=tag, align_bytes=64)
+            product(dw_ps[:], xm_r[1], E4, j - 2, h_r, E5, slice(0, N))
+            dw_sb = tile("dw_late%d" % j, [P, N], F32, tag)
             nc.scalar.copy(dw_sb[:], dw_ps[:])
             return dw_sb
 
-        def place(j, dw_sb):
-            window = windows[j % WINDOWS]
-            nc.vector.tensor_copy(window[:].indirect(offsets[:]), dw_sb[:])
-            nc.sync.dma_start(out_0[j * P:(j + 1) * P, :], window[:])
+        nc.vector.tensor_copy(windows[0][:].indirect(list_half(1)), dw_second[0][:])
+        store_window(0)
+        dw_2 = dw_block(2, "a0", "dw_2")
+        scatter_on_scalar(1, 1, dw_second[1][:])
+        store_window(1)
+        nc.vector.tensor_copy(windows[2][:].indirect(offsets[:]), dw_2[:])
+        store_window(2)
 
-        quantize_w_i(1, w_i_high)
-
-        for j in range(2):
-            place_half(j, 1, dw_second[j])
-        h_i_bf = sb.tile([P, R * PACK], BF16, name="h_i_bf", align_bytes=64)
+        h_i_bf = tile("h_i_bf", [P, R * PACK], BF16)
         h_i_dst = h_i_bf[:].rearrange("q (u e p s) -> q u e p s", u=2, e=2, s=PACK)
-        for u, tag in ((0, "b0"), (1, "b1")):
-            turned = bank(tag)
-            turn_words(turned, h_bf, lambda s: 2 * s + u, 2 * PACK)
-            nc.scalar.copy(h_i_dst[:, u], turned[:].bitcast(BF16).rearrange("q (s p e) -> q e p s", s=PACK, e=2))
-        h_i = mx_operand("h_i")
-        quantize(h_i, E5, h_i_bf, 0, 512)
-        dw_2 = dw_block(2, "a1", "h_bf")
-        dw_3 = dw_block(3, "a1", "dw_3")
-        gx_sb = sb.tile([P, PACK, D], F32, name="gx_sb")
+        for u, tag in ((0, "b1"), (1, "a0")):
+            nc.scalar.copy(h_i_dst[:, u], turn_pairs(tag, h_bf, u).rearrange("q (s p e) -> q e p s", s=PACK, e=2))
+        w_i = mx_operand("w_i", D, "dw_2")
+        for pair in range(2):
+            placed = half_cols(pair)
+            nc.vector.quantize_mx(out=w_i[0][:, placed].bitcast(E4), scales=w_i[1][:, placed], in_=w_i_bf[pair][:])
+        h_i = mx_operand("h_i", R)
+        quantize(h_i, E5, h_i_bf, 0, R)
+        dw_3 = dw_block(3, "b1", "dw_3")
+        for half in range(2):
+            scatter_on_scalar(3, half, dw_3[:, half_cols(half)])
+        gx_sb = tile("gx_sb", [P, PACK, D], F32)
         gx_rows = out_1[0].rearrange("(m j) d -> m j d", j=PACK)
-        for j, tag in enumerate(("b3", "a0", "a2", "a3")):
+        for j, tag in enumerate(("b3", "a2", "a3", "b2")):
             gx_ps = bank(tag)
             product(gx_ps[:], h_i, E5, j, w_i, E4, slice(0, D))
-            nc.scalar.copy(gx_sb[:, j, :].rearrange("m (p u e) -> m p u e", u=2, e=2),
-                           gx_ps[:].rearrange("m (u p e) -> m p u e", u=2, e=2))
+            nc.vector.tensor_copy(gx_sb[:, j, :].rearrange("m (p u k) -> m p u k", u=2, k=2),
+                                  gx_ps[:].rearrange("m (u p k) -> m p u k", u=2, k=2))
             if j % 2 == 1:
-                nc.scalar.dma_start(gx_rows[:, j - 1:j + 1, :], gx_sb[:, j - 1:j + 1, :])
-        place(2, dw_2)
-        place(3, dw_3)
+                nc.sync.dma_start(gx_rows[:, j - 1:j + 1, :], gx_sb[:, j - 1:j + 1, :])
+        store_window(3)

@@ -170,17 +170,10 @@ def tile_attend_glse_wx_ts_kernel(tc, xT, wT, y, lse, wt, ts, xm, offs, out_0, o
             quantize(xm_r[pair], E4, xm_bf[pair], 0, 2 * P)
 
         round_xm(0, shared.tile([P, HALF * PACK], BF16, name="xm_bf0", offset=2048, align_bytes=64), nc.scalar.copy)
-        xm_bf.append(tile("xm_bf1", [P, HALF * PACK], BF16, "w_plane3"))
-        nc.gpsimd.tensor_scalar(xm_bf[1][:].rearrange("p (c t) -> p c t", t=PACK), xm_raw[1][:].rearrange("p t c -> p c t"),
-                                1.0, 0.0, ALU.mult, ALU.add)
-        windows.append(tile("window2", [P, T], F32, "xm_raw1"))
-        windows.append(tile("window3", [P, T], F32, "xm_raw0"))
-        for window in windows[2:]:
-            nc.gpsimd.memset(window[:], 0.0)
 
         probs = []
         for half in range(2):
-            scaled = tile("scaled%d" % half, [P, PACK, HALF], F32)
+            scaled = shared.tile([P, PACK, HALF], F32, name="scaled%d" % half, offset=8192 + half * 4096, align_bytes=64)
             probs.append(tile("probs%d" % half, [P, PACK, HALF], F32))
             for pair in range(2):
                 a_ps = bank("a%d" % (2 * half + pair))
@@ -192,6 +185,8 @@ def tile_attend_glse_wx_ts_kernel(tc, xT, wT, y, lse, wt, ts, xm, offs, out_0, o
                     nc.scalar.activation(probs[half][:, j, :], scaled[:, j, :], ACT.Exp,
                                          bias=neg_lse[:, j:j + 1], scale=1.0)
 
+
+        round_xm(1, shared.tile([P, HALF * PACK], BF16, name="xm_bf1", offset=11264, align_bytes=64), nc.scalar.copy)
 
         h_bf = tile("h_bf", [P, N * PACK], BF16)
         h_dst = h_bf[:].rearrange("p (c i t) -> p c t i", i=4, t=PACK)
@@ -233,7 +228,10 @@ def tile_attend_glse_wx_ts_kernel(tc, xT, wT, y, lse, wt, ts, xm, offs, out_0, o
             weigh(HALF + b * P, diff_second[b][:])
         quantize(h_r, E5, h_bf, HALF, HALF + P)
         quantize(h_r, E5, h_bf, HALF + P, N)
-        quantize_xm(1, "diff1")
+        quantize_xm(1, "probs0")
+        for j, offset in ((2, 4096), (3, 12288)):
+            windows.append(shared.tile([P, T], F32, name="window%d" % j, offset=offset, align_bytes=64))
+            nc.gpsimd.memset(windows[j][:], 0.0)
         dw_second = []
         for j in range(2):
             dw_ps = bank("b1")

@@ -74,15 +74,15 @@ def tile_attend_glse_wx_ts_kernel(tc, xT, wT, y, lse, wt, ts, xm, offs, out_0, o
         y_sb = [tile("y_sb%d" % half, [P, PACK, HALF], F32) for half in range(2)]
         xm_rows = xm[0].rearrange("(p t) d -> p t d", t=PACK)
         xm_raw = [tile("xm_raw%d" % pair, [P, PACK, D // 2], F32) for pair in range(2)]
-        for pair in range(2):
-            nc.sync.dma_start(xm_raw[pair][:], xm_rows[:, :, pair * D // 2:(pair + 1) * D // 2])
+        nc.sync.dma_start(xm_raw[0][:], xm_rows[:, :, 0:D // 2])
         for half in range(2):
             nc.sync.dma_start(y_sb[half][:], y_rows[:, :, half_cols(half)])
+        nc.sync.dma_start(xm_raw[1][:], xm_rows[:, :, D // 2:D])
 
         nc.vector.memset(ts_table[0:P - 1, :], 0.0)
         ident = tile("ident", [P, P], F32)
         make_identity(nc, ident[:])
-        windows = [tile("window%d" % j, [P, T], F32) for j in range(2)]
+        windows = [tile("window%d" % j, [P, T], F32) for j in range(3)]
         for window in windows:
             nc.vector.memset(window[:], 0.0)
         neg_lse = tile("neg_lse", [P, PACK], F32)
@@ -171,22 +171,43 @@ def tile_attend_glse_wx_ts_kernel(tc, xT, wT, y, lse, wt, ts, xm, offs, out_0, o
 
         round_xm(0, shared.tile([P, HALF * PACK], BF16, name="xm_bf0", offset=2048, align_bytes=64), nc.scalar.copy)
 
-        probs = []
-        for half in range(2):
-            scaled = shared.tile([P, PACK, HALF], F32, name="scaled%d" % half, offset=8192 + half * 4096, align_bytes=64)
-            probs.append(tile("probs%d" % half, [P, PACK, HALF], F32))
-            for pair in range(2):
-                a_ps = bank("a%d" % (2 * half + pair))
-                for k in range(2):
-                    product(a_ps[:, half_cols(k)], x_d, E4, 2 * pair + k, w_d, E4, half_cols(half))
-                nc.vector.tensor_tensor(scaled[:, 2 * pair:2 * pair + 2, :], a_ps[:].rearrange("p (j i) -> p j i", i=HALF),
-                                        ts_all[:, half_cols(half)].unsqueeze(1).to_broadcast([P, 2, HALF]), ALU.mult)
-                for j in range(2 * pair, 2 * pair + 2):
-                    nc.scalar.activation(probs[half][:, j, :], scaled[:, j, :], ACT.Exp,
-                                         bias=neg_lse[:, j:j + 1], scale=1.0)
+        probs = [tile("probs%d" % half, [P, PACK, HALF], F32) for half in range(2)]
 
+        def exp_rows(j, c0, src):
+            half = c0 // HALF
+            width = src.shape[1]
+            nc.scalar.activation(probs[half][:, j, c0 - half * HALF:c0 - half * HALF + width], src, ACT.Exp,
+                                 bias=neg_lse[:, j:j + 1], scale=1.0)
 
-        round_xm(1, shared.tile([P, HALF * PACK], BF16, name="xm_bf1", offset=11264, align_bytes=64), nc.scalar.copy)
+        scaled = shared.tile([P, PACK, HALF], F32, name="scaled", offset=10240, align_bytes=64)
+        for pair in range(2):
+            a_ps = bank("a%d" % pair)
+            for k in range(2):
+                product(a_ps[:, half_cols(k)], x_d, E4, 2 * pair + k, w_d, E4, half_cols(0))
+            nc.vector.tensor_tensor(scaled[:, 2 * pair:2 * pair + 2, :], a_ps[:].rearrange("p (j i) -> p j i", i=HALF),
+                                    ts_all[:, half_cols(0)].unsqueeze(1).to_broadcast([P, 2, HALF]), ALU.mult)
+            for j in range(2 * pair, 2 * pair + 2):
+                exp_rows(j, 0, scaled[:, j, :])
+        a_ps = bank("a2")
+        third = slice(HALF, HALF + P)
+        for j in range(PACK):
+            product(a_ps[:, j * P:(j + 1) * P], x_d, E4, j, w_d, E4, third)
+        scaled_third = tile("scaled_third", [P, PACK, P], F32)
+        nc.vector.tensor_tensor(scaled_third[:], a_ps[:].rearrange("p (j i) -> p j i", i=P),
+                                ts_all[:, third].unsqueeze(1).to_broadcast([P, PACK, P]), ALU.mult)
+        a_ps = bank("a3")
+        product(a_ps[:], w_d, E4, 3, x_d, E4, slice(0, R))
+        scaled_last = shared.tile([P, R], F32, name="scaled_last", offset=11264, align_bytes=64)
+        nc.scalar.activation(scaled_last[:], a_ps[:], ACT.Copy, scale=ts_cols[:, 3:4])
+        by_row = bank("b2")
+        for j in range(PACK):
+            nc.tensor.transpose(by_row[:, j * P:(j + 1) * P], scaled_last[:, j * P:(j + 1) * P], ident[:])
+        for j in range(PACK):
+            exp_rows(j, HALF, scaled_third[:, j, :])
+        for j in range(PACK):
+            exp_rows(j, HALF + P, by_row[:, j * P:(j + 1) * P])
+
+        xm_late = shared.tile([P, HALF * PACK], BF16, name="xm_bf1", offset=11264, align_bytes=64)
 
         h_bf = tile("h_bf", [P, N * PACK], BF16)
         h_dst = h_bf[:].rearrange("p (c i t) -> p c t i", i=4, t=PACK)
@@ -204,18 +225,22 @@ def tile_attend_glse_wx_ts_kernel(tc, xT, wT, y, lse, wt, ts, xm, offs, out_0, o
                                     wt_ts[:, :, c0:c0 + P].rearrange("p t (c i) -> p c t i", i=4), ALU.mult)
 
         def store_window(j):
-            nc.sync.dma_start(out_0[j * P:(j + 1) * P, :], windows[j][:])
+            nc.sync.dma_start(out_0[j * P:(j + 1) * P, :], windows[j % 3][:])
 
         def scatter_on_scalar(j, half, src):
-            nc.scalar.activation(windows[j][:].indirect(list_half(half)), src, ACT.Copy)
+            nc.scalar.activation(windows[j % 3][:].indirect(list_half(half)), src, ACT.Copy)
 
-        diff_first = [subtract(b * P, (b + 1) * P, "diff%d" % b) for b in range(2)]
+        diff_first = tile("diff_first", [P, PACK, HALF], F32)
+        for pair in range(2):
+            rows = slice(2 * pair, 2 * pair + 2)
+            nc.vector.tensor_tensor(diff_first[:, rows, :], probs[0][:, rows, :], y_sb[0][:, rows, :], ALU.subtract)
+        quantize_xm(0, "y_sb0")
         for b in range(2):
-            weigh(b * P, diff_first[b][:])
+            weigh(b * P, diff_first[:, :, b * P:(b + 1) * P])
+        round_xm(1, xm_late, nc.scalar.copy)
         quantize(h_r, E5, h_bf, 0, P)
-        quantize_xm(0, "diff0")
         quantize(h_r, E5, h_bf, P, HALF)
-        diff_second = [subtract(HALF, HALF + P, "diff1"), subtract(HALF + P, N, "probs0")]
+        diff_second = [subtract(HALF, HALF + P, "diff_first"), subtract(HALF + P, N, "probs0")]
         dw_first_ps = bank("b0")
         for j in range(2):
             product(dw_first_ps[:, half_cols(j)], xm_r[0], E4, j, h_r, E5, half_cols(0))
@@ -229,15 +254,14 @@ def tile_attend_glse_wx_ts_kernel(tc, xT, wT, y, lse, wt, ts, xm, offs, out_0, o
         quantize(h_r, E5, h_bf, HALF, HALF + P)
         quantize(h_r, E5, h_bf, HALF + P, N)
         quantize_xm(1, "probs0")
-        for j, offset in ((2, 4096), (3, 12288)):
-            windows.append(shared.tile([P, T], F32, name="window%d" % j, offset=offset, align_bytes=64))
-            nc.gpsimd.memset(windows[j][:], 0.0)
-        dw_second = []
-        for j in range(2):
-            dw_ps = bank("b1")
-            product(dw_ps[:, 0:HALF], xm_r[0], E4, j, h_r, E5, half_cols(1))
-            dw_second.append(tile("dw_second%d" % j, [P, HALF], F32))
-            (nc.vector.tensor_copy, nc.scalar.copy)[j](dw_second[j][:], dw_ps[:, 0:HALF])
+        dw_second = [tile("dw_second%d" % j, [P, HALF], F32) for j in range(2)]
+        for b, tag in enumerate(("b3", "b1")):
+            dw_ps = bank(tag)
+            product(dw_ps[:, 0:P], xm_r[0], E4, 0, h_r, E5, slice(HALF + b * P, HALF + (b + 1) * P))
+            nc.vector.tensor_copy(dw_second[0][:, b * P:(b + 1) * P], dw_ps[:, 0:P])
+        dw_ps = bank("b1")
+        product(dw_ps[:, 0:HALF], xm_r[0], E4, 1, h_r, E5, half_cols(1))
+        nc.scalar.copy(dw_second[1][:], dw_ps[:, 0:HALF])
 
         def dw_block(j, bank_tag, tag):
             dw_ps = bank(bank_tag)
@@ -248,6 +272,10 @@ def tile_attend_glse_wx_ts_kernel(tc, xT, wT, y, lse, wt, ts, xm, offs, out_0, o
 
         nc.vector.tensor_copy(windows[0][:].indirect(list_half(1)), dw_second[0][:])
         store_window(0)
+        w_i = mx_operand("w_i", D, "dw_second0")
+        for pair in range(2):
+            placed = half_cols(pair)
+            nc.vector.quantize_mx(out=w_i[0][:, placed].bitcast(E4), scales=w_i[1][:, placed], in_=w_i_bf[pair][:])
         dw_2 = dw_block(2, "a0", "dw_2")
         scatter_on_scalar(1, 1, dw_second[1][:])
         store_window(1)
@@ -258,10 +286,6 @@ def tile_attend_glse_wx_ts_kernel(tc, xT, wT, y, lse, wt, ts, xm, offs, out_0, o
         h_i_dst = h_i_bf[:].rearrange("q (u e p s) -> q u e p s", u=2, e=2, s=PACK)
         for u, tag in ((0, "b1"), (1, "a0")):
             nc.scalar.copy(h_i_dst[:, u], turn_pairs(tag, h_bf, u).rearrange("q (s p e) -> q e p s", s=PACK, e=2))
-        w_i = mx_operand("w_i", D, "dw_2")
-        for pair in range(2):
-            placed = half_cols(pair)
-            nc.vector.quantize_mx(out=w_i[0][:, placed].bitcast(E4), scales=w_i[1][:, placed], in_=w_i_bf[pair][:])
         h_i = mx_operand("h_i", R)
         quantize(h_i, E5, h_i_bf, 0, R)
         dw_3 = dw_block(3, "b1", "dw_3")

@@ -136,14 +136,6 @@ def tile_attend_glse_wx_ts_kernel(tc, xT, wT, y, lse, wt, ts, xm, offs, out_0, o
         w_d = mx_operand("w_d", N)
         quantize(w_d, E4, w_bf, 0, N)
 
-        def turn_pairs(tag, src, u):
-            pairs = bank(tag)
-            words = src[:].bitcast(F32)
-            for s in range(PACK):
-                start = 2 * s + u
-                nc.tensor.transpose(pairs[:, s * P:(s + 1) * P], words[:, start:start + (P - 1) * 8 + 1:8], ident[:])
-            return pairs[:].bitcast(BF16)
-
         x_bf = tile("x_bf", [P, R * PACK], BF16, "w_plane3")
         x_dst = x_bf[:].rearrange("p (j m t) -> p m t j", j=PACK, t=PACK)
         x_src = [x_raw[part][:].rearrange("p t (m j) -> p m t j", j=PACK) for part in range(2)]
@@ -254,6 +246,11 @@ def tile_attend_glse_wx_ts_kernel(tc, xT, wT, y, lse, wt, ts, xm, offs, out_0, o
         quantize(h_r, E5, h_bf, HALF, HALF + P)
         quantize(h_r, E5, h_bf, HALF + P, N)
         quantize_xm(1, "probs0")
+        h_rows = []
+        for pair in range(2):
+            h_rows.append(shared.tile([P, 2, N], BF16, name="h_rows%d" % pair, offset=10240 + 2048 * pair, align_bytes=64))
+            nc.gpsimd.tensor_scalar(h_rows[pair][:], h_bf[:].rearrange("p (i t) -> p t i", t=PACK)[:, 2 * pair:2 * pair + 2, :],
+                                    1.0, 0.0, ALU.mult, ALU.add)
         dw_second = [tile("dw_second%d" % j, [P, HALF], F32) for j in range(2)]
         for b, tag in enumerate(("b3", "b1")):
             dw_ps = bank(tag)
@@ -283,9 +280,14 @@ def tile_attend_glse_wx_ts_kernel(tc, xT, wT, y, lse, wt, ts, xm, offs, out_0, o
         store_window(2)
 
         h_i_bf = tile("h_i_bf", [P, R * PACK], BF16)
-        h_i_dst = h_i_bf[:].rearrange("q (u e p s) -> q u e p s", u=2, e=2, s=PACK)
-        for u, tag in ((0, "b1"), (1, "a0")):
-            nc.scalar.copy(h_i_dst[:, u], turn_pairs(tag, h_bf, u).rearrange("q (s p e) -> q e p s", s=PACK, e=2))
+        h_i_words = h_i_bf[:].bitcast(F32).rearrange("q (j p u) -> q j p u", j=PACK, u=2)
+        for pair, tag in ((0, "b1"), (1, "a0")):
+            turned = bank(tag)
+            for k in range(2):
+                words = h_rows[pair][:, k, :].bitcast(F32)
+                for u in range(2):
+                    nc.tensor.transpose(turned[:, (2 * k + u) * P:(2 * k + u + 1) * P], words[:, u:HALF:2], ident[:])
+            nc.scalar.copy(h_i_words[:, 2 * pair:2 * pair + 2], turned[:].rearrange("q (k u p) -> q k p u", k=2, u=2))
         h_i = mx_operand("h_i", R)
         quantize(h_i, E5, h_i_bf, 0, R)
         dw_3 = dw_block(3, "b1", "dw_3")

@@ -82,7 +82,7 @@ def tile_attend_glse_wx_ts_kernel(tc, xT, wT, y, lse, wt, ts, xm, offs, out_0, o
         nc.vector.memset(ts_table[0:P - 1, :], 0.0)
         ident = tile("ident", [P, P], F32)
         make_identity(nc, ident[:])
-        windows = [tile("window%d" % j, [P, T], F32) for j in range(3)]
+        windows = [tile("window%d" % j, [P, T], F32) for j in range(PACK)]
         for window in windows:
             nc.vector.memset(window[:], 0.0)
         neg_lse = tile("neg_lse", [P, PACK], F32)
@@ -133,8 +133,13 @@ def tile_attend_glse_wx_ts_kernel(tc, xT, wT, y, lse, wt, ts, xm, offs, out_0, o
         nc.scalar.activation(w_rows[1][:, 1, half_cols(1)], w_planes[3][:].indirect(list_half(1)), ACT.Copy)
         for half in range(2):
             weave(1, half_cols(half))
-        w_d = mx_operand("w_d", N)
-        quantize(w_d, E4, w_bf, 0, N)
+        w_d = []
+
+        def quantize_w_d(half, tag):
+            w_d.append(mx_operand("w_d%d" % half, HALF, tag))
+            quantize(w_d[half], E4, w_bf[:, half * HALF * PACK:(half + 1) * HALF * PACK], 0, HALF)
+
+        quantize_w_d(0, "w_d0_codes")
 
         x_bf = tile("x_bf", [P, R * PACK], BF16, "w_plane3")
         x_dst = x_bf[:].rearrange("p (j m t) -> p m t j", j=PACK, t=PACK)
@@ -143,6 +148,7 @@ def tile_attend_glse_wx_ts_kernel(tc, xT, wT, y, lse, wt, ts, xm, offs, out_0, o
         nc.scalar.copy(x_dst[:, 0:64, :, 2:4], x_src[0][:, :, :, 2:4])
         nc.vector.tensor_copy(x_dst[:, 64:128, :, 0:2], x_src[1][:, :, :, 0:2])
         nc.scalar.copy(x_dst[:, 64:128, :, 2:4], x_src[1][:, :, :, 2:4])
+        quantize_w_d(1, "x_raw0")
         x_d = mx_operand("x_d", R)
         quantize(x_d, E4, x_bf, 0, P)
         quantize(x_d, E4, x_bf, P, 2 * P)
@@ -175,7 +181,7 @@ def tile_attend_glse_wx_ts_kernel(tc, xT, wT, y, lse, wt, ts, xm, offs, out_0, o
         for pair in range(2):
             a_ps = bank("a%d" % pair)
             for k in range(2):
-                product(a_ps[:, half_cols(k)], x_d, E4, 2 * pair + k, w_d, E4, half_cols(0))
+                product(a_ps[:, half_cols(k)], x_d, E4, 2 * pair + k, w_d[0], E4, half_cols(0))
             nc.vector.tensor_tensor(scaled[:, 2 * pair:2 * pair + 2, :], a_ps[:].rearrange("p (j i) -> p j i", i=HALF),
                                     ts_all[:, half_cols(0)].unsqueeze(1).to_broadcast([P, 2, HALF]), ALU.mult)
             for j in range(2 * pair, 2 * pair + 2):
@@ -183,12 +189,12 @@ def tile_attend_glse_wx_ts_kernel(tc, xT, wT, y, lse, wt, ts, xm, offs, out_0, o
         a_ps = bank("a2")
         third = slice(HALF, HALF + P)
         for j in range(PACK):
-            product(a_ps[:, j * P:(j + 1) * P], x_d, E4, j, w_d, E4, third)
+            product(a_ps[:, j * P:(j + 1) * P], x_d, E4, j, w_d[1], E4, slice(0, P))
         scaled_third = tile("scaled_third", [P, PACK, P], F32)
         nc.vector.tensor_tensor(scaled_third[:], a_ps[:].rearrange("p (j i) -> p j i", i=P),
                                 ts_all[:, third].unsqueeze(1).to_broadcast([P, PACK, P]), ALU.mult)
         a_ps = bank("a3")
-        product(a_ps[:], w_d, E4, 3, x_d, E4, slice(0, R))
+        product(a_ps[:], w_d[1], E4, 1, x_d, E4, slice(0, R))
         scaled_last = shared.tile([P, R], F32, name="scaled_last", offset=11264, align_bytes=64)
         nc.scalar.activation(scaled_last[:], a_ps[:], ACT.Copy, scale=ts_cols[:, 3:4])
         by_row = bank("b2")
@@ -217,10 +223,10 @@ def tile_attend_glse_wx_ts_kernel(tc, xT, wT, y, lse, wt, ts, xm, offs, out_0, o
                                     wt_ts[:, :, c0:c0 + P].rearrange("p t (c i) -> p c t i", i=4), ALU.mult)
 
         def store_window(j):
-            nc.sync.dma_start(out_0[j * P:(j + 1) * P, :], windows[j % 3][:])
+            nc.sync.dma_start(out_0[j * P:(j + 1) * P, :], windows[j][:])
 
         def scatter_on_scalar(j, half, src):
-            nc.scalar.activation(windows[j % 3][:].indirect(list_half(half)), src, ACT.Copy)
+            nc.scalar.activation(windows[j][:].indirect(list_half(half)), src, ACT.Copy)
 
         diff_first = tile("diff_first", [P, PACK, HALF], F32)
         for pair in range(2):
@@ -289,7 +295,8 @@ def tile_attend_glse_wx_ts_kernel(tc, xT, wT, y, lse, wt, ts, xm, offs, out_0, o
                     nc.tensor.transpose(turned[:, (2 * k + u) * P:(2 * k + u + 1) * P], words[:, u:HALF:2], ident[:])
             nc.scalar.copy(h_i_words[:, 2 * pair:2 * pair + 2], turned[:].rearrange("q (k u p) -> q k p u", k=2, u=2))
         h_i = mx_operand("h_i", R)
-        quantize(h_i, E5, h_i_bf, 0, R)
+        for pair in range(2):
+            quantize(h_i, E5, h_i_bf, pair * HALF, (pair + 1) * HALF)
         dw_3 = dw_block(3, "b1", "dw_3")
         for half in range(2):
             scatter_on_scalar(3, half, dw_3[:, half_cols(half)])

@@ -307,6 +307,5 @@ def tile_attend_glse_wx_ts_kernel(tc, xT, wT, y, lse, wt, ts, xm, offs, out_0, o
             product(gx_ps[:], h_i, E5, j, w_i, E4, slice(0, D))
             nc.vector.tensor_copy(gx_sb[:, j, :].rearrange("m (p u k) -> m p u k", u=2, k=2),
                                   gx_ps[:].rearrange("m (u p k) -> m p u k", u=2, k=2))
-            if j % 2 == 1:
-                nc.sync.dma_start(gx_rows[:, j - 1:j + 1, :], gx_sb[:, j - 1:j + 1, :])
+            nc.sync.dma_start(gx_rows[:, j, :], gx_sb[:, j, :])
         store_window(3)

@@ -100,8 +100,8 @@ def tile_attend_glse_wx_ts_kernel(tc, xT, wT, y, lse, wt, ts, xm, offs, out_0, o
         ts_all_ps = bank("b1")
         for k in range(4):
             nc.tensor.transpose(ts_all_ps[:, k * P:(k + 1) * P], ts_cols[:, k:k + 1].to_broadcast([P, P]), ident[:])
-        ts_all = tile("ts_all", [P, N], F32)
-        nc.scalar.copy(ts_all[:], ts_all_ps[:])
+        ts_all = tile("ts_all", [P, HALF + P], F32)
+        nc.scalar.copy(ts_all[:], ts_all_ps[:, 0:HALF + P])
         wt_ts = tile("wt_ts", [P, PACK, N], F32)
         for t in range(PACK):
             nc.scalar.activation(wt_ts[:, t, :], ts_all_ps[:], ACT.Copy, scale=wt_sb[:, t:t + 1])

@@ -156,10 +156,9 @@ def tile_attend_glse_wx_ts_kernel(tc, xT, wT, y, lse, wt, ts, xm, offs, out_0, o
         turn_w(1, "b1", shared.tile([P, HALF * PACK], BF16, name="w_i_high", offset=0, align_bytes=64))
         xm_bf = []
 
-        def round_xm(pair, dst, copy):
-            xm_bf.append(dst)
-            copy(xm_bf[pair][:].rearrange("p (c i t) -> p c t i", i=4, t=PACK),
-                           xm_raw[pair][:].rearrange("p t (c i) -> p c t i", i=4))
+        def round_xm(pair, cols):
+            nc.scalar.copy(xm_bf[pair][:, PACK * cols.start:PACK * cols.stop].rearrange("p (c i t) -> p c t i", i=4, t=PACK),
+                           xm_raw[pair][:, :, cols].rearrange("p t (c i) -> p c t i", i=4))
 
         xm_r = []
 
@@ -167,7 +166,8 @@ def tile_attend_glse_wx_ts_kernel(tc, xT, wT, y, lse, wt, ts, xm, offs, out_0, o
             xm_r.append(mx_operand("xm_r%d" % pair, 2 * P, tag))
             quantize(xm_r[pair], E4, xm_bf[pair], 0, 2 * P)
 
-        round_xm(0, shared.tile([P, HALF * PACK], BF16, name="xm_bf0", offset=2048, align_bytes=64), nc.scalar.copy)
+        xm_bf.append(shared.tile([P, HALF * PACK], BF16, name="xm_bf0", offset=2048, align_bytes=64))
+        round_xm(0, slice(0, 2 * P))
 
         probs = [tile("probs%d" % half, [P, PACK, HALF], F32) for half in range(2)]
 
@@ -190,7 +190,7 @@ def tile_attend_glse_wx_ts_kernel(tc, xT, wT, y, lse, wt, ts, xm, offs, out_0, o
         third = slice(HALF, HALF + P)
         for j in range(PACK):
             product(a_ps[:, j * P:(j + 1) * P], x_d, E4, j, w_d[1], E4, slice(0, P))
-        scaled_third = tile("scaled_third", [P, PACK, P], F32)
+        scaled_third = shared.tile([P, PACK, P], F32, name="scaled_third", offset=14336, align_bytes=64)
         nc.vector.tensor_tensor(scaled_third[:], a_ps[:].rearrange("p (j i) -> p j i", i=P),
                                 ts_all[:, third].unsqueeze(1).to_broadcast([P, PACK, P]), ALU.mult)
         a_ps = bank("a3")
@@ -202,10 +202,11 @@ def tile_attend_glse_wx_ts_kernel(tc, xT, wT, y, lse, wt, ts, xm, offs, out_0, o
             nc.tensor.transpose(by_row[:, j * P:(j + 1) * P], scaled_last[:, j * P:(j + 1) * P], ident[:])
         for j in range(PACK):
             exp_rows(j, HALF, scaled_third[:, j, :])
+        xm_bf.append(shared.tile([P, HALF * PACK], BF16, name="xm_bf1", offset=14336, align_bytes=64))
+        round_xm(1, slice(0, P))
         for j in range(PACK):
             exp_rows(j, HALF + P, by_row[:, j * P:(j + 1) * P])
-
-        xm_late = shared.tile([P, HALF * PACK], BF16, name="xm_bf1", offset=11264, align_bytes=64)
+        round_xm(1, slice(P, 2 * P))
 
         h_bf = tile("h_bf", [P, N * PACK], BF16)
         h_dst = h_bf[:].rearrange("p (c i t) -> p c t i", i=4, t=PACK)
@@ -235,17 +236,17 @@ def tile_attend_glse_wx_ts_kernel(tc, xT, wT, y, lse, wt, ts, xm, offs, out_0, o
         quantize_xm(0, "y_sb0")
         for b in range(2):
             weigh(b * P, diff_first[:, :, b * P:(b + 1) * P])
-        round_xm(1, xm_late, nc.scalar.copy)
         quantize(h_r, E5, h_bf, 0, P)
         quantize(h_r, E5, h_bf, P, HALF)
         diff_second = [subtract(HALF, HALF + P, "diff_first"), subtract(HALF + P, N, "probs0")]
-        dw_first_ps = bank("b0")
+        dw_first = []
+        for j, tag in enumerate(("b0", "a1")):
+            dw_ps = bank(tag)
+            product(dw_ps[:, 0:HALF], xm_r[0], E4, j, h_r, E5, half_cols(0))
+            dw_first.append(tile("dw_first%d" % j, [P, HALF], F32))
+            nc.scalar.copy(dw_first[j][:], dw_ps[:, 0:HALF])
         for j in range(2):
-            product(dw_first_ps[:, half_cols(j)], xm_r[0], E4, j, h_r, E5, half_cols(0))
-        dw_first = tile("dw_first", [P, N], F32)
-        nc.scalar.copy(dw_first[:], dw_first_ps[:])
-        for j in range(2):
-            scatter_on_scalar(j, 0, dw_first[:, half_cols(j)])
+            scatter_on_scalar(j, 0, dw_first[j][:])
 
         for b in range(2):
             weigh(HALF + b * P, diff_second[b][:])
@@ -254,7 +255,7 @@ def tile_attend_glse_wx_ts_kernel(tc, xT, wT, y, lse, wt, ts, xm, offs, out_0, o
         quantize_xm(1, "probs0")
         h_rows = []
         for pair in range(2):
-            h_rows.append(shared.tile([P, 2, N], BF16, name="h_rows%d" % pair, offset=10240 + 2048 * pair, align_bytes=64))
+            h_rows.append(shared.tile([P, 2, N], BF16, name="h_rows%d" % pair, offset=13312 + 2048 * pair, align_bytes=64))
             nc.gpsimd.tensor_scalar(h_rows[pair][:], h_bf[:].rearrange("p (i t) -> p t i", t=PACK)[:, 2 * pair:2 * pair + 2, :],
                                     1.0, 0.0, ALU.mult, ALU.add)
         dw_second = [tile("dw_second%d" % j, [P, HALF], F32) for j in range(2)]
@@ -266,46 +267,49 @@ def tile_attend_glse_wx_ts_kernel(tc, xT, wT, y, lse, wt, ts, xm, offs, out_0, o
         product(dw_ps[:, 0:HALF], xm_r[0], E4, 1, h_r, E5, half_cols(1))
         nc.scalar.copy(dw_second[1][:], dw_ps[:, 0:HALF])
 
-        def dw_block(j, bank_tag, tag):
+        def dw_block(j, bank_tag, dw_sb):
             dw_ps = bank(bank_tag)
             product(dw_ps[:], xm_r[1], E4, j - 2, h_r, E5, slice(0, N))
-            dw_sb = tile("dw_late%d" % j, [P, N], F32, tag)
             nc.scalar.copy(dw_sb[:], dw_ps[:])
             return dw_sb
 
         nc.vector.tensor_copy(windows[0][:].indirect(list_half(1)), dw_second[0][:])
         store_window(0)
-        w_i = mx_operand("w_i", D, "dw_second0")
-        for pair in range(2):
-            placed = half_cols(pair)
-            nc.vector.quantize_mx(out=w_i[0][:, placed].bitcast(E4), scales=w_i[1][:, placed], in_=w_i_bf[pair][:])
-        dw_2 = dw_block(2, "a0", "dw_2")
+        dw_2 = dw_block(2, "a0", shared.tile([P, N], F32, name="dw_2", offset=20480, align_bytes=64))
         scatter_on_scalar(1, 1, dw_second[1][:])
         store_window(1)
         nc.vector.tensor_copy(windows[2][:].indirect(offsets[:]), dw_2[:])
         store_window(2)
+        dw_ps = bank("b1")
+        product(dw_ps[:], xm_r[1], E4, 1, h_r, E5, slice(0, N))
+        for half in range(2):
+            dw_3 = tile("dw_3%d" % half, [P, HALF], F32, "dw_second1" if half else None)
+            nc.scalar.copy(dw_3[:], dw_ps[:, half_cols(half)])
+            scatter_on_scalar(3, half, dw_3[:])
+        store_window(3)
 
-        h_i_bf = tile("h_i_bf", [P, R * PACK], BF16)
+        h_i_bf = shared.tile([P, R * PACK], BF16, name="h_i_bf", offset=21504, align_bytes=64)
         h_i_words = h_i_bf[:].bitcast(F32).rearrange("q (j p u) -> q j p u", j=PACK, u=2)
-        for pair, tag in ((0, "b1"), (1, "a0")):
+        for pair, tag in ((0, "a1"), (1, "a0")):
             turned = bank(tag)
             for k in range(2):
                 words = h_rows[pair][:, k, :].bitcast(F32)
                 for u in range(2):
                     nc.tensor.transpose(turned[:, (2 * k + u) * P:(2 * k + u + 1) * P], words[:, u:HALF:2], ident[:])
-            nc.scalar.copy(h_i_words[:, 2 * pair:2 * pair + 2], turned[:].rearrange("q (k u p) -> q k p u", k=2, u=2))
+            nc.vector.tensor_copy(h_i_words[:, 2 * pair:2 * pair + 2], turned[:].rearrange("q (k u p) -> q k p u", k=2, u=2))
+        w_i = (shared.tile([P, D], U32, name="w_i_codes", offset=19456, align_bytes=64), tile("w_i_scales", [P, D], U8))
+        for pair in range(2):
+            placed = half_cols(pair)
+            nc.vector.quantize_mx(out=w_i[0][:, placed].bitcast(E4), scales=w_i[1][:, placed], in_=w_i_bf[pair][:])
         h_i = mx_operand("h_i", R)
         for pair in range(2):
             quantize(h_i, E5, h_i_bf, pair * HALF, (pair + 1) * HALF)
-        dw_3 = dw_block(3, "b1", "dw_3")
-        for half in range(2):
-            scatter_on_scalar(3, half, dw_3[:, half_cols(half)])
         gx_sb = tile("gx_sb", [P, PACK, D], F32)
         gx_rows = out_1[0].rearrange("(m j) d -> m j d", j=PACK)
         for j, tag in enumerate(("b3", "a2", "a3", "b2")):
             gx_ps = bank(tag)
             product(gx_ps[:], h_i, E5, j, w_i, E4, slice(0, D))
-            nc.vector.tensor_copy(gx_sb[:, j, :].rearrange("m (p u k) -> m p u k", u=2, k=2),
-                                  gx_ps[:].rearrange("m (u p k) -> m p u k", u=2, k=2))
-            nc.sync.dma_start(gx_rows[:, j, :], gx_sb[:, j, :])
-        store_window(3)
+            copy = nc.vector.tensor_copy if j % 2 else nc.scalar.copy
+            copy(gx_sb[:, j, :].rearrange("m (p u k) -> m p u k", u=2, k=2), gx_ps[:].rearrange("m (u p k) -> m p u k", u=2, k=2))
+            if j % 2:
+                nc.sync.dma_start(gx_rows[:, j - 1:j + 1, :], gx_sb[:, j - 1:j + 1, :])

from contextlib import ExitStack

import concourse.mybir as mybir
from concourse.masks import make_identity

N, T, D, R = 512, 2048, 512, 512
FLOPS = 3 * 2 * N * D * R

F32 = mybir.dt.float32
BF16 = mybir.dt.bfloat16
U32 = mybir.dt.uint32
U16 = mybir.dt.uint16
U8 = mybir.dt.uint8
E4 = mybir.dt.float8_e4m3fn_x4
E5 = mybir.dt.float8_e5m2_x4
ALU = mybir.AluOpType
ACT = mybir.ActivationFunctionType

P = 128
PACK = 4
HALF = N // 2


def tile_attend_glse_wx_ts_kernel(tc, xT, wT, y, lse, wt, ts, xm, offs, out_0, out_1):
    nc = tc.nc
    with ExitStack() as ctx:
        sb = ctx.enter_context(tc.tile_pool(name="sb", bufs=1))
        shared = ctx.enter_context(tc.tile_pool(name="shared", bufs=1))
        ps = ctx.enter_context(tc.psum_pool(name="ps", bufs=1))

        def bank(tag):
            return ps.tile([P, 512], F32, name=tag, tag=tag)

        def tile(name, shape, dtype, tag=None):
            return sb.tile(shape, dtype, name=name, tag=tag or name, align_bytes=64)

        def mx_operand(name, width, tag=None):
            return tile(name + "_codes", [P, width], U32, tag), tile(name + "_scales", [P, width], U8)

        def quantize(operand, fmt, src, c0, c1):
            codes, scales = operand
            nc.vector.quantize_mx(out=codes[:, c0:c1].bitcast(fmt), scales=scales[:, c0:c1],
                                  in_=src[:, PACK * c0:PACK * c1])

        def product(out, lhs, lhs_fmt, j, rhs, rhs_fmt, moving):
            cols = slice(j * P, (j + 1) * P)
            nc.tensor.matmul_mx(out=out, lhsT=lhs[0][:, cols].bitcast(lhs_fmt), lhsT_scale=lhs[1][:, cols],
                                rhs=rhs[0][:, moving].bitcast(rhs_fmt), rhs_scale=rhs[1][:, moving], start=True, stop=True)

        def half_cols(half):
            return slice(half * HALF, (half + 1) * HALF)

        def list_half(half):
            return offsets[:, half * HALF // 16:(half + 1) * HALF // 16]

        w_planes = [tile("w_plane%d" % t, [P, T], F32) for t in range(PACK)]
        wT_planes = wT.rearrange("(p t) c -> t p c", t=PACK)
        offsets = sb.tile([P, N // 16], U16, name="offsets")
        ts_table = tile("ts_table", [P, T], F32)
        nc.scalar.dma_start(ts_table[P - 1:P, :], ts[0:1, :])
        wt_sb = tile("wt_sb", [P, PACK], F32)
        nc.scalar.dma_start(wt_sb[:], wt[0].rearrange("(p t) o -> p (t o)", t=PACK))
        lse_sb = tile("lse_sb", [P, PACK], F32)
        nc.scalar.dma_start(lse_sb[:], lse[0].rearrange("(p t) o -> p (t o)", t=PACK))
        nc.sync.dma_start(offsets[:], offs)
        for t in range(PACK):
            nc.sync.dma_start(w_planes[t][:], wT_planes[t])
        x_raw = [tile("x_raw0", [P, PACK, R // 2], F32),
                 shared.tile([P, PACK, R // 2], F32, name="x_raw1", offset=0, align_bytes=64)]
        for part in range(2):
            nc.sync.dma_start(x_raw[part][:],
                              xT[0].rearrange("(p t) r -> p t r", t=PACK)[:, :, part * R // 2:(part + 1) * R // 2])
        y_rows = y[0].rearrange("(p t) i -> p t i", t=PACK)
        y_sb = [tile("y_sb%d" % half, [P, PACK, HALF], F32) for half in range(2)]
        xm_rows = xm[0].rearrange("(p t) d -> p t d", t=PACK)
        xm_raw = [tile("xm_raw%d" % pair, [P, PACK, D // 2], F32) for pair in range(2)]
        nc.sync.dma_start(xm_raw[0][:], xm_rows[:, :, 0:D // 2])
        for half in range(2):
            nc.sync.dma_start(y_sb[half][:], y_rows[:, :, half_cols(half)])
        nc.sync.dma_start(xm_raw[1][:], xm_rows[:, :, D // 2:D])

        nc.vector.memset(ts_table[0:P - 1, :], 0.0)
        ident = tile("ident", [P, P], F32)
        make_identity(nc, ident[:])
        windows = [tile("window%d" % j, [P, T], F32) for j in range(PACK)]
        for window in windows:
            nc.vector.memset(window[:], 0.0)
        neg_lse = tile("neg_lse", [P, PACK], F32)
        nc.gpsimd.tensor_scalar(neg_lse[:], lse_sb[:], -1.0, 0.0, ALU.mult, ALU.add)

        ts_row = tile("ts_row", [P, N], F32)
        nc.scalar.activation(ts_row[:], ts_table[:].indirect(offsets[:]), ACT.Copy)
        w_rows = [tile("w_rows%d" % pair, [P, 2, N], BF16) for pair in range(2)]
        nc.scalar.activation(w_rows[0][:, 0, :], w_planes[0][:].indirect(offsets[:]), ACT.Copy)
        ts_cols_ps = bank("b0")
        for k in range(4):
            nc.tensor.transpose(ts_cols_ps[:, k * P:(k + 1) * P], ts_row[:, k * P:(k + 1) * P], ident[:])
        ts_cols = tile("ts_cols", [P, 4], F32, "w_plane0")
        nc.scalar.copy(ts_cols[:], ts_cols_ps[:, P - 1:N:P])
        ts_all_ps = bank("b1")
        for k in range(4):
            nc.tensor.transpose(ts_all_ps[:, k * P:(k + 1) * P], ts_cols[:, k:k + 1].to_broadcast([P, P]), ident[:])
        ts_all = tile("ts_all", [P, HALF + P], F32)
        nc.scalar.copy(ts_all[:], ts_all_ps[:, 0:HALF + P])
        wt_ts = tile("wt_ts", [P, PACK, N], F32)
        for t in range(PACK):
            nc.scalar.activation(wt_ts[:, t, :], ts_all_ps[:], ACT.Copy, scale=wt_sb[:, t:t + 1])

        w_bf = tile("w_bf", [P, N * PACK], BF16)
        w_bf3 = w_bf[:].rearrange("p (i t) -> p i t", t=PACK)
        nc.vector.tensor_copy(w_rows[0][:, 1, :], w_planes[1][:].indirect(offsets[:]))

        def weave(pair, slots):
            planes = slice(2 * pair, 2 * pair + 2)
            nc.vector.tensor_copy(w_bf3[:, slots, planes], w_rows[pair][:, :, slots].rearrange("p t i -> p i t"))

        w_i_bf = []

        def turn_w(pair, tag, dst):
            w_i_bf.append(dst)
            turned = bank(tag)
            for k in range(2):
                words = w_rows[pair][:, k, :].bitcast(F32)
                for u in range(2):
                    nc.tensor.transpose(turned[:, (2 * k + u) * P:(2 * k + u + 1) * P], words[:, u:HALF:2], ident[:])
            nc.scalar.copy(dst[:].bitcast(F32).rearrange("q (p k u) -> q p k u", k=2, u=2),
                           turned[:].rearrange("q (k u p) -> q p k u", k=2, u=2))

        weave(0, slice(0, N))
        turn_w(0, "b0", tile("w_i_low", [P, HALF * PACK], BF16))
        nc.vector.tensor_copy(w_rows[1][:, 0, :], w_planes[2][:].indirect(offsets[:]))
        nc.vector.tensor_copy(w_rows[1][:, 1, half_cols(0)], w_planes[3][:].indirect(list_half(0)))
        nc.scalar.activation(w_rows[1][:, 1, half_cols(1)], w_planes[3][:].indirect(list_half(1)), ACT.Copy)
        for half in range(2):
            weave(1, half_cols(half))
        w_d = []

        def quantize_w_d(half, tag):
            w_d.append(mx_operand("w_d%d" % half, HALF, tag))
            quantize(w_d[half], E4, w_bf[:, half * HALF * PACK:(half + 1) * HALF * PACK], 0, HALF)

        quantize_w_d(0, "w_d0_codes")

        x_bf = tile("x_bf", [P, R * PACK], BF16, "w_plane3")
        x_dst = x_bf[:].rearrange("p (j m t) -> p m t j", j=PACK, t=PACK)
        x_src = [x_raw[part][:].rearrange("p t (m j) -> p m t j", j=PACK) for part in range(2)]
        nc.scalar.copy(x_dst[:, 0:64, :, 0:2], x_src[0][:, :, :, 0:2])
        nc.scalar.copy(x_dst[:, 0:64, :, 2:4], x_src[0][:, :, :, 2:4])
        nc.vector.tensor_copy(x_dst[:, 64:128, :, 0:2], x_src[1][:, :, :, 0:2])
        nc.scalar.copy(x_dst[:, 64:128, :, 2:4], x_src[1][:, :, :, 2:4])
        quantize_w_d(1, "x_raw0")
        x_d = mx_operand("x_d", R)
        quantize(x_d, E4, x_bf, 0, P)
        quantize(x_d, E4, x_bf, P, 2 * P)
        quantize(x_d, E4, x_bf, 2 * P, 4 * P)
        turn_w(1, "b1", shared.tile([P, HALF * PACK], BF16, name="w_i_high", offset=0, align_bytes=64))
        xm_bf = []

        def round_xm(pair, cols):
            nc.scalar.copy(xm_bf[pair][:, PACK * cols.start:PACK * cols.stop].rearrange("p (c i t) -> p c t i", i=4, t=PACK),
                           xm_raw[pair][:, :, cols].rearrange("p t (c i) -> p c t i", i=4))

        xm_r = []

        def quantize_xm(pair, tag):
            xm_r.append(mx_operand("xm_r%d" % pair, 2 * P, tag))
            quantize(xm_r[pair], E4, xm_bf[pair], 0, 2 * P)

        xm_bf.append(shared.tile([P, HALF * PACK], BF16, name="xm_bf0", offset=2048, align_bytes=64))
        round_xm(0, slice(0, 2 * P))

        probs = [tile("probs%d" % half, [P, PACK, HALF], F32) for half in range(2)]

        def exp_rows(j, c0, src):
            half = c0 // HALF
            width = src.shape[1]
            nc.scalar.activation(probs[half][:, j, c0 - half * HALF:c0 - half * HALF + width], src, ACT.Exp,
                                 bias=neg_lse[:, j:j + 1], scale=1.0)

        scaled = shared.tile([P, PACK, HALF], F32, name="scaled", offset=10240, align_bytes=64)
        for pair in range(2):
            a_ps = bank("a%d" % pair)
            for k in range(2):
                product(a_ps[:, half_cols(k)], x_d, E4, 2 * pair + k, w_d[0], E4, half_cols(0))
            nc.vector.tensor_tensor(scaled[:, 2 * pair:2 * pair + 2, :], a_ps[:].rearrange("p (j i) -> p j i", i=HALF),
                                    ts_all[:, half_cols(0)].unsqueeze(1).to_broadcast([P, 2, HALF]), ALU.mult)
            for j in range(2 * pair, 2 * pair + 2):
                exp_rows(j, 0, scaled[:, j, :])
        a_ps = bank("a2")
        third = slice(HALF, HALF + P)
        for j in range(PACK):
            product(a_ps[:, j * P:(j + 1) * P], x_d, E4, j, w_d[1], E4, slice(0, P))
        scaled_third = shared.tile([P, PACK, P], F32, name="scaled_third", offset=14336, align_bytes=64)
        nc.vector.tensor_tensor(scaled_third[:], a_ps[:].rearrange("p (j i) -> p j i", i=P),
                                ts_all[:, third].unsqueeze(1).to_broadcast([P, PACK, P]), ALU.mult)
        a_ps = bank("a3")
        product(a_ps[:], w_d[1], E4, 1, x_d, E4, slice(0, R))
        scaled_last = shared.tile([P, R], F32, name="scaled_last", offset=11264, align_bytes=64)
        nc.scalar.activation(scaled_last[:], a_ps[:], ACT.Copy, scale=ts_cols[:, 3:4])
        by_row = bank("b2")
        for j in range(PACK):
            nc.tensor.transpose(by_row[:, j * P:(j + 1) * P], scaled_last[:, j * P:(j + 1) * P], ident[:])
        for j in range(PACK):
            exp_rows(j, HALF, scaled_third[:, j, :])
        xm_bf.append(shared.tile([P, HALF * PACK], BF16, name="xm_bf1", offset=14336, align_bytes=64))
        round_xm(1, slice(0, P))
        for j in range(PACK):
            exp_rows(j, HALF + P, by_row[:, j * P:(j + 1) * P])
        round_xm(1, slice(P, 2 * P))

        h_bf = tile("h_bf", [P, N * PACK], BF16)
        h_dst = h_bf[:].rearrange("p (c i t) -> p c t i", i=4, t=PACK)
        h_r = mx_operand("h_r", N)

        def subtract(c0, c1, tag):
            half = c0 // HALF
            cols = slice(c0 - half * HALF, c1 - half * HALF)
            diff = tile("diff%d" % c0, [P, PACK, c1 - c0], F32, tag)
            nc.vector.tensor_tensor(diff[:], probs[half][:, :, cols], y_sb[half][:, :, cols], ALU.subtract)
            return diff

        def weigh(c0, diff):
            nc.vector.tensor_tensor(h_dst[:, c0 // 4:(c0 + P) // 4], diff.rearrange("p t (c i) -> p c t i", i=4),
                                    wt_ts[:, :, c0:c0 + P].rearrange("p t (c i) -> p c t i", i=4), ALU.mult)

        def store_window(j):
            nc.sync.dma_start(out_0[j * P:(j + 1) * P, :], windows[j][:])

        def scatter_on_scalar(j, half, src):
            nc.scalar.activation(windows[j][:].indirect(list_half(half)), src, ACT.Copy)

        diff_first = tile("diff_first", [P, PACK, HALF], F32)
        for pair in range(2):
            rows = slice(2 * pair, 2 * pair + 2)
            nc.vector.tensor_tensor(diff_first[:, rows, :], probs[0][:, rows, :], y_sb[0][:, rows, :], ALU.subtract)
        quantize_xm(0, "y_sb0")
        for b in range(2):
            weigh(b * P, diff_first[:, :, b * P:(b + 1) * P])
        quantize(h_r, E5, h_bf, 0, P)
        quantize(h_r, E5, h_bf, P, HALF)
        diff_second = [subtract(HALF, HALF + P, "diff_first"), subtract(HALF + P, N, "probs0")]
        dw_first = []
        for j, tag in enumerate(("b0", "a1")):
            dw_ps = bank(tag)
            product(dw_ps[:, 0:HALF], xm_r[0], E4, j, h_r, E5, half_cols(0))
            dw_first.append(tile("dw_first%d" % j, [P, HALF], F32))
            nc.scalar.copy(dw_first[j][:], dw_ps[:, 0:HALF])
        for j in range(2):
            scatter_on_scalar(j, 0, dw_first[j][:])

        for b in range(2):
            weigh(HALF + b * P, diff_second[b][:])
        quantize(h_r, E5, h_bf, HALF, HALF + P)
        quantize(h_r, E5, h_bf, HALF + P, N)
        quantize_xm(1, "probs0")
        h_rows = []
        for pair in range(2):
            h_rows.append(shared.tile([P, 2, N], BF16, name="h_rows%d" % pair, offset=13312 + 2048 * pair, align_bytes=64))
            nc.gpsimd.tensor_scalar(h_rows[pair][:], h_bf[:].rearrange("p (i t) -> p t i", t=PACK)[:, 2 * pair:2 * pair + 2, :],
                                    1.0, 0.0, ALU.mult, ALU.add)
        dw_second = [tile("dw_second%d" % j, [P, HALF], F32) for j in range(2)]
        for b, tag in enumerate(("b3", "b1")):
            dw_ps = bank(tag)
            product(dw_ps[:, 0:P], xm_r[0], E4, 0, h_r, E5, slice(HALF + b * P, HALF + (b + 1) * P))
            nc.vector.tensor_copy(dw_second[0][:, b * P:(b + 1) * P], dw_ps[:, 0:P])
        dw_ps = bank("b1")
        product(dw_ps[:, 0:HALF], xm_r[0], E4, 1, h_r, E5, half_cols(1))
        nc.scalar.copy(dw_second[1][:], dw_ps[:, 0:HALF])

        def dw_block(j, bank_tag, dw_sb):
            dw_ps = bank(bank_tag)
            product(dw_ps[:], xm_r[1], E4, j - 2, h_r, E5, slice(0, N))
            nc.scalar.copy(dw_sb[:], dw_ps[:])
            return dw_sb

        nc.vector.tensor_copy(windows[0][:].indirect(list_half(1)), dw_second[0][:])
        store_window(0)
        dw_2 = dw_block(2, "a0", shared.tile([P, N], F32, name="dw_2", offset=20480, align_bytes=64))
        scatter_on_scalar(1, 1, dw_second[1][:])
        store_window(1)
        nc.vector.tensor_copy(windows[2][:].indirect(offsets[:]), dw_2[:])
        store_window(2)
        dw_ps = bank("b1")
        product(dw_ps[:], xm_r[1], E4, 1, h_r, E5, slice(0, N))
        for half in range(2):
            dw_3 = tile("dw_3%d" % half, [P, HALF], F32, "dw_second1" if half else None)
            nc.scalar.copy(dw_3[:], dw_ps[:, half_cols(half)])
            scatter_on_scalar(3, half, dw_3[:])
        store_window(3)

        h_i_bf = shared.tile([P, R * PACK], BF16, name="h_i_bf", offset=21504, align_bytes=64)
        h_i_words = h_i_bf[:].bitcast(F32).rearrange("q (j p u) -> q j p u", j=PACK, u=2)
        for pair, tag in ((0, "a1"), (1, "a0")):
            turned = bank(tag)
            for k in range(2):
                words = h_rows[pair][:, k, :].bitcast(F32)
                for u in range(2):
                    nc.tensor.transpose(turned[:, (2 * k + u) * P:(2 * k + u + 1) * P], words[:, u:HALF:2], ident[:])
            nc.vector.tensor_copy(h_i_words[:, 2 * pair:2 * pair + 2], turned[:].rearrange("q (k u p) -> q k p u", k=2, u=2))
        w_i = (shared.tile([P, D], U32, name="w_i_codes", offset=19456, align_bytes=64), tile("w_i_scales", [P, D], U8))
        for pair in range(2):
            placed = half_cols(pair)
            nc.vector.quantize_mx(out=w_i[0][:, placed].bitcast(E4), scales=w_i[1][:, placed], in_=w_i_bf[pair][:])
        h_i = mx_operand("h_i", R)
        for pair in range(2):
            quantize(h_i, E5, h_i_bf, pair * HALF, (pair + 1) * HALF)
        gx_sb = tile("gx_sb", [P, PACK, D], F32)
        gx_rows = out_1[0].rearrange("(m j) d -> m j d", j=PACK)
        for j, tag in enumerate(("b3", "a2", "a3", "b2")):
            gx_ps = bank(tag)
            product(gx_ps[:], h_i, E5, j, w_i, E4, slice(0, D))
            copy = nc.vector.tensor_copy if j % 2 else nc.scalar.copy
            copy(gx_sb[:, j, :].rearrange("m (p u k) -> m p u k", u=2, k=2), gx_ps[:].rearrange("m (u p k) -> m p u k", u=2, k=2))
            if j % 2:
                nc.sync.dma_start(gx_rows[:, j - 1:j + 1, :], gx_sb[:, j - 1:j + 1, :])
